import numpy as np, ml_dtypes
CORES = [13,21,141,149]
N = 4
BF = ml_dtypes.bfloat16
W, T, K, R = 2048, 1024, 256, 7
SR, SG = (1, 3), (0, 5)
def pack(x, ix, q, c):
    return {"rec": np.ascontiguousarray(x.reshape(N, 128, W)).astype(np.float32).astype(BF), "idx": np.ascontiguousarray(ix.reshape(N, 128, T)).astype(np.int32),
            "que": np.ascontiguousarray(q).astype(np.int32), "cur": np.ascontiguousarray(c.reshape(N, 8, 1)).astype(np.int32)}
def setup_inputs(rng):
    x = rng.integers(0, 16, (N, 8, 16, W)); ix = rng.integers(0, W, (N, 8, 16, T))
    q = np.ascontiguousarray(np.argsort(rng.random((N, 8, T)), axis=-1)[..., :K]); q[..., 17::32] = q[..., 2::32]
    return pack(x, ix, q, rng.integers(0, T, (N, 8)))
def regions(rng):
    o = 1 + rng.permutation(W - 2)
    return o[:816], o[816:820], np.concatenate([np.array([0, W - 1]), o[820:1330]]), o[1330:]
def give(rng, x, at, k, v):
    v = np.asarray(v)
    x[k, at] = (v >> 8) + (W >> 8) * rng.integers(0, 4096 // W, v.shape); x[(k + 1) % 16, at] = (v >> 4) & 15; x[(k + 2) % 16, at] = v & 15
def twin(rng, rd, w, bits, on):
    return int(rng.choice(rd[np.isin(rd ^ w, rd) & ((rd & bits) == on)]))
def group(rng, reg, edge):
    ixr, sp, dat, rdp = reg
    x = rng.integers(0, 16, (16, W)); x[:, rdp] = rng.integers(1, 16, (16, len(rdp))); o = rng.permutation(ixr); d0 = rng.permutation(dat)
    c0 = int(rng.choice(np.array([0, T - K, T - K - 1, T - 5, int(rng.integers(0, T))]))); q = (c0 + np.arange(K)) & (T - 1); c = (c0 + K) & (T - 1)
    i, j = c & 511, int(np.argmax(d0 == edge)); d0[[i, j]] = d0[[j, i]]
    give(rng, x, o[:512], 0, d0)
    at = o[512:752].reshape(15, 16); give(rng, x, at, np.arange(1, 16)[:, None], rng.choice(rdp, (15, 16)))
    ix = np.zeros((16, T), np.int64); ix[0] = o[np.arange(T) & 511]; ix[1:] = at[np.arange(15)[:, None], rng.integers(0, 16, (15, T))]
    return x, ix, q, c, d0, o[752:]
def blank():
    return np.zeros((N, 8, 16, W), np.int64), np.zeros((N, 8, 16, T), np.int64), np.zeros((N, 8, K), np.int64), np.zeros((N, 8), np.int64)
def setup_inputs_calm(rng):
    reg = regions(rng); s, s2, s3, e = [int(v) for v in reg[1]]; rd = reg[3]; x, ix, q, c = blank(); m = R + 2
    for r in range(N):
        for g in range(8):
            xa, ia, qa, ca, d0, sp = group(rng, reg, (0, W - 1)[(r + g) & 1]); n = (r + g) % 4
            give(rng, xa, sp[:3], 0, np.array([s, s2, s3])); give(rng, xa, sp[3:18], np.arange(1, 16), np.full(15, e))
            ia[0, qa[0]] = sp[0]; ia[0, qa[3:m + 2]] = sp[0]; ia[0, qa[1]] = sp[1]; ia[0, qa[2]] = sp[2]; ia[1:, qa[1:3]] = sp[3:18][:, None]
            kk = int(rng.integers(1, 16)); give(rng, xa, np.array([s]), kk, np.array([s]))
            vic = qa[m + 2 + rng.permutation(K - m - 2)[:n + 1]]; ia[kk, vic[:n]] = s
            j = int(vic[n]); ed = np.zeros(16, np.int64); k2, k3, k4 = [int(v) for v in 1 + rng.permutation(15)[:3]]; a2, a3 = np.array([s2]), np.array([s3])
            if g == 1:
                w = 2184 & (W - 1); v = twin(rng, rd, w, 0, 0); ed[:] = 8
                give(rng, xa, a2, k2, np.array([v])); give(rng, xa, a3, k3, np.array([v ^ w])); ia[k2, j] = s2; ia[k3, j] = s3
            elif g == 3:
                k2 = int(rng.integers(2, 8)); k3 = 2 * k2 + 1; k4 = 1; ed[k2 + 2] = 8; ed[(k3 + 2) & 15] = 12
                give(rng, xa, a2, k2, np.array([twin(rng, rd, 8, 8, 0)])); give(rng, xa, a3, k3, np.array([twin(rng, rd, 4, 4, 4)])); ia[k2, j] = s2; ia[k3, j] = s3
            elif g == 5:
                ed[(k2 + 1) & 15] = 8; give(rng, xa, a2, k2, np.array([twin(rng, rd, 128, 0, 0)])); ia[k2, j] = s2
            elif g == 7:
                k2 = 2 * int(rng.integers(1, 8)); k3 = k2 + 1; k4 = 1; ed[(k3 + 2) & 15] = 1
                give(rng, xa, a2, k3, np.array([twin(rng, rd, 1, 3, 2)])); give(rng, xa, sp[19:20], k2, np.array([W - 1])); ia[k2, j] = sp[19]; ia[k3, j] = s2
            else:
                ed[(k2 + 3 + int(rng.integers(0, 13))) & 15] = 8; give(rng, xa, a2, k2, rng.choice(rd, 1)); ia[k2, j] = s2
            give(rng, xa, sp[18:19], k4, np.array([s2])); ia[k4, j] = sp[18]; xa[:, e] = ed
            x[r, g] = xa; ix[r, g] = ia; q[r, g] = qa; c[r, g] = ca
    return pack(x, ix, q, c)
def setup_inputs_corners(rng):
    reg = regions(rng); s, s2, e = int(reg[1][0]), int(reg[1][1]), int(reg[1][3]); x, ix, q, c = blank(); par = int(rng.integers(0, 2))
    for r in range(N):
        for g in range(8):
            xa, ia, qa, ca, d0, sp = group(rng, reg, (0, W - 1)[(r + g) & 1]); xa[:, e] = 8
            if r % 2 == par:
                z = s2 if g == 4 else s
                kk = int(rng.integers(1, 16)); give(rng, xa, np.array([z]), kk, rng.choice(reg[3], 1)); was = ia[kk].copy(); ia[kk] = z
                if g == 6: ia[0] = int(ia[0, qa[0]])
                if g % 4 == 1: j = np.array([(ca + K - 1) & (T - 1)])
                elif g % 4 == 2: j = np.array([ca])
                elif g % 4 == 3: j = np.nonzero(rng.random(T) < 0.5)[0]
                else: j = np.zeros(0, np.int64)
                ia[kk, j] = was[j]
            else:
                give(rng, xa, sp[:1], 0, np.array([s])); give(rng, xa, sp[33:48], np.arange(1, 16), np.full(15, e)); give(rng, xa, sp[48:49], 0, np.array([s2]))
                two = qa[1:3] if g % 2 == 0 else qa[R + 34:R + 36]
                if g % 2 == 0:
                    ia[0] = sp[0]
                    if g == 2: qa = np.full(K, qa[0])
                else:
                    ia[0, qa[:R + 2]] = sp[0]; j = qa[R + 2:R + 34]
                    give(rng, xa, sp[1:33], 7, d0[j & 511]); ia[7, j] = sp[1:33]
                if g != 2:
                    ia[0, two] = sp[48]; ia[1:, two] = sp[33:48][:, None]
            x[r, g] = xa; ix[r, g] = ia; q[r, g] = qa; c[r, g] = ca
    return pack(x, ix, q, c)
def setup_inputs_crowd(rng):
    reg = regions(rng); x, ix, q, c = blank(); al = np.arange(T)
    for r in range(N):
        kinds = rng.permutation(8)
        for g in range(8):
            xa, ia, qa, ca, d0, sp = group(rng, reg, (0, W - 1)[(r + g) & 1]); h = int(kinds[g])
            if h == 1:
                give(rng, xa, sp[:1], 15, d0[qa[:1] & 511]); ia[15, qa[K - 1]] = sp[0]
            if h == 2: ia[0] = int(ia[0, ca])
            if h == 3:
                j = int(qa[int(rng.choice(np.array([0, K >> 1, K - 1])))]); was = int(ia[0, j]); ia[0] = int(ia[0, ca]); ia[0, j] = was
            if h == 4: ia[0] = ia[0, (ca + rng.integers(0, 2, T)) & (T - 1)]
            if h == 5: ia[0] = ia[0, (ca + rng.integers(0, 3, T)) & (T - 1)]
            if h == 6:
                give(rng, xa, sp[:15], np.arange(1, 16), np.full(15, d0[qa[0] & 511])); kk = rng.integers(1, 16, T); m = al != qa[0]
                ia[kk[m], al[m]] = sp[kk[m] - 1]
            if h == 7:
                give(rng, xa, sp[:15], np.arange(1, 16), np.full(15, d0[ca & 511])); ia[0] = int(ia[0, ca]); ia[1:] = sp[:15][:, None]
            x[r, g] = xa; ix[r, g] = ia; q[r, g] = qa; c[r, g] = ca
    return pack(x, ix, q, c)
def setup_inputs_ends(rng):
    x = 15 * rng.integers(0, 2, (N, 8, 16, W)); x = np.where(rng.random((N, 8, 1, W)) < 0.5, x[:, :, :1], x)
    fr = rng.random((N, 8, W)) < 0.33; fr[..., 0] = False; fr[..., W - 1] = False
    x = np.where(fr[:, :, None], rng.integers(0, 16, x.shape), x)
    z = 15 * (rng.random((N, 8, 1)) < 0.25).astype(np.int64); x[..., 0] = z; x[..., W - 1] = 15 - z
    d, ix, q, c = blank(); c = (T - 1) * rng.integers(0, 2, (N, 8)); c[:, 0] = 0; c[:, 7] = T - 1
    for r in range(N):
        for g in range(8):
            end = rng.random(T) < 0.65; end[0] = True; end[T - 1] = True
            e = rng.integers(0, 2, (16, T)); e = np.where(rng.random(T) < 0.5, e[:1], e)
            if g % 2 == 0: e[:, 0] = 0
            e[:, T - 1] = rng.integers(0, 2, 16); e[0, T - 1] = 1; e[8, T - 1] = 0; e[15, T - 1] = 1
            ix[r, g] = np.where(end, e * (W - 1), rng.choice(np.nonzero(fr[r, g])[0], (16, T)))
            qa = rng.choice(np.nonzero(~end)[0], K); at = rng.permutation(K)[:2 * K // 3]
            qa[at] = (T - 1) * rng.integers(0, 2, len(at)); qa[K - 1] = T - 1; q[r, g] = qa
    return pack(x, ix, q, c)
def setup_inputs_spread(rng):
    e = rng.choice(np.array([0.5, 1.0, 1.0, 2.0, 3.0]), (N, 8, 1, 1)); i = rng.choice(np.array([1.0, 1.0, 2.0, 3.0]), (N, 8, 1, 1)); j = rng.choice(np.array([1.0, 2.0]), (N, 8, 1))
    x = np.minimum((16 * rng.random((N, 8, 16, W)) ** e).astype(np.int64), 15); ix = np.minimum((W * rng.random((N, 8, 16, T)) ** i).astype(np.int64), W - 1)
    q = np.minimum((T * rng.random((N, 8, K)) ** j).astype(np.int64), T - 1)
    return pack(x, ix, q, rng.integers(0, T, (N, 8)))
def check_inputs(d):
    bad = []
    for k, hi in (("rec", 15), ("idx", W - 1), ("que", T - 1), ("cur", T - 1)):
        v = np.asarray(d[k]).astype(np.float64)
        if not np.all((v >= 0) & (v <= hi)): bad.append("range of " + k)
        elif np.any(v != np.floor(v)): bad.append("whole numbers of " + k)
    return bad
def reference(rec, idx, que, cur):
    x = rec.astype(np.float32).astype(np.int64).reshape(N, 8, 16, W); ix = idx.astype(np.int64).reshape(N, 8, 16, T)
    q = que.astype(np.int64); c = cur.astype(np.int64).reshape(N, 8); kept = np.full((N, 8, 16, K), -1, np.int64); pl = np.arange(K)
    ra = np.arange(N)[:, None, None, None]; ga = np.arange(8)[None, :, None, None]; ka = np.arange(16)[None, None, :, None]
    for t in range(R):
        sr, sg = SR[t % len(SR)], SG[t % len(SG)]
        at = ix[ra, ga, ka, q[:, :, None, :]]
        d = (256 * x[ra, ga, ka, at] + 16 * x[ra, ga, (ka + 1) % 16, at] + x[ra, ga, (ka + 2) % 16, at]) & (W - 1)
        fresh = kept[:, :, 0] < 0; redo = ~fresh & np.any(d != kept, axis=2); sent = ~fresh & ~redo
        lock = np.full((N, 8, W), K, np.int64); np.minimum.at(lock, (ra[..., 0], ga[..., 0], d[:, :, 0]), np.where(sent, pl, K))
        low = np.min(np.take_along_axis(lock, d.reshape(N, 8, 16 * K), 2).reshape(N, 8, 16, K), axis=2)
        go = sent & (low >= pl)
        rr, gg, ii = np.nonzero(go); nm = d[rr, gg, :, ii]; ro, go_ = (rr + sr) % N, (gg + sg) % 8
        v = x[ro[:, None], go_[:, None], :, nm]
        x[ro, go_, :, nm[:, 0]] = (v[:, 0] + np.max(v[:, 1:], axis=1)) & 15
        o = np.argsort(np.where(go, 2, np.where(redo, 1, 0)), axis=2, kind="stable"); n = np.sum(go, axis=2)[..., None]
        tail = pl >= K - n
        q = np.where(tail, (c[..., None] + pl - (K - n)) & (T - 1), np.take_along_axis(q, o, 2))
        kept = np.where(tail[:, :, None], -1, np.take_along_axis(d, o[:, :, None, :], 3)); c = (c + n[..., 0]) & (T - 1)
    return {"yx": x.reshape(N, 128, W).astype(np.float32).astype(BF), "yq": q.astype(np.float32), "yd": kept.reshape(N, 128, K).astype(np.float32)}

@@ -1,0 +1,506 @@
+from concourse.bass import DstId, RemoteDMATransfer
+from concourse.mybir import AluOpType as OP, ActivationFunctionType as AF, AxisListType as AX
+
+W, TX, K, R = 2048, 1024, 256, 7
+SR, SG = (1, 3), (0, 5)
+F32, BF, F16, I32, U16 = "float32", "bfloat16", "float16", "int32", "uint16"
+
+
+def _sb(n, d):
+    return ("sbuf", [128, n], d)
+
+
+SCRATCH = {
+    "X": _sb(2560, BF), "IDX": _sb(TX, I32), "IDQ": _sb(1280, F32), "FR": _sb(TX, F32), "L": _sb(2560, F32),
+    "G": _sb(4096, BF), "LG": _sb(4096, BF), "OG": _sb(4096, BF), "OS": _sb(4096, BF),
+    "E": ("sbuf", [128, 16, 128], BF),
+    "QI": _sb(260, I32), "QF": _sb(258, F16), "QW": _sb(16, U16),
+    "PI": _sb(256, F32), "IA": _sb(256, F32), "IG": _sb(256, F32), "DI": _sb(256, I32), "DJ": _sb(256, I32),
+    "PC": _sb(4, I32), "PF": _sb(10, F32), "IW": _sb(16, F32), "DUM": _sb(16, F32),
+    "ZQ": _sb(144, BF), "BQ": _sb(128, BF), "BB": _sb(256, BF), "B4": _sb(256, BF), "RR": _sb(256, BF),
+    "ZD": _sb(144, BF), "ZC": _sb(144, BF), "II": _sb(256, BF), "NI": _sb(128, BF), "NU": _sb(128, BF),
+    "BW": _sb(128, BF), "DM": _sb(256, BF), "M": _sb(256, F32), "THR": _sb(256, F32), "T0": _sb(256, F32), "T1": _sb(256, F32),
+    "SM": _sb(256, BF), "OM": _sb(1024, BF), "WW": _sb(2064, BF), "W16": _sb(64, BF), "BUMP": _sb(48, BF), "H": _sb(64, F32),
+    "AT": _sb(256, U16), "RM": _sb(256, BF), "NE": _sb(256, BF), "DN": _sb(256, I32), "DA": _sb(256, I32),
+    "S16": _sb(256, F16), "SU": _sb(6 * 256, U16), "S0B": _sb(256, F16), "S0W": _sb(16, F32), "DIF": _sb(16, F32), "NB": _sb(16, F32),
+    "GA": _sb(256, BF), "GS": _sb(256, BF), "W1": _sb(16, F32), "W2": _sb(16, F32), "LO": _sb(16, U16),
+    "LT": _sb(256, BF), "MN": _sb(256, F16), "SC": _sb(256, F16), "OFS": _sb(96, U16),
+    "FL": _sb(48, BF), "CF": _sb(48, BF), "PP": _sb(48, F32), "DW": _sb(16, U16), "TL": _sb(16, U16), "NX": _sb(8, F32),
+    "SW": _sb(6 * 512, F32), "AW": _sb(2 * 512, F32), "TT": _sb(256, BF), "TR": _sb(256, BF),
+    "NM": _sb(6 * 256, U16), "OFF": _sb(96, U16), "ND": ("dram", [6 * 256, 256], U16),
+}
+for _b in range(8):
+    SCRATCH["PS%d" % _b] = ("psum", [128, 512], F32)
+SEMAPHORES = (["eV", "eS", "eP", "eG", "ldq", "ldi", "ldx", "ldc", "st", "ls"]
+              + ["n%d" % t for t in range(1, R)] + ["o%d" % t for t in range(1, R)])
+
+CUT = 192
+NV, LV, OE = 120, 112, 176
+
+
+def _split(v):
+    return (("V", 0, 64), ("S", v, CUT), ("V", 64, v), ("S", CUT, K))
+
+
+def _bits(es):
+    return sum(1 << e for e in es)
+
+
+def _owner(T, r, t):
+    return T.cores[(r + SR[t % 2]) % len(T.cores)]
+
+
+def _relay(T, topo, r):
+    c = T.cores[r]
+    ok = [x for x in topo.cores_of(c) if T.rank_of(x) is None and all(topo.may_write(x, _owner(T, r, t)) for t in range(1, R))]
+    ok.sort(key=lambda x: topo.die(x) != topo.die(c))
+    return ok[0]
+
+
+def _rot(t):
+    return (128 - 16 * SG[t % 2]) % 128
+
+
+def _relay_program(g, core, T, topo, r):
+    src = T.cores[r]
+    nin = len(topo.engines(src, core))
+    total = 0
+    for t in range(1, R):
+        d = _owner(T, r, t)
+        rid, pid = topo.addr(d, core)
+        m = topo.mask(core, d)
+        c = t - 1
+        g.wait_ge(T.sem["n%d" % t], nin)
+        if _rot(t):
+            a = T.ND[256 * c + _rot(t):256 * c + _rot(t) + 128, :]
+        else:
+            a = T.NM[:, 256 * c:256 * c + 256]
+        g.remote_dma(T.NM[:, 256 * c:256 * c + 256], a, T.sem["n%d" % t], T.sem.ls, pid, rid, m)
+        g.wait_ge(T.sem["o%d" % t], nin)
+        g.remote_dma(T.OFF[:, 16 * c:16 * c + 16], T.OFF[:, 16 * c:16 * c + 16], T.sem["o%d" % t], T.sem.ls, pid, rid, m)
+        total += 2 * len(topo.engines(core, d))
+    g.wait_ge(T.sem.ls, total)
+
+
+def rank_program(g, core, T, topo):
+    rank = T.rank_of(core)
+    if rank is None:
+        for r in range(len(T.cores)):
+            if _relay(T, topo, r) == core:
+                _relay_program(g, core, T, topo, r)
+        return
+    n = len(T.cores)
+    Q = {"V": g.vector, "S": g.scalar, "P": g.tensor, "G": g, "Y": g.sync}
+    cnt = {"V": 0, "S": 0, "P": 0, "G": 0}
+    known = {q: {} for q in Q}
+    snap = {}
+    log = {}
+
+    def A(name, a=None, b=None, s=None, p=None):
+        t = T[name]
+        if a is None:
+            a, b = 0, SCRATCH[name][1][1]
+        rows = slice(None) if p is None else slice(p[0], p[1])
+        ap = t[rows, a:b] if s is None else t[rows, a:b:s]
+        return (ap, name, a, b)
+
+    def EB(b, a0, a1):
+        return (T.E[:, b, a0:a1], "E", 128 * b + a0, 128 * b + a1)
+
+    def IND(w, o):
+        return (w[0].indirect(o[0]), w[1], w[2], w[3], o)
+
+    def wait(q, sem, val):
+        if known[q].get(sem, 0) >= val:
+            return
+        Q[q].wait_ge(T.sem[sem], val)
+        known[q][sem] = val
+        for k2, v2 in snap.get((sem, val), {}).items():
+            if known[q].get(k2, 0) < v2:
+                known[q][k2] = v2
+
+    def order(q, outs, ins, ev):
+        acc = [(o, True) for o in outs] + [(i, False) for i in ins]
+        acc += [(x[4], False) for x in outs + ins if len(x) > 4]
+        need = {}
+        for x, wr in acc:
+            ps = x[1].startswith("PS")
+            for lo, hi, w2, q2, e2 in log.get(x[1], []):
+                if q == "P" and q2 == "P":
+                    continue
+                if ps and q2 != q:
+                    hit = True
+                else:
+                    hit = (wr or w2) and lo < x[3] and x[2] < hi
+                if hit and need.get(e2[0], 0) < e2[1]:
+                    need[e2[0]] = e2[1]
+        for sem in sorted(need, key=lambda s: s == "e" + q):
+            wait(q, sem, need[sem])
+        for x, wr in acc:
+            log.setdefault(x[1], []).append((x[2], x[3], wr, q, ev))
+        old = snap.setdefault(ev, {})
+        for k2, v2 in known[q].items():
+            old[k2] = max(old.get(k2, 0), v2)
+
+    def run(q, outs, ins, fn, inc=True):
+        order(q, outs, ins, ("e" + q, cnt[q] + 1))
+        ins_ = fn()
+        if inc:
+            ins_.then_inc(T.sem["e" + q], 1)
+            cnt[q] += 1
+
+    def landed(x, sem, val):
+        log.setdefault(x[1], []).append((x[2], x[3], True, "remote", (sem, val)))
+
+    def aps(*xs):
+        return [x for x in xs if isinstance(x, tuple)]
+
+    def val(x):
+        return x[0] if isinstance(x, tuple) else x
+
+    def cp(o, i):
+        run("V", [o], [i], lambda: g.vector.tensor_copy(o[0], i[0]))
+
+    def tt(o, a, b, op):
+        run("V", [o], [a, b], lambda: g.vector.tensor_tensor(o[0], a[0], b[0], op))
+
+    def ts(o, a, s1, op0, s2=None, op1=None):
+        if s2 is None:
+            run("V", [o], aps(a, s1), lambda: g.vector.tensor_scalar(o[0], a[0], val(s1), None, op0))
+        else:
+            run("V", [o], aps(a, s1, s2), lambda: g.vector.tensor_scalar(o[0], a[0], val(s1), val(s2), op0, op1))
+
+    def scan(o, d0, d1, init, op0, op1):
+        run("V", [o], [d0, d1], lambda: g.vector.tensor_tensor_scan(o[0], d0[0], d1[0], init, op0, op1))
+
+    def ms(o, c):
+        run("V", [o], [], lambda: g.vector.memset(o[0], c))
+
+    def act(o, i, bias=0.0, scale=1.0):
+        f = AF.Copy if (not isinstance(bias, tuple) and bias == 0.0) else AF.Identity
+        run("S", [o], aps(i, bias, scale), lambda: g.scalar.activation(o[0], i[0], f, bias=val(bias), scale=val(scale)))
+
+    def mm(o, l, r, start, stop, inc=None):
+        run("P", [o], [l, r], lambda: g.tensor.matmul(o[0], l[0], r[0], start, stop), stop if inc is None else inc)
+
+    def iota(o, pat, base, cm, fl=True):
+        if fl:
+            run("G", [o], [], lambda: g.iota(o[0], pat, base, cm, allow_small_or_imprecise_dtypes=True))
+        else:
+            run("G", [o], [], lambda: g.iota(o[0], pat, base, cm))
+
+    def dma(q, sem, total, o, i, outs, ins, **kw):
+        order(q, outs, ins, (sem, total))
+        Q[q].dma_start(o, i, **kw).then_inc(T.sem[sem], 16)
+
+    def gather(q, o, i):
+        (cp if q == "V" else act)(o, i)
+
+    rl = _relay(T, topo, rank)
+    rrid, rpid = topo.addr(rl, core)
+    reng = topo.engines(core, rl)
+    sends = 2 * (R - 1) * len(reng)
+
+    def send_names(t):
+        c = t - 1
+        src = A("SU", 256 * c, 256 * c + 256)
+        order("G", [], [src], ("ls", sends))
+        sem = T.sem["n%d" % t]
+        if _rot(t):
+            h = len(reng) // 2
+            g.remote_dma_fused([RemoteDMATransfer(dst_ids=[DstId(rid=rrid, pnc=rpid)], dma_engine_mask=_bits(reng[h * j:h * j + h]), remote_sem=sem,
+                                                  src=src[0], dst=T.ND[256 * c + 128 * j:256 * c + 128 * j + 128, :]) for j in range(2)],
+                               local_sem=T.sem.ls)
+        else:
+            g.remote_dma(T.NM[:, 256 * c:256 * c + 256], src[0], sem, T.sem.ls, rpid, rrid, _bits(reng))
+
+    def send_offsets(t):
+        c = t - 1
+        src = A("OFS", 16 * c, 16 * c + 16)
+        order("G", [], [src], ("ls", sends))
+        g.remote_dma(T.OFF[:, 16 * c:16 * c + 16], src[0], T.sem["o%d" % t], T.sem.ls, rpid, rrid, _bits(reng))
+
+    for t in range(1, R):
+        back = (rank - SR[t % 2]) % n
+        e = len(topo.engines(_relay(T, topo, back), core))
+        landed(A("NM", 256 * (t - 1), 256 * t), "n%d" % t, e)
+        landed(A("OFF", 16 * (t - 1), 16 * t), "o%d" % t, e)
+
+    q8 = (0, 8)
+    dma("Y", "ldq", 16, T.QI[0:8, 0:256], T.que[:], [A("QI", 0, 256)], [])
+    dma("Y", "ldi", 16, T.IDX[:], T.idx[:], [A("IDX")], [])
+    dma("Y", "ldx", 16, T.X[:, 0:W], T.rec[:], [A("X", 0, W)], [])
+
+    PI = A("PI")
+    pa, pg, pz, p15, pq, pw, pp, ph, pc = [A("PF", j, j + 1) for j in range(9)]
+    iota(PI, [[1, 256]], 0, 0)
+    iota(pq, [[0, 1]], 15, 16)
+    iota(A("PC", 0, 1), [[0, 1]], 0, 1, False)
+    iota(A("IG"), [[0, 2], [1, 8], [0, 16]], 0, 0)
+    iota(A("DI"), [[1, 256]], 128, -1, False)
+    iota(A("IA"), [[0, 16], [1, 16]], 0, 0)
+    iota(p15, [[0, 1]], 15, 1)
+    iota(pp, [[0, 1]], 0, 1)
+    dma("G", "ldc", 16, T.QI[0:8, 256:257], T.cur[:], [A("QI", 256, 257)], [], allow_slow_non_contiguous=True)
+    ms(A("WW"), 0.0)
+    for j in range(4):
+        act(A("FR", 256 * j, 256 * j + 256), PI, bias=j / 8.0, scale=1.0 / 2048)
+    act(A("OM"), A("FR"), bias=1.0, scale=0.0)
+    act(A("OM", 1, 1024, 16), A("PI", 0, 64), scale=0.0)
+    act(A("NE"), PI, scale=0.0)
+    act(A("T0"), PI, bias=2048.0, scale=2.0)
+    ts(A("ZQ", p=q8), A("PI", 0, 144, p=q8), A("PF", 4, 5, p=q8), OP.is_equal)
+    ts(A("PC", 1, 2), A("PC", 0, 1), 15, OP.bitwise_and)
+    ts(A("PC", 2, 3), A("PC", 0, 1), 4, OP.arith_shift_right)
+    cp(A("QF", 0, 256, p=q8), A("QI", 0, 256, p=q8))
+    for a in range(16):
+        mm(A("PS2", 0, 16), A("ZQ", 15 - a, 143 - a, p=q8), A("QF", a, 256, 16, p=q8), a == 0, a == 15)
+    cp(A("PF", 0, 2), A("PC", 1, 3))
+    ts(A("DJ"), A("DI"), 15, OP.bitwise_and)
+    ts(A("BB"), A("IG"), pg, OP.is_equal)
+    ts(A("W16", 0, 16), A("DJ", 0, 16), 0.0, OP.is_equal, 256.0, OP.mult)
+    ts(A("W16", 16, 32), A("DJ", 0, 16), 15.0, OP.is_equal, 16.0, OP.mult)
+    ts(A("W16", 32, 48), A("DJ", 0, 16), 14.0, OP.is_equal)
+    ts(pz, pa, 0.0, OP.is_equal)
+    tt(A("W16", 48, 64), A("W16", 0, 16), A("W16", 16, 32), OP.add)
+    cp(A("QW"), A("PS2", 0, 16))
+    tt(A("W16", 0, 16), A("W16", 48, 64), A("W16", 32, 48), OP.add)
+    ts(A("DM"), A("DJ"), 0.0, OP.is_equal)
+    first = A("WW")
+    for j in range(8):
+        o = A("WW", 16 * j, 16 * j + 129 * 15 + 1, 129)
+        ts((o[0], "WW", j, j + 1), A("W16", 0, 16), A("BB", 16 * j, 16 * j + 1), OP.mult)
+    log["WW"].append((0, 2064, True, "V", ("eV", cnt["V"])))
+    act(A("RR"), A("BB"), scale=pz)
+    act(A("B4"), A("BB"), scale=4096.0)
+    act(A("IW"), A("PI", 0, 256, 16), bias=pa)
+    act(A("DUM"), A("IW"), bias=2048.0, scale=2.0)
+    cp(A("AT"), IND(A("IDX"), A("QW")))
+    ts(A("ZD"), A("PI", 0, 144), p15, OP.is_equal, pz, OP.mult)
+    ts(A("H", 0, 16), A("IA", 0, 16), 0.0, OP.not_equal, 0.5, OP.mult)
+    ts(A("H", 16, 32), A("IA", 0, 16), 0.0, OP.is_equal, 4096.0, OP.mult)
+    tt(A("IDQ", 0, TX), A("IDX"), A("FR"), OP.add)
+
+    def late_constants():
+        scan(A("H", 32, 48), A("H", 0, 16), A("H", 16, 32), 0.0, OP.mult, OP.add)
+        ts(A("SM"), A("IA"), 0.0, OP.not_equal)
+        tt(A("H", 48, 64), A("H", 32, 48), A("DM", 0, 16), OP.mult)
+        ms(A("FL"), 0.0)
+        run("V", [pw], [A("H", 48, 64)], lambda: g.vector.tensor_reduce(pw[0], T.H[:, 48:64], AX.X, OP.max))
+        ms(A("BUMP"), 0.0)
+        ts(ph, pw, 0.5, OP.mult)
+
+    def later_constants():
+        tt(A("M"), A("T0"), A("DM"), OP.mult)
+        tt(A("II"), A("DM"), A("BB"), OP.mult)
+        ms(A("BUMP", 32, 33), 16.0)
+
+    def latest_constants():
+        ts(A("T1", 0, 128), A("IA", 0, 128), pa, OP.is_lt, -1.0, OP.mult)
+        ts(pc, pg, 16.0, OP.mult, 15.0, OP.add)
+        ts(A("BQ", p=q8), A("IG", 0, 128, p=q8), A("PF", 6, 7, p=q8), OP.is_equal)
+        cp(A("QF", 256, 257, p=q8), A("QI", 256, 257, p=q8))
+        tt(A("NU"), A("T1", 0, 128), A("BB", 0, 128), OP.mult)
+        mm(A("PS2", 16, 17), A("BQ", p=q8), A("QF", 256, 257, p=q8), True, True)
+        ts(A("ZC"), A("PI", 0, 144), pc, OP.is_equal)
+        cp(A("NX", 0, 1), A("PS2", 16, 17))
+
+    parts = ((0, CUT), (CUT, K))
+
+    def bank(b0, c0, c1):
+        return A("PS%d" % (b0 + (c0 >= CUT)), c0, c1)
+
+    def first_names():
+        mm(A("PS3", 0, 256), A("RR", 0, 128), A("S16"), True, True)
+        for a in range(16):
+            mm(A("PS5", 0, 16), A("ZD", 15 - a, 143 - a), A("S16", a, 256, 16), a == 0, a == 15)
+
+    def first_names_out():
+        cp(A("S0B"), A("PS3", 0, 256))
+        cp(A("S0W"), A("PS5", 0, 16))
+
+    def own_gather(q, t, c0, c1):
+        gather(q, A("OG", 16 * c0, 16 * c1), IND(A("X", 0, W), A("NM", 256 * (t - 1) + c0, 256 * (t - 1) + c1)))
+
+    def own_max(c0, c1):
+        for a in range(c0, c1, 64):
+            b = min(a + 64, c1)
+            scan(A("OS", 16 * a, 16 * b), A("OM", 0, 16 * (b - a)), A("OG", 16 * a, 16 * b), 0.0, OP.mult, OP.max)
+
+    def sums():
+        mm(A("PS1", 0, 256), A("II", 0, 128), A("OG", 0, 4096, 16), True, False)
+        mm(A("PS1", 0, 256), A("II", 0, 128), A("OS", 15, 4096, 16), False, True)
+        act(A("TT"), A("PS1", 0, 256))
+
+    for t in range(1, R):
+        c, u = t - 1, SG[t % 2]
+        SU = 256 * c
+        for q, c0, c1 in _split(NV):
+            gather(q, A("G", 16 * c0, 16 * c1), IND(A("X", 0, W), A("AT", c0, c1)))
+        if t > 1:
+            ts(A("NX", 2, 3), A("NX", 1, 2), 768.0, OP.is_ge, 1024.0, OP.mult)
+            first_names_out()
+            ts(A("NX", 0, 1), A("NX", 1, 2), A("NX", 2, 3), OP.subtract, 256.0, OP.add)
+        else:
+            late_constants()
+        for q, c0, c1 in _split(NV):
+            if t > 1:
+                mm(bank(0, c0, c1), A("NI"), A("S16", c0, c1), True, False)
+            for k in range(16):
+                mm(bank(0, c0, c1), A("WW", 128 * k, 128 * k + 128), A("G", 16 * c0 + k, 16 * c1, 16), t == 1 and k == 0, k == 15)
+        if t == 1:
+            act(A("THR"), A("DM"), scale=pw)
+            act(A("BW"), A("BB", 0, 128), scale=ph)
+            for c0, c1 in parts:
+                ts(A("RM", c0, c1), bank(0, c0, c1), 2048.0, OP.is_ge, 2048.0, OP.mult)
+            for c0, c1 in parts:
+                tt(A("S16", c0, c1), bank(0, c0, c1), A("RM", c0, c1), OP.subtract)
+            first_names()
+            cp(A("SU", 0, 256), A("S16"))
+            send_names(1)
+            first_names_out()
+            tt(A("DIF"), A("S0W"), A("DUM"), OP.subtract)
+            act(A("L", 0, TX), A("FR"), bias=4096.0, scale=0.0)
+            act(A("L", TX, W), A("FR"), bias=4096.0, scale=0.0)
+            act(A("IDQ", TX, 1280), A("IDQ", 0, 256))
+            act(A("AW", 0, 256), IND(A("IDQ", 0, TX), A("QW")))
+            for j in range(6):
+                iota(A("SW", 512 * j, 512 * j + 256), [[0, 256]], -1 if j == 5 else -4096, 0)
+            names = A("S16")
+        else:
+            for c0, c1 in parts:
+                ts(A("RM", c0, c1), bank(0, c0, c1), 1024.0, OP.is_ge, 2048.0, OP.mult)
+                tt(A("NE", c0, c1), bank(0, c0, c1), A("RM", c0, c1), OP.not_equal)
+            for a in range(16):
+                mm(A("PS2", 0, 16), A("ZC", 15 - a, 143 - a), A("NE", a, 256, 16), a == 0, a == 15)
+            tt(A("DIF"), A("S0W"), A("DUM"), OP.subtract)
+            ts(A("NB"), A("S0W"), 0.0, OP.is_lt, 100.0, OP.mult)
+            for c0, c1 in parts:
+                tt(A("DN", c0, c1), bank(0, c0, c1), A("S16", c0, c1), OP.add)
+            names = A("DA")
+            own_gather("S", t, 0, OE)
+        for h, ps in ((1, "PS5"), (0, "PS3")):
+            e0 = 128 * h
+            mm(A(ps, e0, e0 + 128), A("B4", 0, 128), A("NE", e0, e0 + 128), True, False)
+            for b in range(8 * h, 8 * h + 8):
+                wd = e0 + 128 - 16 * b
+                o, i, s = EB(b, 0, wd), A("S0B", 16 * b, e0 + 128), A("S0W", b, b + 1)
+                if t == 1:
+                    ts(o, i, s, OP.is_equal)
+                else:
+                    ts(o, i, s, OP.is_equal, A("PS2", b, b + 1), OP.is_gt)
+                if wd > 16:
+                    mm(A(ps, 16 * b + 16, e0 + 128), A("B4", 0, 128), EB(b, 16, wd), False, False)
+            mm(A(ps, e0, e0 + 128), A("BW"), (T.E[:, 8 * h:8 * h + 8, 0:16], "E", 1024 * h, 1024 * h + 1024), False, True)
+        rot = 16 * ((8 - u) % 8)
+        for c0, c1 in parts:
+            mm(bank(6, c0, c1), A("RR", rot, rot + 128), A("S16", c0, c1), True, False)
+            mm(bank(6, c0, c1), A("B4", rot, rot + 128), A("NE", c0, c1), False, False)
+        tt(A("GA", 128, 256), A("PS5", 128, 256), A("THR", 128, 256), OP.is_lt)
+        if t > 1:
+            tt(A("FL", 16, 32), A("PS2", 0, 16), A("NB"), OP.is_gt)
+        tt(A("GA", 0, 128), A("PS3", 0, 128), A("THR", 0, 128), OP.is_lt)
+        scan(A("GS"), A("SM"), A("GA"), 0.0, OP.mult, OP.add)
+        tt(A("W1"), A("GS", 15, 256, 16), A("DIF"), OP.mult)
+        tt(A("W2"), A("W1"), A("DUM"), OP.add)
+        cp(A("LO"), A("W2"))
+        base = 256.0 * (R - t)
+        for h in (1, 0):
+            ts(IND(A("L"), A("LO", 8 * h, 8 * h + 8)), A("PI", 128 * h, 128 * h + 128), 1.0, OP.mult, base, OP.add)
+        for q, c0, c1 in _split(128 if t == 1 else LV):
+            o, i = A("LG", 16 * c0, 16 * c1), IND(A("L", 0, W), A("SU", SU + c0, SU + c1))
+            if q == "V":
+                ts(o, i, -base, OP.add)
+            else:
+                act(o, i, bias=-base)
+
+        def pick(c0, c1):
+            for k in range(16):
+                mm(bank(4, c0, c1), A("ZD", 15 - k, 143 - k), A("LG", 16 * c0 + k, 16 * c1, 16), k == 0, k == 15)
+
+        for q, c0, c1 in _split(128 if t == 1 else LV)[:3]:
+            pick(c0, c1)
+        if t > 1:
+            own_max(0, 64)
+        else:
+            later_constants()
+        for c0, c1 in parts:
+            tt(A("LT", c0, c1), bank(4, c0, c1), A("PI", c0, c1), OP.is_lt)
+            mm(bank(6, c0, c1), A("B4", rot, rot + 128), A("LT", c0, c1), False, True)
+            if c0 == 0:
+                pick(CUT, K)
+                if t > 1:
+                    ts(A("DA"), A("DN"), W - 1, OP.bitwise_and)
+            tt(A("MN", c0, c1), bank(6, c0, c1), A("M", c0, c1), OP.min)
+            scan(A("SC", c0, c1), A("SM", c0, c1), A("MN", c0, c1), 0.0, OP.mult, OP.add)
+        cp(A("OFS", 16 * c, 16 * c + 16), A("SC", 15, 256, 16))
+        send_offsets(t)
+        if t == 1:
+            own_gather("S", t, 0, 64)
+            own_gather("S", t, 64, 128)
+            latest_constants()
+        else:
+            own_gather("S", t, OE, 256)
+        if u:
+            mm(A("PS0", 0, 16), A("II", 16 * u, 16 * u + 128), A("SC", 15, 256, 16), True, True)
+            if t > 1:
+                own_max(64, 96)
+            ts(A("FL", 32, 48), A("PS0", 0, 16), 2048.0, OP.is_lt)
+        else:
+            ts(A("FL", 32, 48), A("SC", 15, 256, 16), 2048.0, OP.is_lt)
+            own_max(64, 96)
+        tt(A("FL", 0, 16), A("FL", 16, 32), A("FL", 32, 48), OP.is_equal)
+        if t > 1:
+            own_max(96, 112)
+        scan(A("CF"), A("BUMP"), A("FL"), 0.0, OP.add, OP.add)
+        mm(A("PS0", 0, 48), A("NU"), A("FL"), True, False)
+        mm(A("PS0", 0, 48), A("BB", 0, 128), A("CF"), False, True, False)
+        mm(A("PS0", 64, 65), A("BB", 0, 128), A("CF", 31, 32), True, True)
+        if t > 1:
+            own_max(112, OE)
+        tt(A("PP"), A("PS0", 0, 48), A("FL"), OP.mult)
+        tt(A("NX", 1, 2), A("NX", 0, 1), A("PS0", 64, 65), OP.subtract)
+        tt(A("W1"), A("PP", 0, 16), A("PP", 16, 32), OP.add)
+        ts(A("TL"), A("IW"), A("NX", 1, 2), OP.add)
+        tt(A("W2"), A("W1"), A("PP", 32, 48), OP.add)
+        a0, a1 = 512 * (c % 2), 512 * (t % 2)
+        act(A("AW", a1, a1 + 256), IND(A("IDQ"), A("TL")))
+        if t > 1:
+            own_max(OE, 256)
+            sums()
+        else:
+            own_gather("S", t, 128, 192)
+            own_gather("S", t, 192, 256)
+            act(A("NI"), A("II", 0, 128), scale=-1.0)
+        ts(A("DW"), A("W2"), -1.0, OP.add)
+        cp(IND(A("SW", 512 * c, 512 * c + 512), A("DW")), names)
+        kept = A("SW", 512 * c, 512 * c + 256)
+        if t < R - 1:
+            cp(A("SU", SU + 256, SU + 512), kept)
+            send_names(t + 1)
+            cp(A("S16"), kept)
+            first_names()
+        else:
+            dma("Y", "st", 64, T.yd[:], kept[0], [], [kept])
+        if t == 1:
+            own_max(0, 128)
+        cp(IND(A("AW", a1, a1 + 512), A("DW")), A("AW", a0, a0 + 256))
+        if t == 1:
+            own_max(128, 256)
+            sums()
+        if t < R - 1:
+            cp(A("AT"), A("AW", a1, a1 + 256))
+        else:
+            cp(A("DN"), A("AW", a1, a1 + 256))
+            tt(A("T0"), A("AW", a1, a1 + 256), A("DN"), OP.subtract)
+            act(A("T1"), A("T0"), scale=2048.0)
+            dma("Y", "st", 64, T.yq[:], T.T1[0:128:16, :], [], [A("T1")])
+        ts(A("TR"), A("TT"), 16.0, OP.is_ge, -16.0, OP.mult)
+        tt(IND(A("X"), A("OFF", 16 * c, 16 * c + 16)), A("TT"), A("TR"), OP.add)
+
+    dma("Y", "st", 64, T.yx[0:64, :], T.X[0:64, 0:W], [], [A("X")])
+    dma("S", "st", 64, T.yx[64:128, :], T.X[64:128, 0:W], [], [A("X")])
+    for q in ("V", "S", "P", "G"):
+        wait("G", "e" + q, cnt[q])
+    wait("G", "ls", sends)
+    wait("G", "st", 64)

@@ -1,31 +1,42 @@
+import numpy as np
 from concourse.bass import DstId, RemoteDMATransfer
-from concourse.mybir import AluOpType as OP, ActivationFunctionType as AF, AxisListType as AX
+from concourse.mybir import AluOpType as OP, ActivationFunctionType as AF
 
 W, TX, K, R = 2048, 1024, 256, 7
 SR, SG = (1, 3), (0, 5)
 F32, BF, F16, I32, U16 = "float32", "bfloat16", "float16", "int32", "uint16"
+NEW = -40960
+FAR = float(2 ** 26)
 
 
 def _sb(n, d):
-    return ("sbuf", [128, n], d)
+    return ("sbuf", [128] + (list(n) if isinstance(n, tuple) else [n]), d)
 
+
+PASSES = ((64, 128), (128, 192), (192, 256), (0, 64))
+PARTS = ((64, 256), (0, 64))
+NV = 32
+LV1, LS, LV2 = (0, 80), ((80, 144), (144, 192)), (192, 256)
+OWN0, OWN1 = ((0, 48), (48, 112), (112, 176)), ((176, 216), (216, 256))
+FIRST_V, FIRST_S = (0, 96), ((96, 160), (160, 208), (208, 256))
 
 SCRATCH = {
-    "X": _sb(2560, BF), "IDX": _sb(TX, I32), "IDQ": _sb(1280, F32), "FR": _sb(TX, F32), "L": _sb(2560, F32),
-    "G": _sb(4096, BF), "LG": _sb(4096, BF), "OG": _sb(4096, BF), "OS": _sb(4096, BF),
-    "E": ("sbuf", [128, 16, 128], BF),
+    "X": _sb(2560, BF), "IDX": _sb(TX, I32), "IDQ": _sb(1280, F32), "FR": _sb(TX, F32), "L": _sb(2 * 2560, BF),
+    "G": _sb(4096, BF), "LG": _sb(4096, BF), "OG": _sb(4096, BF), "OS": _sb(4096, BF), "PR": _sb(4096, BF),
     "QI": _sb(260, I32), "QF": _sb(258, F16), "QW": _sb(16, U16),
-    "PI": _sb(256, F32), "IA": _sb(256, F32), "IG": _sb(256, F32), "DI": _sb(256, I32), "DJ": _sb(256, I32),
-    "PC": _sb(4, I32), "PF": _sb(10, F32), "IW": _sb(16, F32), "DUM": _sb(16, F32),
-    "ZQ": _sb(144, BF), "BQ": _sb(128, BF), "BB": _sb(256, BF), "B4": _sb(256, BF), "RR": _sb(256, BF),
-    "ZD": _sb(144, BF), "ZC": _sb(144, BF), "II": _sb(256, BF), "NI": _sb(128, BF), "NU": _sb(128, BF),
-    "BW": _sb(128, BF), "DM": _sb(256, BF), "M": _sb(256, F32), "THR": _sb(256, F32), "T0": _sb(256, F32), "T1": _sb(256, F32),
-    "SM": _sb(256, BF), "OM": _sb(1024, BF), "WW": _sb(2064, BF), "W16": _sb(64, BF), "BUMP": _sb(48, BF), "H": _sb(64, F32),
-    "AT": _sb(256, U16), "RM": _sb(256, BF), "NE": _sb(256, BF), "DN": _sb(256, I32), "DA": _sb(256, I32),
-    "S16": _sb(256, F16), "SU": _sb(6 * 256, U16), "S0B": _sb(256, F16), "S0W": _sb(16, F32), "DIF": _sb(16, F32), "NB": _sb(16, F32),
-    "GA": _sb(256, BF), "GS": _sb(256, BF), "W1": _sb(16, F32), "W2": _sb(16, F32), "LO": _sb(16, U16),
-    "LT": _sb(256, BF), "MN": _sb(256, F16), "SC": _sb(256, F16), "OFS": _sb(96, U16),
-    "FL": _sb(48, BF), "CF": _sb(48, BF), "PP": _sb(48, F32), "DW": _sb(16, U16), "TL": _sb(16, U16), "NX": _sb(8, F32),
+    "PI": _sb(256, F32), "PB": _sb(256, BF), "IA": _sb(256, F32), "IG": _sb(256, F32), "DI": _sb(256, I32), "DJ": _sb(256, I32),
+    "PC": _sb(4, I32), "PF": _sb(10, F32), "IW": _sb(16, F32),
+    "ZQ": _sb(144, BF), "BQ": _sb(128, BF), "BB": _sb(256, BF), "B4": _sb(256, BF), "RR": _sb(256, BF), "R4": _sb(256, BF),
+    "ZD": _sb(256, BF), "ZC": _sb(256, BF), "II": _sb(256, BF), "NI": _sb(128, BF), "NU": _sb(256, BF), "IB": _sb(256, BF), "IN": _sb(256, BF),
+    "DM": _sb(256, BF), "ML": _sb(256, F32), "T0": _sb(256, F32), "T1": _sb(256, F32),
+    "OM": _sb(1024, BF), "WW": _sb(2064, BF), "W16": _sb(64, BF),
+    "TRI": _sb((40, 16), BF), "EP": _sb(640, F16), "EM": _sb(640, F16), "EO": _sb(640, F16), "LF": _sb(16, F32),
+    "SLI": _sb(24, I32), "SL": _sb(24, U16), "SRP": _sb(384, F32), "S0W": _sb(16, F32), "LO": _sb(16, U16),
+    "M": _sb(256, F32), "SM": _sb(256, BF), "MN": _sb(256, F16), "SC": _sb(256, F16), "LT": _sb(256, BF), "OFS": _sb(96, U16),
+    "AT": _sb(256, U16), "RM": _sb(256, BF), "NE": _sb((16, 16), BF), "DN": _sb(256, I32), "DA": _sb(256, I32),
+    "S16": _sb((16, 16), F16), "SU": _sb(6 * 256, U16),
+    "FL": _sb(32, BF), "CF": _sb(32, BF), "ZE": _sb(32, BF), "THK": _sb(16, F32), "C3": _sb(48, F16), "M3": _sb(48, F32),
+    "PP": _sb(48, F32), "DW": _sb(16, U16), "TL": _sb(16, U16), "NX": _sb(8, F32),
     "SW": _sb(6 * 512, F32), "AW": _sb(2 * 512, F32), "TT": _sb(256, BF), "TR": _sb(256, BF),
     "NM": _sb(6 * 256, U16), "OFF": _sb(96, U16), "ND": ("dram", [6 * 256, 256], U16),
 }
@@ -33,13 +44,6 @@ for _b in range(8):
     SCRATCH["PS%d" % _b] = ("psum", [128, 512], F32)
 SEMAPHORES = (["eV", "eS", "eP", "eG", "ldq", "ldi", "ldx", "ldc", "st", "ls"]
               + ["n%d" % t for t in range(1, R)] + ["o%d" % t for t in range(1, R)])
-
-CUT = 192
-NV, LV, OE = 120, 112, 176
-
-
-def _split(v):
-    return (("V", 0, 64), ("S", v, CUT), ("V", 64, v), ("S", CUT, K))
 
 
 def _bits(es):
@@ -102,13 +106,20 @@ def rank_program(g, core, T, topo):
             a, b = 0, SCRATCH[name][1][1]
         rows = slice(None) if p is None else slice(p[0], p[1])
         ap = t[rows, a:b] if s is None else t[rows, a:b:s]
-        return (ap, name, a, b)
+        return (ap, name, (1 << b) - (1 << a) if s is None else _bits(range(a, b, s)))
 
-    def EB(b, a0, a1):
-        return (T.E[:, b, a0:a1], "E", 128 * b + a0, 128 * b + a1)
+    def B(name, *ix):
+        dims = SCRATCH[name][1][1:]
+        ix = tuple(slice(None) if i is None else slice(*i) if isinstance(i, tuple) else i for i in ix)
+        ix += (slice(None),) * (len(dims) - len(ix))
+        at = np.arange(int(np.prod(dims))).reshape(dims)[ix]
+        return (T[name][(slice(None),) + ix], name, _bits(at.ravel().tolist()))
+
+    def P16(name, c0, c1):
+        return B(name, (c0 // 16, c1 // 16))
 
     def IND(w, o):
-        return (w[0].indirect(o[0]), w[1], w[2], w[3], o)
+        return (w[0].indirect(o[0]), w[1], w[2], o)
 
     def wait(q, sem, val):
         if known[q].get(sem, 0) >= val:
@@ -121,23 +132,20 @@ def rank_program(g, core, T, topo):
 
     def order(q, outs, ins, ev):
         acc = [(o, True) for o in outs] + [(i, False) for i in ins]
-        acc += [(x[4], False) for x in outs + ins if len(x) > 4]
+        acc += [(x[3], False) for x in outs + ins if len(x) > 3]
         need = {}
         for x, wr in acc:
             ps = x[1].startswith("PS")
-            for lo, hi, w2, q2, e2 in log.get(x[1], []):
+            for cols, w2, q2, e2 in log.get(x[1], []):
                 if q == "P" and q2 == "P":
                     continue
-                if ps and q2 != q:
-                    hit = True
-                else:
-                    hit = (wr or w2) and lo < x[3] and x[2] < hi
+                hit = (ps and q2 != q) or ((wr or w2) and cols & x[2])
                 if hit and need.get(e2[0], 0) < e2[1]:
                     need[e2[0]] = e2[1]
         for sem in sorted(need, key=lambda s: s == "e" + q):
             wait(q, sem, need[sem])
         for x, wr in acc:
-            log.setdefault(x[1], []).append((x[2], x[3], wr, q, ev))
+            log.setdefault(x[1], []).append((x[2], wr, q, ev))
         old = snap.setdefault(ev, {})
         for k2, v2 in known[q].items():
             old[k2] = max(old.get(k2, 0), v2)
@@ -150,7 +158,7 @@ def rank_program(g, core, T, topo):
             cnt[q] += 1
 
     def landed(x, sem, val):
-        log.setdefault(x[1], []).append((x[2], x[3], True, "remote", (sem, val)))
+        log.setdefault(x[1], []).append((x[2], True, "remote", (sem, val)))
 
     def aps(*xs):
         return [x for x in xs if isinstance(x, tuple)]
@@ -176,8 +184,9 @@ def rank_program(g, core, T, topo):
     def ms(o, c):
         run("V", [o], [], lambda: g.vector.memset(o[0], c))
 
-    def act(o, i, bias=0.0, scale=1.0):
-        f = AF.Copy if (not isinstance(bias, tuple) and bias == 0.0) else AF.Identity
+    def act(o, i, bias=0.0, scale=1.0, f=None):
+        if f is None:
+            f = AF.Copy if (not isinstance(bias, tuple) and bias == 0.0) else AF.Identity
         run("S", [o], aps(i, bias, scale), lambda: g.scalar.activation(o[0], i[0], f, bias=val(bias), scale=val(scale)))
 
     def mm(o, l, r, start, stop, inc=None):
@@ -226,30 +235,39 @@ def rank_program(g, core, T, topo):
         landed(A("NM", 256 * (t - 1), 256 * t), "n%d" % t, e)
         landed(A("OFF", 16 * (t - 1), 16 * t), "o%d" % t, e)
 
+    def table(t, width):
+        return A("L", 2560 * (t % 2), 2560 * (t % 2) + width)
+
+    def regions(c0, c1, sbuf=False):
+        m, o = c1 - c0, 480 if sbuf and c0 == 0 else 0
+        whole = lambda name: P16(name, c0, c1)
+        return ((o, o + m, whole), (o + m, o + m + m // 2, lambda name: B(name, (c0 // 16, c1 // 16, 2))), (o + m + m // 2, o + 2 * m + m // 2, whole))
+
     q8 = (0, 8)
     dma("Y", "ldq", 16, T.QI[0:8, 0:256], T.que[:], [A("QI", 0, 256)], [])
     dma("Y", "ldi", 16, T.IDX[:], T.idx[:], [A("IDX")], [])
     dma("Y", "ldx", 16, T.X[:, 0:W], T.rec[:], [A("X", 0, W)], [])
 
     PI = A("PI")
-    pa, pg, pz, p15, pq, pw, pp, ph, pc = [A("PF", j, j + 1) for j in range(9)]
+    pa, pg, pz, pq, pp = [A("PF", j, j + 1) for j in range(5)]
     iota(PI, [[1, 256]], 0, 0)
     iota(pq, [[0, 1]], 15, 16)
     iota(A("PC", 0, 1), [[0, 1]], 0, 1, False)
     iota(A("IG"), [[0, 2], [1, 8], [0, 16]], 0, 0)
     iota(A("DI"), [[1, 256]], 128, -1, False)
     iota(A("IA"), [[0, 16], [1, 16]], 0, 0)
-    iota(p15, [[0, 1]], 15, 1)
+    iota(A("SLI", 0, 16), [[2, 8], [0, 2]], 1, 0, False)
+    iota(A("SLI", 16, 24), [[2, 8]], 0, 0, False)
+    iota(A("T0"), [[0, 8], [32, 2], [0, 16]], W, 2)
+    for c0, c1 in (LV1, LV2):
+        iota(A("PR", 16 * c0, 16 * c1), [[1, c1 - c0], [0, 16]], c0, 0)
     iota(pp, [[0, 1]], 0, 1)
-    dma("G", "ldc", 16, T.QI[0:8, 256:257], T.cur[:], [A("QI", 256, 257)], [], allow_slow_non_contiguous=True)
     ms(A("WW"), 0.0)
     for j in range(4):
         act(A("FR", 256 * j, 256 * j + 256), PI, bias=j / 8.0, scale=1.0 / 2048)
     act(A("OM"), A("FR"), bias=1.0, scale=0.0)
     act(A("OM", 1, 1024, 16), A("PI", 0, 64), scale=0.0)
-    act(A("NE"), PI, scale=0.0)
-    act(A("T0"), PI, bias=2048.0, scale=2.0)
-    ts(A("ZQ", p=q8), A("PI", 0, 144, p=q8), A("PF", 4, 5, p=q8), OP.is_equal)
+    ts(A("ZQ", p=q8), A("PI", 0, 144, p=q8), A("PF", 3, 4, p=q8), OP.is_equal)
     ts(A("PC", 1, 2), A("PC", 0, 1), 15, OP.bitwise_and)
     ts(A("PC", 2, 3), A("PC", 0, 1), 4, OP.arith_shift_right)
     cp(A("QF", 0, 256, p=q8), A("QI", 0, 256, p=q8))
@@ -266,58 +284,104 @@ def rank_program(g, core, T, topo):
     cp(A("QW"), A("PS2", 0, 16))
     tt(A("W16", 0, 16), A("W16", 48, 64), A("W16", 32, 48), OP.add)
     ts(A("DM"), A("DJ"), 0.0, OP.is_equal)
-    first = A("WW")
     for j in range(8):
-        o = A("WW", 16 * j, 16 * j + 129 * 15 + 1, 129)
-        ts((o[0], "WW", j, j + 1), A("W16", 0, 16), A("BB", 16 * j, 16 * j + 1), OP.mult)
-    log["WW"].append((0, 2064, True, "V", ("eV", cnt["V"])))
+        ts(A("WW", 16 * j, 16 * j + 129 * 15 + 1, 129), A("W16", 0, 16), A("BB", 16 * j, 16 * j + 1), OP.mult)
     act(A("RR"), A("BB"), scale=pz)
     act(A("B4"), A("BB"), scale=4096.0)
     act(A("IW"), A("PI", 0, 256, 16), bias=pa)
-    act(A("DUM"), A("IW"), bias=2048.0, scale=2.0)
+    act(A("PB"), PI)
+    act(A("T1"), PI, bias=2048.0, scale=2.0)
+    ms(A("ZD"), 0.0)
+    ms(B("TRI"), 0.0)
+    for j in range(2):
+        ts(A("II", 128 * j, 128 * j + 128), A("DI", 128 * j, 128 * j + 128), 128.0 * j + 128, OP.is_equal)
     cp(A("AT"), IND(A("IDX"), A("QW")))
-    ts(A("ZD"), A("PI", 0, 144), p15, OP.is_equal, pz, OP.mult)
-    ts(A("H", 0, 16), A("IA", 0, 16), 0.0, OP.not_equal, 0.5, OP.mult)
-    ts(A("H", 16, 32), A("IA", 0, 16), 0.0, OP.is_equal, 4096.0, OP.mult)
+    cp(A("ZD", 15, 256, 16), A("RR", 15, 256, 16))
+    for blocks in ((1, 12, 2), (12, 18), (31, 34, 2), (34, 36)):
+        o = B("TRI", blocks)
+        ts(o, A("IA", 0, 16 * len(range(*blocks))), pa, OP.is_ge, FAR, OP.mult)
+    cp(A("SL"), A("SLI"))
     tt(A("IDQ", 0, TX), A("IDX"), A("FR"), OP.add)
+    for j in range(2):
+        act(A("L", 2560 + TX * j, 2560 + TX * j + TX), A("FR"), bias=256.0, scale=0.0)
+    act(A("R4"), A("RR"), scale=4096.0)
+    act(A("NI"), A("II", 0, 128), scale=-1.0)
 
-    def late_constants():
-        scan(A("H", 32, 48), A("H", 0, 16), A("H", 16, 32), 0.0, OP.mult, OP.add)
-        ts(A("SM"), A("IA"), 0.0, OP.not_equal)
-        tt(A("H", 48, 64), A("H", 32, 48), A("DM", 0, 16), OP.mult)
-        ms(A("FL"), 0.0)
-        run("V", [pw], [A("H", 48, 64)], lambda: g.vector.tensor_reduce(pw[0], T.H[:, 48:64], AX.X, OP.max))
-        ms(A("BUMP"), 0.0)
-        ts(ph, pw, 0.5, OP.mult)
+    def lock_constants():
+        ms(A("EM"), 1.0)
+        tt(A("ML"), A("T0"), A("DM"), OP.mult)
+        for c0, c1 in PARTS:
+            (o, e, _), (_, w, _), (_, z, _) = regions(c0, c1, True)
+            ms(A("EM", o, e, 32), 0.0)
+            ms(A("EM", e, z, 16), 0.0)
+            cp(A("EM", o + 31, e, 32), A("T0", c0 + 16, c1, 32))
+            cp(A("EM", e + 15, w, 16), A("T0", c0, c1, 32))
 
-    def later_constants():
-        tt(A("M"), A("T0"), A("DM"), OP.mult)
-        tt(A("II"), A("DM"), A("BB"), OP.mult)
-        ms(A("BUMP", 32, 33), 16.0)
+    def small_constants(part):
+        if part == 0:
+            ms(A("FL"), 0.0)
+            ms(A("ZE"), 0.0)
+            ms(A("THK"), W - 0.5)
+        elif part == 1:
+            ms(A("M3"), 1.0)
+            ms(A("C3", 0, 48, 3), 0.0)
+            ms(A("C3", 1, 48, 3), -1024.0)
+            ts(A("C3", 2, 48, 3), A("IW"), 256.0, OP.add)
+            ms(A("M3", 0, 48, 3), 0.0)
+        elif part == 2:
+            ts(A("BQ", p=q8), A("IG", 0, 128, p=q8), A("PF", 4, 5, p=q8), OP.is_equal)
+            cp(A("QF", 256, 257, p=q8), A("QI", 256, 257, p=q8))
+            mm(A("PS2", 16, 17), A("BQ", p=q8), A("QF", 256, 257, p=q8), True, True)
+        else:
+            ms(A("ZC"), 0.0)
+            ts(A("ZC", 15, 256, 16), A("BB", 15, 256, 16), 2048.0, OP.mult)
 
-    def latest_constants():
-        ts(A("T1", 0, 128), A("IA", 0, 128), pa, OP.is_lt, -1.0, OP.mult)
-        ts(pc, pg, 16.0, OP.mult, 15.0, OP.add)
-        ts(A("BQ", p=q8), A("IG", 0, 128, p=q8), A("PF", 6, 7, p=q8), OP.is_equal)
-        cp(A("QF", 256, 257, p=q8), A("QI", 256, 257, p=q8))
-        tt(A("NU"), A("T1", 0, 128), A("BB", 0, 128), OP.mult)
-        mm(A("PS2", 16, 17), A("BQ", p=q8), A("QF", 256, 257, p=q8), True, True)
-        ts(A("ZC"), A("PI", 0, 144), pc, OP.is_equal)
-        cp(A("NX", 0, 1), A("PS2", 16, 17))
+    def nbank(c0, c1):
+        return A("PS0" if c0 else "PS1", c0, c1)
 
-    parts = ((0, CUT), (CUT, K))
+    def obank(c0, c1):
+        return A("PS7" if c0 >= LV2[0] else "PS6", c0, c1)
 
-    def bank(b0, c0, c1):
-        return A("PS%d" % (b0 + (c0 >= CUT)), c0, c1)
-
-    def first_names():
-        mm(A("PS3", 0, 256), A("RR", 0, 128), A("S16"), True, True)
+    def pick_first():
         for a in range(16):
-            mm(A("PS5", 0, 16), A("ZD", 15 - a, 143 - a), A("S16", a, 256, 16), a == 0, a == 15)
+            mm(A("PS4", 0, 16), A("ZD", 15 - a, 143 - a), B("S16", None, a), a == 0, a == 15)
 
-    def first_names_out():
-        cp(A("S0B"), A("PS3", 0, 256))
-        cp(A("S0W"), A("PS5", 0, 16))
+    def open_compare(t):
+        for (c0, c1), ps, blocks in zip(PARTS, ("PS3", "PS5"), ((0, 30), (30, 40))):
+            mm(A(ps, 0, 16 * (blocks[1] - blocks[0])), A("II", 0, 128), B("TRI", blocks), True, False)
+            for j, (a, b, view) in enumerate(regions(c0, c1)):
+                mm(A(ps, a, b), A("RR", 0, 128), view("S16"), False, t == 1 and j == 2)
+
+    def close_compare(ps, c0, c1):
+        for j, (a, b, view) in enumerate(regions(c0, c1)):
+            mm(A(ps, a, b), A("B4", 0, 128), view("NE"), False, j == 2)
+
+    def spread_first():
+        act(A("S0W"), A("PS4", 0, 16))
+        act(A("SRP"), IND(A("S0W"), A("SL")))
+
+    def compare(ps, c0, c1):
+        (_, m, _), (_, h, _), (_, e, _) = regions(c0, c1)
+        o = regions(c0, c1, True)[0][0]
+        tt(A("EP", o + h, o + e), A(ps, h, e), A("ML", c0, c1), OP.min)
+        tt(A("EP", o + m, o + h), A(ps, m, h), A("SRP", 256 + c0 // 2, 256 + c1 // 2), OP.is_equal)
+        tt(A("EP", o, o + m), A(ps, 0, m), A("SRP", c0, c1), OP.is_equal)
+
+    def lock_scan(c0, c1):
+        o, e = regions(c0, c1, True)[0][0], regions(c0, c1, True)[2][1]
+        scan(A("EO", o, e), A("EM", o, e), A("EP", o, e), 0.0, OP.mult, OP.max)
+
+    def lock_max(c0, c1):
+        (o, e, _), (_, w, _), (_, z, _) = regions(c0, c1, True)
+        tt(A("LF", c0 // 16, c1 // 16, 2), A("EO", e + 15, w, 16), A("EO", w + 15, z, 32), OP.max)
+        tt(A("LF", c0 // 16 + 1, c1 // 16, 2), A("EO", o + 31, e, 32), A("EO", w + 31, z, 32), OP.max)
+
+    def lock_list(c0, c1):
+        cp(A("LO", c0 // 16, c1 // 16), A("LF", c0 // 16, c1 // 16))
+
+    def lock_write(t, es):
+        for e in es:
+            cp(IND(table(t, 2560), A("LO", 2 * e, 2 * e + 2)), A("PB", 32 * e, 32 * e + 32))
 
     def own_gather(q, t, c0, c1):
         gather(q, A("OG", 16 * c0, 16 * c1), IND(A("X", 0, W), A("NM", 256 * (t - 1) + c0, 256 * (t - 1) + c1)))
@@ -327,179 +391,221 @@ def rank_program(g, core, T, topo):
             b = min(a + 64, c1)
             scan(A("OS", 16 * a, 16 * b), A("OM", 0, 16 * (b - a)), A("OG", 16 * a, 16 * b), 0.0, OP.mult, OP.max)
 
-    def sums():
-        mm(A("PS1", 0, 256), A("II", 0, 128), A("OG", 0, 4096, 16), True, False)
-        mm(A("PS1", 0, 256), A("II", 0, 128), A("OS", 15, 4096, 16), False, True)
-        act(A("TT"), A("PS1", 0, 256))
+    def sums(c0, c1):
+        mm(A("PS1", c0, c1), A("II", 0, 128), A("OG", 16 * c0, 16 * c1, 16), True, False)
+        mm(A("PS1", c0, c1), A("II", 0, 128), A("OS", 16 * c0 + 15, 16 * c1, 16), False, True)
+
+    def clamp(c0, c1):
+        tt(A("MN", c0, c1), obank(c0, c1), A("M", c0, c1), OP.min)
+
+    def offsets(c0, c1):
+        scan(A("SC", c0, c1), A("SM", c0, c1), A("MN", c0, c1), 0.0, OP.mult, OP.add)
 
     for t in range(1, R):
         c, u = t - 1, SG[t % 2]
         SU = 256 * c
-        for q, c0, c1 in _split(NV):
-            gather(q, A("G", 16 * c0, 16 * c1), IND(A("X", 0, W), A("AT", c0, c1)))
+        rot, back = 16 * ((8 - u) % 8), 16 * u
+        for c0, c1 in PASSES:
+            for q, a, b in (("V", c0, c0 + NV), ("S", c0 + NV, c1)):
+                gather(q, A("G", 16 * a, 16 * b), IND(A("X", 0, W), A("AT", a, b)))
         if t > 1:
-            ts(A("NX", 2, 3), A("NX", 1, 2), 768.0, OP.is_ge, 1024.0, OP.mult)
-            first_names_out()
-            ts(A("NX", 0, 1), A("NX", 1, 2), A("NX", 2, 3), OP.subtract, 256.0, OP.add)
-        else:
-            late_constants()
-        for q, c0, c1 in _split(NV):
+            for a in range(16):
+                mm(A("PS2", 0, 16), A("ZD", 15 - a + rot, 143 - a + rot), B("S16", None, a), a == 0, False)
+            open_compare(t)
+        for c0, c1 in PASSES:
             if t > 1:
-                mm(bank(0, c0, c1), A("NI"), A("S16", c0, c1), True, False)
+                mm(nbank(c0, c1), A("NI"), P16("S16", c0, c1), True, False)
             for k in range(16):
-                mm(bank(0, c0, c1), A("WW", 128 * k, 128 * k + 128), A("G", 16 * c0 + k, 16 * c1, 16), t == 1 and k == 0, k == 15)
+                mm(nbank(c0, c1), A("WW", 128 * k, 128 * k + 128), A("G", 16 * c0 + k, 16 * c1, 16), t == 1 and k == 0, k == 15)
+        (a0, a1), (b0, b1) = PARTS
         if t == 1:
-            act(A("THR"), A("DM"), scale=pw)
-            act(A("BW"), A("BB", 0, 128), scale=ph)
-            for c0, c1 in parts:
-                ts(A("RM", c0, c1), bank(0, c0, c1), 2048.0, OP.is_ge, 2048.0, OP.mult)
-            for c0, c1 in parts:
-                tt(A("S16", c0, c1), bank(0, c0, c1), A("RM", c0, c1), OP.subtract)
-            first_names()
-            cp(A("SU", 0, 256), A("S16"))
+            ts(A("RM", a0, a1), nbank(a0, a1), 2048.0, OP.is_ge, 2048.0, OP.mult)
+            small_constants(0)
+            tt(P16("S16", a0, a1), nbank(a0, a1), A("RM", a0, a1), OP.subtract)
+            small_constants(1)
+            ts(A("RM", b0, b1), nbank(b0, b1), 2048.0, OP.is_ge, 2048.0, OP.mult)
+            cp(A("SU", a0, a1), P16("S16", a0, a1))
+            tt(P16("S16", b0, b1), nbank(b0, b1), A("RM", b0, b1), OP.subtract)
+            pick_first()
+            open_compare(t)
+            ts(A("LT"), A("IA"), pa, OP.is_le, -1.0, OP.mult)
+            cp(A("SU", b0, b1), P16("S16", b0, b1))
             send_names(1)
-            first_names_out()
-            tt(A("DIF"), A("S0W"), A("DUM"), OP.subtract)
-            act(A("L", 0, TX), A("FR"), bias=4096.0, scale=0.0)
-            act(A("L", TX, W), A("FR"), bias=4096.0, scale=0.0)
+            act(A("IB"), A("II"), scale=1024.0)
+            act(A("IN"), A("II"), scale=-1024.0)
+            spread_first()
+            lock_constants()
+            cp(A("DA"), B("S16"))
             act(A("IDQ", TX, 1280), A("IDQ", 0, 256))
             act(A("AW", 0, 256), IND(A("IDQ", 0, TX), A("QW")))
-            for j in range(6):
-                iota(A("SW", 512 * j, 512 * j + 256), [[0, 256]], -1 if j == 5 else -4096, 0)
-            names = A("S16")
+            iota(table(2, W), [[0, W]], 256, 0)
+            iota(A("SW", 0, 256), [[0, 256]], NEW, 0)
+            dma("G", "ldc", 16, T.QI[0:8, 256:257], T.cur[:], [A("QI", 256, 257)], [], allow_slow_non_contiguous=True)
+            compare("PS3", a0, a1)
+            compare("PS5", b0, b1)
+            lock_scan(a0, a1)
+            lock_scan(b0, b1)
+            lock_max(a0, a1)
+            lock_max(b0, b1)
+            ts(A("SM"), A("IA"), 0.0, OP.not_equal)
+            lock_list(0, K)
+            for e in range(7, -1, -1):
+                tt(A("NU" if e % 2 else "M", 64 * (e // 2), 64 * (e // 2) + 64), A("LT" if e % 2 else "T1", 64 * (e // 2), 64 * (e // 2) + 64),
+                   A("BB" if e % 2 else "DM", 64 * (e // 2), 64 * (e // 2) + 64), OP.mult)
+                lock_write(t, (e,))
         else:
-            for c0, c1 in parts:
-                ts(A("RM", c0, c1), bank(0, c0, c1), 1024.0, OP.is_ge, 2048.0, OP.mult)
-                tt(A("NE", c0, c1), bank(0, c0, c1), A("RM", c0, c1), OP.not_equal)
+            spread_first()
+            for c0, c1 in OWN0:
+                own_gather("S", t, c0, c1)
+            ts(A("RM", a0, a1), nbank(a0, a1), 1024.0, OP.is_ge, 2048.0, OP.mult)
+            ts(A("NX", 2, 3), A("NX", 1, 2), 768.0, OP.is_ge, 1024.0, OP.mult)
+            tt(P16("NE", a0, a1), nbank(a0, a1), A("RM", a0, a1), OP.not_equal)
+            close_compare("PS3", a0, a1)
+            tt(A("DN", a0, a1), nbank(a0, a1), P16("S16", a0, a1), OP.add)
+            ts(A("RM", b0, b1), nbank(b0, b1), 1024.0, OP.is_ge, 2048.0, OP.mult)
+            ts(A("NX", 0, 1), A("NX", 1, 2), A("NX", 2, 3), OP.subtract, 256.0, OP.add)
+            tt(P16("NE", b0, b1), nbank(b0, b1), A("RM", b0, b1), OP.not_equal)
+            close_compare("PS5", b0, b1)
             for a in range(16):
-                mm(A("PS2", 0, 16), A("ZC", 15 - a, 143 - a), A("NE", a, 256, 16), a == 0, a == 15)
-            tt(A("DIF"), A("S0W"), A("DUM"), OP.subtract)
-            ts(A("NB"), A("S0W"), 0.0, OP.is_lt, 100.0, OP.mult)
-            for c0, c1 in parts:
-                tt(A("DN", c0, c1), bank(0, c0, c1), A("S16", c0, c1), OP.add)
-            names = A("DA")
-            own_gather("S", t, 0, OE)
-        for h, ps in ((1, "PS5"), (0, "PS3")):
-            e0 = 128 * h
-            mm(A(ps, e0, e0 + 128), A("B4", 0, 128), A("NE", e0, e0 + 128), True, False)
-            for b in range(8 * h, 8 * h + 8):
-                wd = e0 + 128 - 16 * b
-                o, i, s = EB(b, 0, wd), A("S0B", 16 * b, e0 + 128), A("S0W", b, b + 1)
-                if t == 1:
-                    ts(o, i, s, OP.is_equal)
-                else:
-                    ts(o, i, s, OP.is_equal, A("PS2", b, b + 1), OP.is_gt)
-                if wd > 16:
-                    mm(A(ps, 16 * b + 16, e0 + 128), A("B4", 0, 128), EB(b, 16, wd), False, False)
-            mm(A(ps, e0, e0 + 128), A("BW"), (T.E[:, 8 * h:8 * h + 8, 0:16], "E", 1024 * h, 1024 * h + 1024), False, True)
-        rot = 16 * ((8 - u) % 8)
-        for c0, c1 in parts:
-            mm(bank(6, c0, c1), A("RR", rot, rot + 128), A("S16", c0, c1), True, False)
-            mm(bank(6, c0, c1), A("B4", rot, rot + 128), A("NE", c0, c1), False, False)
-        tt(A("GA", 128, 256), A("PS5", 128, 256), A("THR", 128, 256), OP.is_lt)
-        if t > 1:
-            tt(A("FL", 16, 32), A("PS2", 0, 16), A("NB"), OP.is_gt)
-        tt(A("GA", 0, 128), A("PS3", 0, 128), A("THR", 0, 128), OP.is_lt)
-        scan(A("GS"), A("SM"), A("GA"), 0.0, OP.mult, OP.add)
-        tt(A("W1"), A("GS", 15, 256, 16), A("DIF"), OP.mult)
-        tt(A("W2"), A("W1"), A("DUM"), OP.add)
-        cp(A("LO"), A("W2"))
-        base = 256.0 * (R - t)
-        for h in (1, 0):
-            ts(IND(A("L"), A("LO", 8 * h, 8 * h + 8)), A("PI", 128 * h, 128 * h + 128), 1.0, OP.mult, base, OP.add)
-        for q, c0, c1 in _split(128 if t == 1 else LV):
-            o, i = A("LG", 16 * c0, 16 * c1), IND(A("L", 0, W), A("SU", SU + c0, SU + c1))
-            if q == "V":
-                ts(o, i, -base, OP.add)
-            else:
-                act(o, i, bias=-base)
+                mm(A("PS2", 0, 16), A("ZC", 15 - a + rot, 143 - a + rot), B("NE", None, a), False, a == 15)
+            compare("PS3", a0, a1)
+            tt(A("DN", b0, b1), nbank(b0, b1), P16("S16", b0, b1), OP.add)
+            lock_scan(a0, a1)
+            compare("PS5", b0, b1)
+            lock_max(a0, a1)
+            lock_scan(b0, b1)
+            ts(A("FL", 16, 32), A("PS2", 0, 16), 2048.0, OP.is_ge)
+            lock_list(a0, a1)
+            lock_max(b0, b1)
+            between = [lambda: (lock_list(b0, b1), ts(A("THK"), A("FL", 16, 32), 8192.0, OP.mult, W - 0.5, OP.add))]
+            between += [lambda a=a: ts(A("DA", a, a + 128), A("DN", a, a + 128), W - 1, OP.bitwise_and) for a in (0, 128)]
+            between += [lambda a=a: own_max(a, a + 12) for a in (0, 12, 24, 36)]
+            for e in range(7, -1, -1):
+                lock_write(t, (e,))
+                if between:
+                    between.pop(0)()
+        for c0, c1 in ((0, LV2[0]), LV2):
+            mm(obank(c0, c1), A("RR", rot, rot + 128), P16("S16", c0, c1), True, False)
+            if t > 1:
+                mm(obank(c0, c1), A("B4", rot, rot + 128), P16("NE", c0, c1), False, False)
+        s0, s1 = LS[0][0], LS[-1][1]
+
+        def waits(c0, c1):
+            tt(A("LG", 16 * c0, 16 * c1), IND(table(t, W), A("SU", SU + c0, SU + c1)), A("PR", 16 * c0, 16 * c1), OP.is_lt)
+
+        def count(c0, c1, stop):
+            for k in range(16):
+                mm(obank(c0, c1), A("R4", rot, rot + 128), A("LG", 16 * c0 + k, 16 * c1, 16), False, stop and k == 15)
 
         def pick(c0, c1):
+            mm(A("PS4", c0, c1), A("NI"), A("PB", c0, c1), True, False)
             for k in range(16):
-                mm(bank(4, c0, c1), A("ZD", 15 - k, 143 - k), A("LG", 16 * c0 + k, 16 * c1, 16), k == 0, k == 15)
+                mm(A("PS4", c0, c1), A("ZD", 15 - k, 143 - k), A("LG", 16 * c0 + k, 16 * c1, 16), False, k == 15)
 
-        for q, c0, c1 in _split(128 if t == 1 else LV)[:3]:
-            pick(c0, c1)
+        waits(*LV1)
+        for c0, c1 in LS:
+            act(A("LG", 16 * c0, 16 * c1), IND(table(t, W), A("SU", SU + c0, SU + c1)))
+        waits(*LV2)
+        pick(*LS[0])
+        count(*LV1, False)
+        pick(*LS[1])
+        act(A("LT", s0, s1), A("PS4", s0, s1), scale=-1.0, f=AF.Relu)
+        count(*LV2, True)
+        mm(obank(s0, s1), A("B4", rot, rot + 128), A("LT", s0, s1), False, True)
         if t > 1:
-            own_max(0, 64)
+            own_max(48, 112)
+            for c0, c1 in OWN1:
+                own_gather("S", t, c0, c1)
         else:
-            later_constants()
-        for c0, c1 in parts:
-            tt(A("LT", c0, c1), bank(4, c0, c1), A("PI", c0, c1), OP.is_lt)
-            mm(bank(6, c0, c1), A("B4", rot, rot + 128), A("LT", c0, c1), False, True)
-            if c0 == 0:
-                pick(CUT, K)
-                if t > 1:
-                    ts(A("DA"), A("DN"), W - 1, OP.bitwise_and)
-            tt(A("MN", c0, c1), bank(6, c0, c1), A("M", c0, c1), OP.min)
-            scan(A("SC", c0, c1), A("SM", c0, c1), A("MN", c0, c1), 0.0, OP.mult, OP.add)
+            small_constants(3)
+        clamp(*LV2)
+        clamp(0, LV2[0])
+        offsets(*LV2)
+        offsets(0, LV2[0])
+        if t == 1:
+            small_constants(2)
+        else:
+            own_max(112, 128)
         cp(A("OFS", 16 * c, 16 * c + 16), A("SC", 15, 256, 16))
         send_offsets(t)
-        if t == 1:
-            own_gather("S", t, 0, 64)
-            own_gather("S", t, 64, 128)
-            latest_constants()
-        else:
-            own_gather("S", t, OE, 256)
-        if u:
-            mm(A("PS0", 0, 16), A("II", 16 * u, 16 * u + 128), A("SC", 15, 256, 16), True, True)
-            if t > 1:
-                own_max(64, 96)
-            ts(A("FL", 32, 48), A("PS0", 0, 16), 2048.0, OP.is_lt)
-        else:
-            ts(A("FL", 32, 48), A("SC", 15, 256, 16), 2048.0, OP.is_lt)
-            own_max(64, 96)
-        tt(A("FL", 0, 16), A("FL", 16, 32), A("FL", 32, 48), OP.is_equal)
+        def cand(j):
+            return A("PS0", j, 48, 3)
+
+        def un(name):
+            return A(name, back, back + 128)
+
+        keep, redo = A("FL", 0, 16), A("FL", 16, 32)
+        tt(keep, A("SC", 15, 256, 16), A("THK"), OP.is_gt)
+        mm(A("PS0", 0, 48), A("II", 0, 128), A("C3"), True, False)
         if t > 1:
-            own_max(96, 112)
-        scan(A("CF"), A("BUMP"), A("FL"), 0.0, OP.add, OP.add)
-        mm(A("PS0", 0, 48), A("NU"), A("FL"), True, False)
-        mm(A("PS0", 0, 48), A("BB", 0, 128), A("CF"), False, True, False)
-        mm(A("PS0", 64, 65), A("BB", 0, 128), A("CF", 31, 32), True, True)
+            mm(cand(1), un("NU"), redo, False, False)
+            mm(cand(1), un("IB"), redo, False, False)
+            mm(cand(2), un("IN"), redo, False, False)
+            own_max(128, 144)
+        else:
+            cp(A("NX", 0, 1), A("PS2", 16, 17))
+        scan(A("CF"), A("ZE"), A("FL"), 0.0, OP.add, OP.add)
+        mm(cand(0), un("NU"), keep, False, False)
+        mm(cand(2), un("IN"), keep, False, False)
+        mm(cand(0), un("BB"), A("CF", 0, 16), False, False)
+        mm(cand(1), un("BB"), A("CF", 16, 32), False, True, False)
+        mm(A("PS0", 64, 65), un("BB"), A("CF", 31, 32), True, True)
         if t > 1:
-            own_max(112, OE)
-        tt(A("PP"), A("PS0", 0, 48), A("FL"), OP.mult)
+            own_max(144, 192)
+        scan(A("PP"), A("M3"), A("PS0", 0, 48), 0.0, OP.mult, OP.max)
+        ts(A("TL"), A("IW"), A("NX", 0, 1), OP.add, A("PS0", 64, 65), OP.subtract)
         tt(A("NX", 1, 2), A("NX", 0, 1), A("PS0", 64, 65), OP.subtract)
-        tt(A("W1"), A("PP", 0, 16), A("PP", 16, 32), OP.add)
-        ts(A("TL"), A("IW"), A("NX", 1, 2), OP.add)
-        tt(A("W2"), A("W1"), A("PP", 32, 48), OP.add)
-        a0, a1 = 512 * (c % 2), 512 * (t % 2)
-        act(A("AW", a1, a1 + 256), IND(A("IDQ"), A("TL")))
+        cp(A("DW"), A("PP", 2, 48, 3))
+        w0, w1 = 512 * (c % 2), 512 * (t % 2)
+        act(A("AW", w1, w1 + 256), IND(A("IDQ"), A("TL")))
         if t > 1:
-            own_max(OE, 256)
-            sums()
+            own_max(192, 216)
         else:
-            own_gather("S", t, 128, 192)
-            own_gather("S", t, 192, 256)
-            act(A("NI"), A("II", 0, 128), scale=-1.0)
-        ts(A("DW"), A("W2"), -1.0, OP.add)
-        cp(IND(A("SW", 512 * c, 512 * c + 512), A("DW")), names)
+            for c0, c1 in FIRST_S:
+                own_gather("S", t, c0, c1)
+        cp(IND(A("SW", 512 * c, 512 * c + 512), A("DW")), A("DA"))
         kept = A("SW", 512 * c, 512 * c + 256)
+        if t > 1:
+            own_max(216, K)
+            sums(0, K)
+            act(A("TT"), A("PS1", 0, K))
         if t < R - 1:
             cp(A("SU", SU + 256, SU + 512), kept)
             send_names(t + 1)
-            cp(A("S16"), kept)
-            first_names()
+            if t + 2 < R:
+                iota(table(t + 2, W), [[0, W]], 256, 0)
+            iota(A("SW", 512 * t, 512 * t + 256), [[0, 256]], -1 if t == R - 2 else NEW, 0)
+            cp(B("S16"), kept)
         else:
             dma("Y", "st", 64, T.yd[:], kept[0], [], [kept])
-        if t == 1:
-            own_max(0, 128)
-        cp(IND(A("AW", a1, a1 + 512), A("DW")), A("AW", a0, a0 + 256))
-        if t == 1:
-            own_max(128, 256)
-            sums()
         if t < R - 1:
-            cp(A("AT"), A("AW", a1, a1 + 256))
+            pick_first()
+        cp(IND(A("AW", w1, w1 + 512), A("DW")), A("AW", w0, w0 + 256))
+        if t == 1:
+            last = FIRST_S[-1][0]
+            own_gather("V", t, *FIRST_V)
+            cp(A("AT"), A("AW", w1, w1 + 256))
+            own_max(0, last)
+            sums(0, last)
+            act(A("TT", 0, last), A("PS1", 0, last))
+            own_max(last, K)
+            sums(last, K)
+            ts(A("TR", 0, last), A("TT", 0, last), 16.0, OP.is_ge, -16.0, OP.mult)
+            ts(A("TR", last, K), A("PS1", last, K), 16.0, OP.is_ge, -16.0, OP.mult)
+            cp(A("TT", last, K), A("PS1", last, K))
         else:
-            cp(A("DN"), A("AW", a1, a1 + 256))
-            tt(A("T0"), A("AW", a1, a1 + 256), A("DN"), OP.subtract)
-            act(A("T1"), A("T0"), scale=2048.0)
-            dma("Y", "st", 64, T.yq[:], T.T1[0:128:16, :], [], [A("T1")])
-        ts(A("TR"), A("TT"), 16.0, OP.is_ge, -16.0, OP.mult)
+            ts(A("TR"), A("TT"), 16.0, OP.is_ge, -16.0, OP.mult)
+            if t < R - 1:
+                cp(A("AT"), A("AW", w1, w1 + 256))
         tt(IND(A("X"), A("OFF", 16 * c, 16 * c + 16)), A("TT"), A("TR"), OP.add)
 
     dma("Y", "st", 64, T.yx[0:64, :], T.X[0:64, 0:W], [], [A("X")])
     dma("S", "st", 64, T.yx[64:128, :], T.X[64:128, 0:W], [], [A("X")])
+    w1 = 512 * ((R - 1) % 2)
+    cp(A("DN"), A("AW", w1, w1 + 256))
+    tt(A("T0"), A("AW", w1, w1 + 256), A("DN"), OP.subtract)
+    act(A("T1"), A("T0"), scale=2048.0)
+    dma("Y", "st", 64, T.yq[:], T.T1[0:128:16, :], [], [A("T1")])
     for q in ("V", "S", "P", "G"):
         wait("G", "e" + q, cnt[q])
     wait("G", "ls", sends)

@@ -13,12 +13,16 @@ def _sb(n, d):
     return ("sbuf", [128] + (list(n) if isinstance(n, tuple) else [n]), d)
 
 
-PASSES = ((64, 128), (128, 192), (192, 256), (0, 64))
-PARTS = ((64, 256), (0, 64))
-NV = 32
+PASSES = ((192, 256), (128, 192), (64, 128), (0, 64))
+NV = (32, 32, 28, 20)
+CMP = ("PS3", "PS5", "PS6", "PS7")
+START = "v0 n0 v1 n1 t0 a2 r0 b2 n2 u0 g0 t1 a3 r1 b3 n3 t2 u1 r2"
+LATER = "v0 n0 v1 n1 t0 a2 d0 c0 b2 n2 t1 k0 d1 c1 s0 a3 l0 b3 n3 t2 w7 k1 d2 c2 w6 s1 t3 l1 d3 c3 z0 w5 k2 w4 s2 k3 l2 s3 w3 l3 w2 e0 e1 w1 e2 e3 w0"
+FIRST = "k0 k1 s0 k2 s1 l0 k3 s2 w7 l1 s3 w6 l2 l3 w5 p0 w4 p1 w3 p2 w2 p3 w1 p4 w0"
+FILL = ("x2 x0 m0-3 x3 x1 x4 x5", "m3-4", "m4-5", "m5-8", "m8-9", "m9-11", "m11-16")
 LV1, LS, LV2 = (0, 80), ((80, 144), (144, 192)), (192, 256)
-OWN0, OWN1 = ((0, 48), (48, 112), (112, 176)), ((176, 216), (216, 256))
-FIRST_V, FIRST_S = (0, 96), ((96, 160), (160, 208), (208, 256))
+OWN0, OWN1 = ((0, 48), (48, 96), (96, 144)), ((144, 200), (200, 256))
+FILL1 = ("p5 p6 p7", "q2", "", "", "q3", "m12-16", "m8-12")
 
 SCRATCH = {
     "X": _sb(2560, BF), "IDX": _sb(TX, I32), "IDQ": _sb(1280, F32), "FR": _sb(TX, F32), "L": _sb(2 * 2560, BF),
@@ -28,9 +32,9 @@ SCRATCH = {
     "PC": _sb(4, I32), "PF": _sb(10, F32), "IW": _sb(16, F32),
     "ZQ": _sb(144, BF), "BQ": _sb(128, BF), "BB": _sb(256, BF), "B4": _sb(256, BF), "RR": _sb(256, BF), "R4": _sb(256, BF),
     "ZD": _sb(256, BF), "ZC": _sb(256, BF), "II": _sb(256, BF), "NI": _sb(128, BF), "NU": _sb(256, BF), "IB": _sb(256, BF), "IN": _sb(256, BF),
-    "DM": _sb(256, BF), "ML": _sb(256, F32), "T0": _sb(256, F32), "T1": _sb(256, F32),
+    "DM": _sb(256, BF), "ML": _sb((6, 16), F32), "DU": _sb(2, F32), "T0": _sb(256, F32), "T1": _sb(256, F32),
     "OM": _sb(1024, BF), "WW": _sb(2064, BF), "W16": _sb(64, BF),
-    "TRI": _sb((40, 16), BF), "EP": _sb(640, F16), "EM": _sb(640, F16), "EO": _sb(640, F16), "LF": _sb(16, F32),
+    "TRI": _sb((12, 16), BF), "EP": _sb(768, F16), "EM": _sb(192, F16), "EO": _sb(768, F16),
     "SLI": _sb(24, I32), "SL": _sb(24, U16), "SRP": _sb(384, F32), "S0W": _sb(16, F32), "LO": _sb(16, U16),
     "M": _sb(256, F32), "SM": _sb(256, BF), "MN": _sb(256, F16), "SC": _sb(256, F16), "LT": _sb(256, BF), "OFS": _sb(96, U16),
     "AT": _sb(256, U16), "RM": _sb(256, BF), "NE": _sb((16, 16), BF), "DN": _sb(256, I32), "DA": _sb(256, I32),
@@ -38,12 +42,22 @@ SCRATCH = {
     "FL": _sb(32, BF), "CF": _sb(32, BF), "ZE": _sb(32, BF), "THK": _sb(16, F32), "C3": _sb(48, F16), "M3": _sb(48, F32),
     "PP": _sb(48, F32), "DW": _sb(16, U16), "TL": _sb(16, U16), "NX": _sb(8, F32),
     "SW": _sb(6 * 512, F32), "AW": _sb(2 * 512, F32), "TT": _sb(256, BF), "TR": _sb(256, BF),
-    "NM": _sb(6 * 256, U16), "OFF": _sb(96, U16), "ND": ("dram", [6 * 256, 256], U16),
+    "NM": _sb(6 * 256, U16), "OFF": _sb(96, U16),
 }
+
+
+def _names(t):
+    c = 256 * (t - 1)
+    return (("n1", *PASSES[0]), ("m1", 0, PASSES[0][0])) if t == 1 else (("n%d" % t, c, c + 256),)
+
+
 for _b in range(8):
     SCRATCH["PS%d" % _b] = ("psum", [128, 512], F32)
+for _t in range(1, R, 2):
+    for _name, _a, _b in _names(_t):
+        SCRATCH["D" + _name] = ("dram", [256, _b - _a], U16)
 SEMAPHORES = (["eV", "eS", "eP", "eG", "ldq", "ldi", "ldx", "ldc", "st", "ls"]
-              + ["n%d" % t for t in range(1, R)] + ["o%d" % t for t in range(1, R)])
+              + [m[0] for t in range(1, R) for m in _names(t)] + ["o%d" % t for t in range(1, R)])
 
 
 def _bits(es):
@@ -74,15 +88,13 @@ def _relay_program(g, core, T, topo, r):
         rid, pid = topo.addr(d, core)
         m = topo.mask(core, d)
         c = t - 1
-        g.wait_ge(T.sem["n%d" % t], nin)
-        if _rot(t):
-            a = T.ND[256 * c + _rot(t):256 * c + _rot(t) + 128, :]
-        else:
-            a = T.NM[:, 256 * c:256 * c + 256]
-        g.remote_dma(T.NM[:, 256 * c:256 * c + 256], a, T.sem["n%d" % t], T.sem.ls, pid, rid, m)
+        for name, a, b in _names(t):
+            g.wait_ge(T.sem[name], nin)
+            here = T["D" + name][_rot(t):_rot(t) + 128, :] if _rot(t) else T.NM[:, a:b]
+            g.remote_dma(T.NM[:, a:b], here, T.sem[name], T.sem.ls, pid, rid, m)
         g.wait_ge(T.sem["o%d" % t], nin)
         g.remote_dma(T.OFF[:, 16 * c:16 * c + 16], T.OFF[:, 16 * c:16 * c + 16], T.sem["o%d" % t], T.sem.ls, pid, rid, m)
-        total += 2 * len(topo.engines(core, d))
+        total += (len(_names(t)) + 1) * len(topo.engines(core, d))
     g.wait_ge(T.sem.ls, total)
 
 
@@ -208,20 +220,20 @@ def rank_program(g, core, T, topo):
     rl = _relay(T, topo, rank)
     rrid, rpid = topo.addr(rl, core)
     reng = topo.engines(core, rl)
-    sends = 2 * (R - 1) * len(reng)
+    sends = sum(len(_names(t)) + 1 for t in range(1, R)) * len(reng)
 
-    def send_names(t):
-        c = t - 1
-        src = A("SU", 256 * c, 256 * c + 256)
+    def send_names(t, j=0):
+        name, a, b = _names(t)[j]
+        src = A("SU", a, b)
         order("G", [], [src], ("ls", sends))
-        sem = T.sem["n%d" % t]
+        sem = T.sem[name]
         if _rot(t):
             h = len(reng) // 2
-            g.remote_dma_fused([RemoteDMATransfer(dst_ids=[DstId(rid=rrid, pnc=rpid)], dma_engine_mask=_bits(reng[h * j:h * j + h]), remote_sem=sem,
-                                                  src=src[0], dst=T.ND[256 * c + 128 * j:256 * c + 128 * j + 128, :]) for j in range(2)],
+            g.remote_dma_fused([RemoteDMATransfer(dst_ids=[DstId(rid=rrid, pnc=rpid)], dma_engine_mask=_bits(reng[h * i:h * i + h]), remote_sem=sem,
+                                                  src=src[0], dst=T["D" + name][128 * i:128 * i + 128, :]) for i in range(2)],
                                local_sem=T.sem.ls)
         else:
-            g.remote_dma(T.NM[:, 256 * c:256 * c + 256], src[0], sem, T.sem.ls, rpid, rrid, _bits(reng))
+            g.remote_dma(T.NM[:, a:b], src[0], sem, T.sem.ls, rpid, rrid, _bits(reng))
 
     def send_offsets(t):
         c = t - 1
@@ -232,16 +244,12 @@ def rank_program(g, core, T, topo):
     for t in range(1, R):
         back = (rank - SR[t % 2]) % n
         e = len(topo.engines(_relay(T, topo, back), core))
-        landed(A("NM", 256 * (t - 1), 256 * t), "n%d" % t, e)
+        for name, a, b in _names(t):
+            landed(A("NM", a, b), name, e)
         landed(A("OFF", 16 * (t - 1), 16 * t), "o%d" % t, e)
 
     def table(t, width):
         return A("L", 2560 * (t % 2), 2560 * (t % 2) + width)
-
-    def regions(c0, c1, sbuf=False):
-        m, o = c1 - c0, 480 if sbuf and c0 == 0 else 0
-        whole = lambda name: P16(name, c0, c1)
-        return ((o, o + m, whole), (o + m, o + m + m // 2, lambda name: B(name, (c0 // 16, c1 // 16, 2))), (o + m + m // 2, o + 2 * m + m // 2, whole))
 
     q8 = (0, 8)
     dma("Y", "ldq", 16, T.QI[0:8, 0:256], T.que[:], [A("QI", 0, 256)], [])
@@ -256,9 +264,9 @@ def rank_program(g, core, T, topo):
     iota(A("IG"), [[0, 2], [1, 8], [0, 16]], 0, 0)
     iota(A("DI"), [[1, 256]], 128, -1, False)
     iota(A("IA"), [[0, 16], [1, 16]], 0, 0)
-    iota(A("SLI", 0, 16), [[2, 8], [0, 2]], 1, 0, False)
-    iota(A("SLI", 16, 24), [[2, 8]], 0, 0, False)
-    iota(A("T0"), [[0, 8], [32, 2], [0, 16]], W, 2)
+    for j, b in enumerate((1, 1, 3, 3, 0, 2)):
+        iota(A("SLI", j, 24, 6), [[-4, 4]], 12 + b, 0, False)
+    iota(A("DU"), [[32, 2]], W, 2)
     for c0, c1 in (LV1, LV2):
         iota(A("PR", 16 * c0, 16 * c1), [[1, c1 - c0], [0, 16]], c0, 0)
     iota(pp, [[0, 1]], 0, 1)
@@ -297,10 +305,11 @@ def rank_program(g, core, T, topo):
         ts(A("II", 128 * j, 128 * j + 128), A("DI", 128 * j, 128 * j + 128), 128.0 * j + 128, OP.is_equal)
     cp(A("AT"), IND(A("IDX"), A("QW")))
     cp(A("ZD", 15, 256, 16), A("RR", 15, 256, 16))
-    for blocks in ((1, 12, 2), (12, 18), (31, 34, 2), (34, 36)):
-        o = B("TRI", blocks)
-        ts(o, A("IA", 0, 16 * len(range(*blocks))), pa, OP.is_ge, FAR, OP.mult)
+    own = ((1, 4, 2), (4, 6))
+    for blocks in own:
+        ts(B("TRI", blocks), A("IA", 0, 32), pa, OP.is_ge, FAR, OP.mult)
     cp(A("SL"), A("SLI"))
+    ms(A("S0W"), 0.0)
     tt(A("IDQ", 0, TX), A("IDX"), A("FR"), OP.add)
     for j in range(2):
         act(A("L", 2560 + TX * j, 2560 + TX * j + TX), A("FR"), bias=256.0, scale=0.0)
@@ -308,14 +317,13 @@ def rank_program(g, core, T, topo):
     act(A("NI"), A("II", 0, 128), scale=-1.0)
 
     def lock_constants():
-        ms(A("EM"), 1.0)
-        tt(A("ML"), A("T0"), A("DM"), OP.mult)
-        for c0, c1 in PARTS:
-            (o, e, _), (_, w, _), (_, z, _) = regions(c0, c1, True)
-            ms(A("EM", o, e, 32), 0.0)
-            ms(A("EM", e, z, 16), 0.0)
-            cp(A("EM", o + 31, e, 32), A("T0", c0 + 16, c1, 32))
-            cp(A("EM", e + 15, w, 16), A("T0", c0, c1, 32))
+        ms(B("ML", (0, 3, 2)), 0.0)
+        for blocks, j in zip(own, (1, 0)):
+            ts(B("ML", blocks), A("DM", 0, 32), A("DU", j, j + 1), OP.mult)
+        ms(A("EM", 0, 192, 2), 1.0)
+        ts(A("EM", 1, 192, 2), B("ML"), 1.0, OP.max)
+        ms(A("EM", 0, 128, 64), 0.0)
+        ms(A("EM", 128, 192, 32), 0.0)
 
     def small_constants(part):
         if part == 0:
@@ -336,52 +344,45 @@ def rank_program(g, core, T, topo):
             ms(A("ZC"), 0.0)
             ts(A("ZC", 15, 256, 16), A("BB", 15, 256, 16), 2048.0, OP.mult)
 
-    def nbank(c0, c1):
-        return A("PS0" if c0 else "PS1", c0, c1)
-
     def obank(c0, c1):
         return A("PS7" if c0 >= LV2[0] else "PS6", c0, c1)
 
-    def pick_first():
+    def pick_first(ps="PS4", b0=0, b1=16):
         for a in range(16):
-            mm(A("PS4", 0, 16), A("ZD", 15 - a, 143 - a), B("S16", None, a), a == 0, a == 15)
+            mm(A(ps, b0, b1), A("ZD", 15 - a, 143 - a), B("S16", (b0, b1), a), a == 0, a == 15)
 
-    def open_compare(t):
-        for (c0, c1), ps, blocks in zip(PARTS, ("PS3", "PS5"), ((0, 30), (30, 40))):
-            mm(A(ps, 0, 16 * (blocks[1] - blocks[0])), A("II", 0, 128), B("TRI", blocks), True, False)
-            for j, (a, b, view) in enumerate(regions(c0, c1)):
-                mm(A(ps, a, b), A("RR", 0, 128), view("S16"), False, t == 1 and j == 2)
+    def open_compare(t, passes=range(4)):
+        for p in passes:
+            mm(A(CMP[p], 0, 192), A("II", 0, 128), B("TRI"), True, False)
+            views(p, "RR", "S16", t == 1)
 
-    def close_compare(ps, c0, c1):
-        for j, (a, b, view) in enumerate(regions(c0, c1)):
-            mm(A(ps, a, b), A("B4", 0, 128), view("NE"), False, j == 2)
+    def views(p, weights, name, stop):
+        b = PASSES[p][0] // 16
+        for o in (0, 96):
+            mm(A(CMP[p], o, o + 64), A(weights, 0, 128), B(name, (b, b + 4)), False, False)
+            mm(A(CMP[p], o + 64, o + 96), A(weights, 0, 128), B(name, (b, b + 4, 2)), False, stop and o == 96)
 
-    def spread_first():
-        act(A("S0W"), A("PS4", 0, 16))
-        act(A("SRP"), IND(A("S0W"), A("SL")))
+    def close_compare(p):
+        views(p, "B4", "NE", True)
 
-    def compare(ps, c0, c1):
-        (_, m, _), (_, h, _), (_, e, _) = regions(c0, c1)
-        o = regions(c0, c1, True)[0][0]
-        tt(A("EP", o + h, o + e), A(ps, h, e), A("ML", c0, c1), OP.min)
-        tt(A("EP", o + m, o + h), A(ps, m, h), A("SRP", 256 + c0 // 2, 256 + c1 // 2), OP.is_equal)
-        tt(A("EP", o, o + m), A(ps, 0, m), A("SRP", c0, c1), OP.is_equal)
+    def spread_first(ps="PS4", b0=0, b1=16, p0=0, p1=4):
+        act(A("S0W", b0, b1), A(ps, b0, b1))
+        act(A("SRP", 96 * p0, 96 * p1), IND(A("S0W", 0, b1), A("SL", 6 * p0, 6 * p1)))
 
-    def lock_scan(c0, c1):
-        o, e = regions(c0, c1, True)[0][0], regions(c0, c1, True)[2][1]
-        scan(A("EO", o, e), A("EM", o, e), A("EP", o, e), 0.0, OP.mult, OP.max)
+    def compare(p):
+        tt(A("EP", 192 * p + 1, 192 * p + 192, 2), A(CMP[p], 96, 192), B("ML"), OP.min)
+        tt(A("EP", 192 * p, 192 * p + 192, 2), A(CMP[p], 0, 96), A("SRP", 96 * p, 96 * p + 96), OP.is_equal)
 
-    def lock_max(c0, c1):
-        (o, e, _), (_, w, _), (_, z, _) = regions(c0, c1, True)
-        tt(A("LF", c0 // 16, c1 // 16, 2), A("EO", e + 15, w, 16), A("EO", w + 15, z, 32), OP.max)
-        tt(A("LF", c0 // 16 + 1, c1 // 16, 2), A("EO", o + 31, e, 32), A("EO", w + 31, z, 32), OP.max)
+    def lock_scan(p):
+        scan(A("EO", 192 * p, 192 * p + 192), A("EM"), A("EP", 192 * p, 192 * p + 192), 0.0, OP.mult, OP.max)
 
-    def lock_list(c0, c1):
-        cp(A("LO", c0 // 16, c1 // 16), A("LF", c0 // 16, c1 // 16))
+    def lock_list(p):
+        b = PASSES[p][0] // 16
+        cp(A("LO", b + 1, b + 4, 2), A("EO", 192 * p + 63, 192 * p + 128, 64))
+        cp(A("LO", b, b + 4, 2), A("EO", 192 * p + 159, 192 * p + 192, 32))
 
-    def lock_write(t, es):
-        for e in es:
-            cp(IND(table(t, 2560), A("LO", 2 * e, 2 * e + 2)), A("PB", 32 * e, 32 * e + 32))
+    def lock_write(t, e):
+        cp(IND(table(t, 2560), A("LO", 2 * e, 2 * e + 2)), A("PB", 32 * e, 32 * e + 32))
 
     def own_gather(q, t, c0, c1):
         gather(q, A("OG", 16 * c0, 16 * c1), IND(A("X", 0, W), A("NM", 256 * (t - 1) + c0, 256 * (t - 1) + c1)))
@@ -391,9 +392,9 @@ def rank_program(g, core, T, topo):
             b = min(a + 64, c1)
             scan(A("OS", 16 * a, 16 * b), A("OM", 0, 16 * (b - a)), A("OG", 16 * a, 16 * b), 0.0, OP.mult, OP.max)
 
-    def sums(c0, c1):
-        mm(A("PS1", c0, c1), A("II", 0, 128), A("OG", 16 * c0, 16 * c1, 16), True, False)
-        mm(A("PS1", c0, c1), A("II", 0, 128), A("OS", 16 * c0 + 15, 16 * c1, 16), False, True)
+    def sums(c0, c1, ps="PS1"):
+        mm(A(ps, c0, c1), A("II", 0, 128), A("OG", 16 * c0, 16 * c1, 16), True, False)
+        mm(A(ps, c0, c1), A("II", 0, 128), A("OS", 16 * c0 + 15, 16 * c1, 16), False, True)
 
     def clamp(c0, c1):
         tt(A("MN", c0, c1), obank(c0, c1), A("M", c0, c1), OP.min)
@@ -405,85 +406,103 @@ def rank_program(g, core, T, topo):
         c, u = t - 1, SG[t % 2]
         SU = 256 * c
         rot, back = 16 * ((8 - u) % 8), 16 * u
-        for c0, c1 in PASSES:
-            for q, a, b in (("V", c0, c0 + NV), ("S", c0 + NV, c1)):
-                gather(q, A("G", 16 * a, 16 * b), IND(A("X", 0, W), A("AT", a, b)))
+        def nbank(p):
+            return A(("PS0", "PS1", "PS6", "PS7")[p if t == 1 else p % 2], *PASSES[p])
+
+        def digits(q, p, half=None):
+            c0, c1 = PASSES[p]
+            v = c0 + (32 if t == 1 else NV[p])
+            a, b = (c0, v) if q == "V" else (v, c1)
+            if half is not None:
+                a, b = (a, (a + b) // 4 * 2) if half == 0 else ((a + b) // 4 * 2, b)
+            gather(q, A("G", 16 * a, 16 * b), IND(A("X", 0, W), A("AT", a, b)))
+
+        def weigh(p):
+            c0, c1 = PASSES[p]
+            if t > 1:
+                mm(nbank(p), A("NI"), P16("S16", c0, c1), True, False)
+            for k in range(16):
+                mm(nbank(p), A("WW", 128 * k, 128 * k + 128), A("G", 16 * c0 + k, 16 * c1, 16), t == 1 and k == 0, k == 15)
+
+        def top(p):
+            ts(A("RM", *PASSES[p]), nbank(p), 2048.0 if t == 1 else 1024.0, OP.is_ge, 2048.0, OP.mult)
+
+        def differ(p):
+            tt(P16("NE", *PASSES[p]), nbank(p), A("RM", *PASSES[p]), OP.not_equal)
+
+        def restore(p):
+            tt(A("DN", *PASSES[p]), nbank(p), P16("S16", *PASSES[p]), OP.add)
+
+        def count_changed(_):
+            for a in range(16):
+                mm(A("PS2", 0, 16), A("ZC", 15 - a + rot, 143 - a + rot), B("NE", None, a), False, a == 15)
+
+        def small(j):
+            if j == 0:
+                ts(A("NX", 2, 3), A("NX", 1, 2), 768.0, OP.is_ge, 1024.0, OP.mult)
+            elif j == 1:
+                ts(A("NX", 0, 1), A("NX", 1, 2), A("NX", 2, 3), OP.subtract, 256.0, OP.add)
+            elif j == 2:
+                ts(A("FL", 16, 32), A("PS2", 0, 16), 2048.0, OP.is_ge)
+            elif j == 3:
+                ts(A("THK"), A("FL", 16, 32), 8192.0, OP.mult, W - 0.5, OP.add)
+            else:
+                a = 128 * (j - 4)
+                ts(A("DA", a, a + 128), A("DN", a, a + 128), W - 1, OP.bitwise_and)
+
+        step = {"v": lambda p: digits("V", p), "a": lambda p: digits("V", p, 0), "b": lambda p: digits("V", p, 1), "n": weigh, "t": top, "d": differ, "e": restore,
+                "c": close_compare, "k": compare, "s": lock_scan, "l": lock_list, "w": lambda e: lock_write(t, e), "z": count_changed,
+                "x": small, "m": lambda a, b: own_max(16 * a, 16 * b)}
+
+        def steps(text):
+            for s in text.split():
+                step[s[0]](*[int(j) for j in s[1:].split("-")])
+
+        def fill(j):
+            steps((FILL if t > 1 else FILL1)[j])
+
         if t > 1:
             for a in range(16):
                 mm(A("PS2", 0, 16), A("ZD", 15 - a + rot, 143 - a + rot), B("S16", None, a), a == 0, False)
             open_compare(t)
-        for c0, c1 in PASSES:
-            if t > 1:
-                mm(nbank(c0, c1), A("NI"), P16("S16", c0, c1), True, False)
-            for k in range(16):
-                mm(nbank(c0, c1), A("WW", 128 * k, 128 * k + 128), A("G", 16 * c0 + k, 16 * c1, 16), t == 1 and k == 0, k == 15)
-        (a0, a1), (b0, b1) = PARTS
-        if t == 1:
-            ts(A("RM", a0, a1), nbank(a0, a1), 2048.0, OP.is_ge, 2048.0, OP.mult)
-            small_constants(0)
-            tt(P16("S16", a0, a1), nbank(a0, a1), A("RM", a0, a1), OP.subtract)
-            small_constants(1)
-            ts(A("RM", b0, b1), nbank(b0, b1), 2048.0, OP.is_ge, 2048.0, OP.mult)
-            cp(A("SU", a0, a1), P16("S16", a0, a1))
-            tt(P16("S16", b0, b1), nbank(b0, b1), A("RM", b0, b1), OP.subtract)
-            pick_first()
-            open_compare(t)
+            for p in range(4):
+                digits("S", p)
+            for c0, c1 in OWN0:
+                own_gather("S", t, c0, c1)
+            steps(LATER)
+        else:
+            step["r"] = lambda p: tt(P16("S16", *PASSES[p]), nbank(p), A("RM", *PASSES[p]), OP.subtract)
+            step["u"] = lambda p: cp(A("SU", *PASSES[p]), P16("S16", *PASSES[p]))
+            step["g"] = lambda j: send_names(1, j)
+            step["q"] = small_constants
+            for p in range(4):
+                digits("S", p)
+            steps(START)
+            pick_first("PS4", 4, 16)
+            open_compare(t, range(3))
+            lock_constants()
+            steps("t3 u2 r3")
+            pick_first("PS2", 0, 4)
+            open_compare(t, (3,))
+            spread_first("PS4", 4, 16, 0, 3)
             ts(A("LT"), A("IA"), pa, OP.is_le, -1.0, OP.mult)
-            cp(A("SU", b0, b1), P16("S16", b0, b1))
-            send_names(1)
+            steps("u3 g1 q0 q1")
+            spread_first("PS2", 0, 4, 3, 4)
             act(A("IB"), A("II"), scale=1024.0)
             act(A("IN"), A("II"), scale=-1024.0)
-            spread_first()
-            lock_constants()
-            cp(A("DA"), B("S16"))
             act(A("IDQ", TX, 1280), A("IDQ", 0, 256))
             act(A("AW", 0, 256), IND(A("IDQ", 0, TX), A("QW")))
             iota(table(2, W), [[0, W]], 256, 0)
             iota(A("SW", 0, 256), [[0, 256]], NEW, 0)
             dma("G", "ldc", 16, T.QI[0:8, 256:257], T.cur[:], [A("QI", 256, 257)], [], allow_slow_non_contiguous=True)
-            compare("PS3", a0, a1)
-            compare("PS5", b0, b1)
-            lock_scan(a0, a1)
-            lock_scan(b0, b1)
-            lock_max(a0, a1)
-            lock_max(b0, b1)
-            ts(A("SM"), A("IA"), 0.0, OP.not_equal)
-            lock_list(0, K)
-            for e in range(7, -1, -1):
-                tt(A("NU" if e % 2 else "M", 64 * (e // 2), 64 * (e // 2) + 64), A("LT" if e % 2 else "T1", 64 * (e // 2), 64 * (e // 2) + 64),
-                   A("BB" if e % 2 else "DM", 64 * (e // 2), 64 * (e // 2) + 64), OP.mult)
-                lock_write(t, (e,))
-        else:
-            spread_first()
-            for c0, c1 in OWN0:
-                own_gather("S", t, c0, c1)
-            ts(A("RM", a0, a1), nbank(a0, a1), 1024.0, OP.is_ge, 2048.0, OP.mult)
-            ts(A("NX", 2, 3), A("NX", 1, 2), 768.0, OP.is_ge, 1024.0, OP.mult)
-            tt(P16("NE", a0, a1), nbank(a0, a1), A("RM", a0, a1), OP.not_equal)
-            close_compare("PS3", a0, a1)
-            tt(A("DN", a0, a1), nbank(a0, a1), P16("S16", a0, a1), OP.add)
-            ts(A("RM", b0, b1), nbank(b0, b1), 1024.0, OP.is_ge, 2048.0, OP.mult)
-            ts(A("NX", 0, 1), A("NX", 1, 2), A("NX", 2, 3), OP.subtract, 256.0, OP.add)
-            tt(P16("NE", b0, b1), nbank(b0, b1), A("RM", b0, b1), OP.not_equal)
-            close_compare("PS5", b0, b1)
-            for a in range(16):
-                mm(A("PS2", 0, 16), A("ZC", 15 - a + rot, 143 - a + rot), B("NE", None, a), False, a == 15)
-            compare("PS3", a0, a1)
-            tt(A("DN", b0, b1), nbank(b0, b1), P16("S16", b0, b1), OP.add)
-            lock_scan(a0, a1)
-            compare("PS5", b0, b1)
-            lock_max(a0, a1)
-            lock_scan(b0, b1)
-            ts(A("FL", 16, 32), A("PS2", 0, 16), 2048.0, OP.is_ge)
-            lock_list(a0, a1)
-            lock_max(b0, b1)
-            between = [lambda: (lock_list(b0, b1), ts(A("THK"), A("FL", 16, 32), 8192.0, OP.mult, W - 0.5, OP.add))]
-            between += [lambda a=a: ts(A("DA", a, a + 128), A("DN", a, a + 128), W - 1, OP.bitwise_and) for a in (0, 128)]
-            between += [lambda a=a: own_max(a, a + 12) for a in (0, 12, 24, 36)]
-            for e in range(7, -1, -1):
-                lock_write(t, (e,))
-                if between:
-                    between.pop(0)()
+
+            def product(j):
+                a = 64 * (j % 4)
+                o, x, y = ("NU", "LT", "BB") if j < 4 else ("M", "T1", "DM")
+                tt(A(o, a, a + 64), A(x, a, a + 64), A(y, a, a + 64), OP.mult)
+
+            step["p"] = product
+            steps(FIRST)
         for c0, c1 in ((0, LV2[0]), LV2):
             mm(obank(c0, c1), A("RR", rot, rot + 128), P16("S16", c0, c1), True, False)
             if t > 1:
@@ -513,19 +532,18 @@ def rank_program(g, core, T, topo):
         count(*LV2, True)
         mm(obank(s0, s1), A("B4", rot, rot + 128), A("LT", s0, s1), False, True)
         if t > 1:
-            own_max(48, 112)
             for c0, c1 in OWN1:
                 own_gather("S", t, c0, c1)
         else:
-            small_constants(3)
+            for c0, c1 in PASSES[:2]:
+                own_gather("S", t, c0, c1)
+            ts(A("SM"), A("IA"), 0.0, OP.not_equal)
+        fill(0)
         clamp(*LV2)
         clamp(0, LV2[0])
         offsets(*LV2)
         offsets(0, LV2[0])
-        if t == 1:
-            small_constants(2)
-        else:
-            own_max(112, 128)
+        fill(1)
         cp(A("OFS", 16 * c, 16 * c + 16), A("SC", 15, 256, 16))
         send_offsets(t)
         def cand(j):
@@ -541,34 +559,31 @@ def rank_program(g, core, T, topo):
             mm(cand(1), un("NU"), redo, False, False)
             mm(cand(1), un("IB"), redo, False, False)
             mm(cand(2), un("IN"), redo, False, False)
-            own_max(128, 144)
         else:
             cp(A("NX", 0, 1), A("PS2", 16, 17))
+        fill(2)
         scan(A("CF"), A("ZE"), A("FL"), 0.0, OP.add, OP.add)
         mm(cand(0), un("NU"), keep, False, False)
         mm(cand(2), un("IN"), keep, False, False)
         mm(cand(0), un("BB"), A("CF", 0, 16), False, False)
         mm(cand(1), un("BB"), A("CF", 16, 32), False, True, False)
         mm(A("PS0", 64, 65), un("BB"), A("CF", 31, 32), True, True)
-        if t > 1:
-            own_max(144, 192)
+        fill(3)
+        if t == 1:
+            cp(A("DA"), B("S16"))
         scan(A("PP"), A("M3"), A("PS0", 0, 48), 0.0, OP.mult, OP.max)
         ts(A("TL"), A("IW"), A("NX", 0, 1), OP.add, A("PS0", 64, 65), OP.subtract)
         tt(A("NX", 1, 2), A("NX", 0, 1), A("PS0", 64, 65), OP.subtract)
         cp(A("DW"), A("PP", 2, 48, 3))
         w0, w1 = 512 * (c % 2), 512 * (t % 2)
         act(A("AW", w1, w1 + 256), IND(A("IDQ"), A("TL")))
-        if t > 1:
-            own_max(192, 216)
-        else:
-            for c0, c1 in FIRST_S:
+        if t == 1:
+            for c0, c1 in PASSES[2:]:
                 own_gather("S", t, c0, c1)
+        fill(4)
         cp(IND(A("SW", 512 * c, 512 * c + 512), A("DW")), A("DA"))
         kept = A("SW", 512 * c, 512 * c + 256)
-        if t > 1:
-            own_max(216, K)
-            sums(0, K)
-            act(A("TT"), A("PS1", 0, K))
+        fill(5)
         if t < R - 1:
             cp(A("SU", SU + 256, SU + 512), kept)
             send_names(t + 1)
@@ -580,23 +595,27 @@ def rank_program(g, core, T, topo):
             dma("Y", "st", 64, T.yd[:], kept[0], [], [kept])
         if t < R - 1:
             pick_first()
+        fill(6)
+        if t > 1:
+            sums(0, K)
+            act(A("TT"), A("PS1", 0, K))
         cp(IND(A("AW", w1, w1 + 512), A("DW")), A("AW", w0, w0 + 256))
         if t == 1:
-            last = FIRST_S[-1][0]
-            own_gather("V", t, *FIRST_V)
+            own_max(*PASSES[2])
+            sums(64, K)
+            act(A("TT", 64, K), A("PS1", 64, K))
             cp(A("AT"), A("AW", w1, w1 + 256))
-            own_max(0, last)
-            sums(0, last)
-            act(A("TT", 0, last), A("PS1", 0, last))
-            own_max(last, K)
-            sums(last, K)
-            ts(A("TR", 0, last), A("TT", 0, last), 16.0, OP.is_ge, -16.0, OP.mult)
-            ts(A("TR", last, K), A("PS1", last, K), 16.0, OP.is_ge, -16.0, OP.mult)
-            cp(A("TT", last, K), A("PS1", last, K))
+            own_max(*PASSES[3])
+            sums(0, 64, "PS0")
+            ts(A("TR", 64, K), A("TT", 64, K), 16.0, OP.is_ge, -16.0, OP.mult)
+            ts(A("TR", 0, 64), A("PS0", 0, 64), 16.0, OP.is_ge, -16.0, OP.mult)
+            cp(A("TT", 0, 64), A("PS0", 0, 64))
         else:
             ts(A("TR"), A("TT"), 16.0, OP.is_ge, -16.0, OP.mult)
             if t < R - 1:
                 cp(A("AT"), A("AW", w1, w1 + 256))
+        if t < R - 1:
+            spread_first()
         tt(IND(A("X"), A("OFF", 16 * c, 16 * c + 16)), A("TT"), A("TR"), OP.add)
 
     dma("Y", "st", 64, T.yx[0:64, :], T.X[0:64, 0:W], [], [A("X")])

@@ -1,11 +1,12 @@
 import numpy as np
 from concourse.bass import DstId, RemoteDMATransfer
-from concourse.mybir import AluOpType as OP, ActivationFunctionType as AF
+from concourse.mybir import AluOpType as OP, ActivationFunctionType as AF, AxisListType as AX
 
 W, TX, K, R = 2048, 1024, 256, 7
 SR, SG = (1, 3), (0, 5)
 F32, BF, F16, I32, U16 = "float32", "bfloat16", "float16", "int32", "uint16"
 NEW = -40960
+PAD = 32
 FAR = float(2 ** 26)
 
 
@@ -16,24 +17,27 @@ def _sb(n, d):
 PASSES = ((192, 256), (128, 192), (64, 128), (0, 64))
 NV = (32, 32, 28, 20)
 CMP = ("PS3", "PS5", "PS6", "PS7")
-START = "v0 n0 v1 n1 t0 a2 r0 b2 n2 u0 g0 t1 a3 r1 b3 n3 t2 u1 r2"
+START = "q6 v0 n0 v1 n1 t0 q7 a2 r0 b2 n2 u0 g0 t1 a3 r1"
 LATER = "v0 n0 v1 n1 t0 a2 d0 c0 b2 n2 t1 k0 d1 c1 s0 a3 l0 b3 n3 t2 w7 k1 d2 c2 w6 s1 t3 l1 d3 c3 z0 w5 k2 w4 s2 k3 l2 s3 w3 l3 w2 e0 e1 w1 e2 e3 w0"
-FIRST = "k0 k1 s0 k2 s1 l0 k3 s2 w7 l1 s3 w6 l2 l3 w5 p0 w4 p1 w3 p2 w2 p3 w1 p4 w0"
-FILL = ("x2 x0 m0-3 x3 x1 x4 x5", "m3-4", "m4-5", "m5-8", "m8-9", "m9-11", "m11-16")
-LV1, LS, LV2 = (0, 80), ((80, 144), (144, 192)), (192, 256)
-OWN0, OWN1 = ((0, 48), (48, 96), (96, 144)), ((144, 200), (200, 256))
-FILL1 = ("p5 p6 p7", "q2", "", "", "q3", "m12-16", "m8-12")
+FIRST = "k1 s0 s1 l0 l1 w7 q2 w6 k2 w5 k3 s2 w4 s3 l2 l3 q4 w3 p0 w2 p1 w1 p2 w0"
+FILL = ("x2 m0-4 x3 x4 x5", "m4-5", "m5-6", "m6-9", "m9-10", "m10-16", "")
+FILL6 = FILL[:4] + (FILL[4] + " " + FILL[5], "", "")
+EARLY = 160
+LV1, LS, LV2 = (0, 84), ((84, 144), (144, 192)), (192, 256)
+OWN0, OWNM, OWN1 = ((0, 64), (64, 136)), (136, 160), ((160, 256),)
+FILL1 = ("p3 p4 p5 p6 p7 q5", "q3", "", "m12-14", "m14-16", "m8-12", "")
 
 SCRATCH = {
-    "X": _sb(2560, BF), "IDX": _sb(TX, I32), "IDQ": _sb(1280, F32), "FR": _sb(TX, F32), "L": _sb(2 * 2560, BF),
+    "X": _sb(PAD + 2560, BF), "IDX": _sb(TX, I32), "IDQ": _sb(2560, F32), "FR": _sb(260, F32), "FI": _sb(260, I32), "FJ": _sb(260, I32),
+    "PW": _sb(80, F32), "BW": _sb(128, BF), "L": _sb(2 * 2560, BF),
     "G": _sb(4096, BF), "LG": _sb(4096, BF), "OG": _sb(4096, BF), "OS": _sb(4096, BF), "PR": _sb(4096, BF),
     "QI": _sb(260, I32), "QF": _sb(258, F16), "QW": _sb(16, U16),
-    "PI": _sb(256, F32), "PB": _sb(256, BF), "IA": _sb(256, F32), "IG": _sb(256, F32), "DI": _sb(256, I32), "DJ": _sb(256, I32),
+    "PI": _sb(260, F32), "PB": _sb(256, BF), "IA": _sb(256, F32), "IG": _sb(256, F32), "DI": _sb(256, I32), "DJ": _sb(256, I32),
     "PC": _sb(4, I32), "PF": _sb(10, F32), "IW": _sb(16, F32),
     "ZQ": _sb(144, BF), "BQ": _sb(128, BF), "BB": _sb(256, BF), "B4": _sb(256, BF), "RR": _sb(256, BF), "R4": _sb(256, BF),
     "ZD": _sb(256, BF), "ZC": _sb(256, BF), "II": _sb(256, BF), "NI": _sb(128, BF), "NU": _sb(256, BF), "IB": _sb(256, BF), "IN": _sb(256, BF),
     "DM": _sb(256, BF), "ML": _sb((6, 16), F32), "DU": _sb(2, F32), "T0": _sb(256, F32), "T1": _sb(256, F32),
-    "OM": _sb(1024, BF), "WW": _sb(2064, BF), "W16": _sb(64, BF),
+    "OM": _sb(1024, BF), "WW": _sb(2064, BF), "W16": _sb(64, BF), "H": _sb(8, F32),
     "TRI": _sb((12, 16), BF), "EP": _sb(768, F16), "EM": _sb(192, F16), "EO": _sb(768, F16),
     "SLI": _sb(24, I32), "SL": _sb(24, U16), "SRP": _sb(384, F32), "S0W": _sb(16, F32), "LO": _sb(16, U16),
     "M": _sb(256, F32), "SM": _sb(256, BF), "MN": _sb(256, F16), "SC": _sb(256, F16), "LT": _sb(256, BF), "OFS": _sb(96, U16),
@@ -56,7 +60,7 @@ for _b in range(8):
 for _t in range(1, R, 2):
     for _name, _a, _b in _names(_t):
         SCRATCH["D" + _name] = ("dram", [256, _b - _a], U16)
-SEMAPHORES = (["eV", "eS", "eP", "eG", "ldq", "ldi", "ldx", "ldc", "st", "ls"]
+SEMAPHORES = (["eV", "eS", "eP", "eG", "ldq", "ldi", "ldx", "ldc", "lda", "lde", "ldf", "ldg", "st", "ls"]
               + [m[0] for t in range(1, R) for m in _names(t)] + ["o%d" % t for t in range(1, R)])
 
 
@@ -214,6 +218,9 @@ def rank_program(g, core, T, topo):
         order(q, outs, ins, (sem, total))
         Q[q].dma_start(o, i, **kw).then_inc(T.sem[sem], 16)
 
+    def gcp(o, i, width):
+        run("G", [o], [i], lambda: g.affine_select(o[0], i[0], [[0, width]], OP.is_ge, 0.0, 0, 0))
+
     def gather(q, o, i):
         (cp if q == "V" else act)(o, i)
 
@@ -254,27 +261,30 @@ def rank_program(g, core, T, topo):
     q8 = (0, 8)
     dma("Y", "ldq", 16, T.QI[0:8, 0:256], T.que[:], [A("QI", 0, 256)], [])
     dma("Y", "ldi", 16, T.IDX[:], T.idx[:], [A("IDX")], [])
-    dma("Y", "ldx", 16, T.X[:, 0:W], T.rec[:], [A("X", 0, W)], [])
+    dma("Y", "ldx", 16, T.X[:, PAD:PAD + W], T.rec[:], [A("X", PAD, PAD + W)], [])
 
-    PI = A("PI")
+    PI = A("PI", 0, K)
     pa, pg, pz, pq, pp = [A("PF", j, j + 1) for j in range(5)]
     iota(PI, [[1, 256]], 0, 0)
     iota(pq, [[0, 1]], 15, 16)
     iota(A("PC", 0, 1), [[0, 1]], 0, 1, False)
-    iota(A("IG"), [[0, 2], [1, 8], [0, 16]], 0, 0)
     iota(A("DI"), [[1, 256]], 128, -1, False)
+    iota(A("IG"), [[0, 2], [1, 8], [0, 16]], 0, 0)
+    iota(A("PI", K, K + 4), [[K, 4]], 0, 0)
     iota(A("IA"), [[0, 16], [1, 16]], 0, 0)
     for j, b in enumerate((1, 1, 3, 3, 0, 2)):
         iota(A("SLI", j, 24, 6), [[-4, 4]], 12 + b, 0, False)
     iota(A("DU"), [[32, 2]], W, 2)
-    for c0, c1 in (LV1, LV2):
-        iota(A("PR", 16 * c0, 16 * c1), [[1, c1 - c0], [0, 16]], c0, 0)
     iota(pp, [[0, 1]], 0, 1)
+
+    def places(c0, c1):
+        iota(A("PR", 16 * c0, 16 * c1), [[1, c1 - c0], [0, 16]], c0, 0)
+
+    iota(A("L", 2560 + TX, 2560 + W), [[0, TX]], 256, 0)
     ms(A("WW"), 0.0)
+    ms(A("X", 0, PAD), 0.0)
     for j in range(4):
-        act(A("FR", 256 * j, 256 * j + 256), PI, bias=j / 8.0, scale=1.0 / 2048)
-    act(A("OM"), A("FR"), bias=1.0, scale=0.0)
-    act(A("OM", 1, 1024, 16), A("PI", 0, 64), scale=0.0)
+        act(A("L", 2560 + K * j, 2560 + K * j + K), PI, bias=256.0, scale=0.0, f=AF.Silu)
     ts(A("ZQ", p=q8), A("PI", 0, 144, p=q8), A("PF", 3, 4, p=q8), OP.is_equal)
     ts(A("PC", 1, 2), A("PC", 0, 1), 15, OP.bitwise_and)
     ts(A("PC", 2, 3), A("PC", 0, 1), 4, OP.arith_shift_right)
@@ -283,7 +293,7 @@ def rank_program(g, core, T, topo):
         mm(A("PS2", 0, 16), A("ZQ", 15 - a, 143 - a, p=q8), A("QF", a, 256, 16, p=q8), a == 0, a == 15)
     cp(A("PF", 0, 2), A("PC", 1, 3))
     ts(A("DJ"), A("DI"), 15, OP.bitwise_and)
-    ts(A("BB"), A("IG"), pg, OP.is_equal)
+    ts(A("H", 0, 8), A("PI", 0, 8), pg, OP.is_equal)
     ts(A("W16", 0, 16), A("DJ", 0, 16), 0.0, OP.is_equal, 256.0, OP.mult)
     ts(A("W16", 16, 32), A("DJ", 0, 16), 15.0, OP.is_equal, 16.0, OP.mult)
     ts(A("W16", 32, 48), A("DJ", 0, 16), 14.0, OP.is_equal)
@@ -291,58 +301,62 @@ def rank_program(g, core, T, topo):
     tt(A("W16", 48, 64), A("W16", 0, 16), A("W16", 16, 32), OP.add)
     cp(A("QW"), A("PS2", 0, 16))
     tt(A("W16", 0, 16), A("W16", 48, 64), A("W16", 32, 48), OP.add)
-    ts(A("DM"), A("DJ"), 0.0, OP.is_equal)
+    ts(A("BB"), A("IG"), pg, OP.is_equal)
+    ts(A("AT"), IND(A("IDX"), A("QW")), float(PAD), OP.add)
+    half, own1, pdown = A("PW", 0, 16), A("PW", 16, 32), A("PW", 64, 65)
+    ms(half, 0.5)
+    ts(own1, A("DJ", 0, 16), 0.0, OP.is_equal)
+    ms(A("PW", 32, 48), 0.0)
     for j in range(8):
-        ts(A("WW", 16 * j, 16 * j + 129 * 15 + 1, 129), A("W16", 0, 16), A("BB", 16 * j, 16 * j + 1), OP.mult)
+        ts(A("WW", 16 * j, 16 * j + 129 * 15 + 1, 129), A("W16", 0, 16), A("H", j, j + 1), OP.mult)
+        if j == 1:
+            scan(A("PW", 48, 64), half, A("PW", 32, 48), 2.0, OP.mult, OP.add)
+        elif j == 4:
+            tt(A("PW", 32, 48), A("PW", 48, 64), own1, OP.mult)
+    run("V", [pdown], [A("PW", 32, 48)], lambda: g.vector.tensor_reduce(pdown[0], T.PW[:, 32:48], AX.X, OP.add))
     act(A("RR"), A("BB"), scale=pz)
-    act(A("B4"), A("BB"), scale=4096.0)
-    act(A("IW"), A("PI", 0, 256, 16), bias=pa)
-    act(A("PB"), PI)
-    act(A("T1"), PI, bias=2048.0, scale=2.0)
-    ms(A("ZD"), 0.0)
-    ms(B("TRI"), 0.0)
-    for j in range(2):
-        ts(A("II", 128 * j, 128 * j + 128), A("DI", 128 * j, 128 * j + 128), 128.0 * j + 128, OP.is_equal)
-    cp(A("AT"), IND(A("IDX"), A("QW")))
-    cp(A("ZD", 15, 256, 16), A("RR", 15, 256, 16))
+    act(A("FI"), A("PI"), scale=pdown, bias=-0.4995)
     own = ((1, 4, 2), (4, 6))
-    for blocks in own:
-        ts(B("TRI", blocks), A("IA", 0, 32), pa, OP.is_ge, FAR, OP.mult)
-    cp(A("SL"), A("SLI"))
-    ms(A("S0W"), 0.0)
-    tt(A("IDQ", 0, TX), A("IDX"), A("FR"), OP.add)
-    for j in range(2):
-        act(A("L", 2560 + TX * j, 2560 + TX * j + TX), A("FR"), bias=256.0, scale=0.0)
-    act(A("R4"), A("RR"), scale=4096.0)
-    act(A("NI"), A("II", 0, 128), scale=-1.0)
 
-    def lock_constants():
-        ms(B("ML", (0, 3, 2)), 0.0)
-        for blocks, j in zip(own, (1, 0)):
-            ts(B("ML", blocks), A("DM", 0, 32), A("DU", j, j + 1), OP.mult)
-        ms(A("EM", 0, 192, 2), 1.0)
-        ts(A("EM", 1, 192, 2), B("ML"), 1.0, OP.max)
-        ms(A("EM", 0, 128, 64), 0.0)
-        ms(A("EM", 128, 192, 32), 0.0)
-
-    def small_constants(part):
-        if part == 0:
+    def vector_constants(part):
+        if part == 6:
+            ms(A("ZD"), 0.0)
+            ms(A("S0W"), 0.0)
+            cp(A("SL"), A("SLI"))
+            cp(A("ZD", 15, 256, 16), A("RR", 15, 256, 16))
+        elif part == 7:
+            ts(A("FJ"), A("FI"), 1, OP.bitwise_and)
+        elif part == 0:
+            ms(B("TRI"), 0.0)
+            for j in range(2):
+                ts(A("II", 128 * j, 128 * j + 128), A("DI", 128 * j, 128 * j + 128), 128.0 * j + 128, OP.is_equal)
+            for blocks in own:
+                ts(B("TRI", blocks), A("IA", 0, 32), pa, OP.is_ge, FAR, OP.mult)
+        elif part == 1:
+            ts(A("DM"), A("DJ"), 0.0, OP.is_equal)
+            ms(B("ML", (0, 3, 2)), 0.0)
+            ms(A("EM", 0, 192, 2), 1.0)
+            for blocks, j in zip(own, (1, 0)):
+                ts(B("ML", blocks), A("DM", 0, 32), A("DU", j, j + 1), OP.mult)
+            ms(A("EM", 0, 128, 64), 0.0)
+            ms(A("EM", 128, 192, 32), 0.0)
+            ts(A("EM", 1, 192, 2), B("ML"), 1.0, OP.max)
+        elif part == 2:
+            ts(A("LT"), A("IA"), pa, OP.is_le, -1.0, OP.mult)
+        elif part == 3:
             ms(A("FL"), 0.0)
             ms(A("ZE"), 0.0)
-            ms(A("THK"), W - 0.5)
-        elif part == 1:
-            ms(A("M3"), 1.0)
-            ms(A("C3", 0, 48, 3), 0.0)
-            ms(A("C3", 1, 48, 3), -1024.0)
-            ts(A("C3", 2, 48, 3), A("IW"), 256.0, OP.add)
-            ms(A("M3", 0, 48, 3), 0.0)
-        elif part == 2:
+        elif part == 4:
+            ts(A("B4"), A("BB"), 4096.0, OP.mult)
+        else:
             ts(A("BQ", p=q8), A("IG", 0, 128, p=q8), A("PF", 4, 5, p=q8), OP.is_equal)
             cp(A("QF", 256, 257, p=q8), A("QI", 256, 257, p=q8))
             mm(A("PS2", 16, 17), A("BQ", p=q8), A("QF", 256, 257, p=q8), True, True)
-        else:
-            ms(A("ZC"), 0.0)
-            ts(A("ZC", 15, 256, 16), A("BB", 15, 256, 16), 2048.0, OP.mult)
+
+    def product(j):
+        a = 64 * (j % 4)
+        o, x, y = ("NU", "LT", "BB") if j < 4 else ("M", "T1", "DM")
+        tt(A(o, a, a + 64), A(x, a, a + 64), A(y, a, a + 64), OP.mult)
 
     def obank(c0, c1):
         return A("PS7" if c0 >= LV2[0] else "PS6", c0, c1)
@@ -385,12 +399,12 @@ def rank_program(g, core, T, topo):
         cp(IND(table(t, 2560), A("LO", 2 * e, 2 * e + 2)), A("PB", 32 * e, 32 * e + 32))
 
     def own_gather(q, t, c0, c1):
-        gather(q, A("OG", 16 * c0, 16 * c1), IND(A("X", 0, W), A("NM", 256 * (t - 1) + c0, 256 * (t - 1) + c1)))
+        gather(q, A("OG", 16 * c0, 16 * c1), IND(A("X", PAD, PAD + W), A("NM", 256 * (t - 1) + c0, 256 * (t - 1) + c1)))
 
     def own_max(c0, c1):
         for a in range(c0, c1, 64):
             b = min(a + 64, c1)
-            scan(A("OS", 16 * a, 16 * b), A("OM", 0, 16 * (b - a)), A("OG", 16 * a, 16 * b), 0.0, OP.mult, OP.max)
+            scan(A("OS", 16 * a, 16 * b), A("OM", 0, 16 * (b - a)), A("OG", 16 * a, 16 * b), 0.0, OP.min, OP.max)
 
     def sums(c0, c1, ps="PS1"):
         mm(A(ps, c0, c1), A("II", 0, 128), A("OG", 16 * c0, 16 * c1, 16), True, False)
@@ -415,7 +429,7 @@ def rank_program(g, core, T, topo):
             a, b = (c0, v) if q == "V" else (v, c1)
             if half is not None:
                 a, b = (a, (a + b) // 4 * 2) if half == 0 else ((a + b) // 4 * 2, b)
-            gather(q, A("G", 16 * a, 16 * b), IND(A("X", 0, W), A("AT", a, b)))
+            gather(q, A("G", 16 * a, 16 * b), IND(A("X", 0, PAD + W), A("AT", a, b)))
 
         def weigh(p):
             c0, c1 = PASSES[p]
@@ -438,11 +452,7 @@ def rank_program(g, core, T, topo):
                 mm(A("PS2", 0, 16), A("ZC", 15 - a + rot, 143 - a + rot), B("NE", None, a), False, a == 15)
 
         def small(j):
-            if j == 0:
-                ts(A("NX", 2, 3), A("NX", 1, 2), 768.0, OP.is_ge, 1024.0, OP.mult)
-            elif j == 1:
-                ts(A("NX", 0, 1), A("NX", 1, 2), A("NX", 2, 3), OP.subtract, 256.0, OP.add)
-            elif j == 2:
+            if j == 2:
                 ts(A("FL", 16, 32), A("PS2", 0, 16), 2048.0, OP.is_ge)
             elif j == 3:
                 ts(A("THK"), A("FL", 16, 32), 8192.0, OP.mult, W - 0.5, OP.add)
@@ -459,7 +469,7 @@ def rank_program(g, core, T, topo):
                 step[s[0]](*[int(j) for j in s[1:].split("-")])
 
         def fill(j):
-            steps((FILL if t > 1 else FILL1)[j])
+            steps((FILL1 if t == 1 else FILL if t < R - 1 else FILL6)[j])
 
         if t > 1:
             for a in range(16):
@@ -474,34 +484,45 @@ def rank_program(g, core, T, topo):
             step["r"] = lambda p: tt(P16("S16", *PASSES[p]), nbank(p), A("RM", *PASSES[p]), OP.subtract)
             step["u"] = lambda p: cp(A("SU", *PASSES[p]), P16("S16", *PASSES[p]))
             step["g"] = lambda j: send_names(1, j)
-            step["q"] = small_constants
+            step["q"] = vector_constants
+            step["p"] = product
             for p in range(4):
                 digits("S", p)
             steps(START)
-            pick_first("PS4", 4, 16)
-            open_compare(t, range(3))
-            lock_constants()
-            steps("t3 u2 r3")
-            pick_first("PS2", 0, 4)
-            open_compare(t, (3,))
-            spread_first("PS4", 4, 16, 0, 3)
-            ts(A("LT"), A("IA"), pa, OP.is_le, -1.0, OP.mult)
-            steps("u3 g1 q0 q1")
-            spread_first("PS2", 0, 4, 3, 4)
-            act(A("IB"), A("II"), scale=1024.0)
-            act(A("IN"), A("II"), scale=-1024.0)
-            act(A("IDQ", TX, 1280), A("IDQ", 0, 256))
-            act(A("AW", 0, 256), IND(A("IDQ", 0, TX), A("QW")))
-            iota(table(2, W), [[0, W]], 256, 0)
-            iota(A("SW", 0, 256), [[0, 256]], NEW, 0)
             dma("G", "ldc", 16, T.QI[0:8, 256:257], T.cur[:], [A("QI", 256, 257)], [], allow_slow_non_contiguous=True)
-
-            def product(j):
-                a = 64 * (j % 4)
-                o, x, y = ("NU", "LT", "BB") if j < 4 else ("M", "T1", "DM")
-                tt(A(o, a, a + 64), A(x, a, a + 64), A(y, a, a + 64), OP.mult)
-
-            step["p"] = product
+            places(*LV1)
+            act(A("PB"), PI)
+            act(A("FR", 0, K), A("FJ", 0, K), scale=0.25)
+            act(A("FR", K, K + 4), A("FJ", K, K + 4), scale=0.25, bias=PAD + 0.125)
+            pick_first("PS4", 8, 16)
+            spread_first("PS4", 8, 16, 0, 2)
+            for j in range(4):
+                act(A("IDQ", K * j, K * j + K), A("IDX", K * j, K * j + K), bias=A("FR", K + j, K + j + 1))
+            steps("b3 n3 t2 q0 r2 u1")
+            open_compare(t, (0, 1))
+            steps("q1 t3 u2 r3")
+            pick_first("PS2", 0, 8)
+            open_compare(t, (2, 3))
+            spread_first("PS2", 0, 8, 2, 4)
+            steps("k0 u3 g1")
+            for j in range(4):
+                dma("G", "lda", 64, T.IDQ[:, K * j:K * j + K], T.FR[:, 0:K], [A("IDQ", K * j, K * j + K)], [A("FR", 0, K)], accum_op=OP.add)
+            act(A("T1"), PI, bias=2048.0, scale=2.0)
+            for sem, a, b in (("lde", TX, TX + K), ("ldf", TX + K, 2 * TX), ("ldg", 2 * TX, 2560)):
+                dma("Y", sem, 16, T.IDQ[:, a:b], T.IDQ[:, a % TX:a % TX + b - a], [A("IDQ", a, b)], [A("IDQ", a % TX, a % TX + b - a)])
+            places(*LV2)
+            act(A("R4"), A("RR"), scale=4096.0)
+            act(A("NI"), A("II", 0, 128), scale=-1.0)
+            act(A("IW"), A("PI", 0, 256, 16), bias=pa)
+            act(A("SM"), A("IA"), f=AF.Sign)
+            act(A("IN"), A("II"), scale=-1024.0)
+            for o, v in ((A("THK"), W - 0.5), (A("M3", 0, 48, 3), 0.0), (A("M3", 1, 48, 3), 1.0), (A("M3", 2, 48, 3), 1.0),
+                         (A("C3", 0, 48, 3), 0.0), (A("C3", 1, 48, 3), -1024.0)):
+                act(o, A("IW"), bias=v, scale=0.0)
+            act(A("C3", 2, 48, 3), A("IW"), bias=256.0)
+            gcp(A("DA"), B("S16"), K)
+            iota(A("SW", 0, 256), [[0, 256]], NEW, 0)
+            iota(A("OM"), [[0, 64], [16, 16]], -16, 0)
             steps(FIRST)
         for c0, c1 in ((0, LV2[0]), LV2):
             mm(obank(c0, c1), A("RR", rot, rot + 128), P16("S16", c0, c1), True, False)
@@ -528,6 +549,10 @@ def rank_program(g, core, T, topo):
         pick(*LS[0])
         count(*LV1, False)
         pick(*LS[1])
+        if t > 1:
+            own_gather("S", t, *OWNM)
+        else:
+            act(A("AW", 0, 256), IND(A("IDQ", 0, TX), A("QW")))
         act(A("LT", s0, s1), A("PS4", s0, s1), scale=-1.0, f=AF.Relu)
         count(*LV2, True)
         mm(obank(s0, s1), A("B4", rot, rot + 128), A("LT", s0, s1), False, True)
@@ -537,7 +562,6 @@ def rank_program(g, core, T, topo):
         else:
             for c0, c1 in PASSES[:2]:
                 own_gather("S", t, c0, c1)
-            ts(A("SM"), A("IA"), 0.0, OP.not_equal)
         fill(0)
         clamp(*LV2)
         clamp(0, LV2[0])
@@ -569,61 +593,75 @@ def rank_program(g, core, T, topo):
         mm(cand(1), un("BB"), A("CF", 16, 32), False, True, False)
         mm(A("PS0", 64, 65), un("BB"), A("CF", 31, 32), True, True)
         fill(3)
-        if t == 1:
-            cp(A("DA"), B("S16"))
         scan(A("PP"), A("M3"), A("PS0", 0, 48), 0.0, OP.mult, OP.max)
-        ts(A("TL"), A("IW"), A("NX", 0, 1), OP.add, A("PS0", 64, 65), OP.subtract)
-        tt(A("NX", 1, 2), A("NX", 0, 1), A("PS0", 64, 65), OP.subtract)
+        ts(A("TL"), A("IW"), A("NX", c, t), OP.add, A("PS0", 64, 65), OP.subtract)
+        ts(A("NX", t, t + 1), A("NX", c, t), A("PS0", 64, 65), OP.subtract, 256.0, OP.add)
         cp(A("DW"), A("PP", 2, 48, 3))
         w0, w1 = 512 * (c % 2), 512 * (t % 2)
-        act(A("AW", w1, w1 + 256), IND(A("IDQ"), A("TL")))
+        act(A("AW", w1, w1 + 256), IND(A("IDQ", 0, TX + K * t), A("TL")))
         if t == 1:
             for c0, c1 in PASSES[2:]:
                 own_gather("S", t, c0, c1)
         fill(4)
+        early, late = ((64, K), (0, 64)) if t == 1 else ((0, EARLY), (EARLY, K))
+        if t > 1:
+            sums(*early)
+            act(A("TT", *early), A("PS1", *early))
         cp(IND(A("SW", 512 * c, 512 * c + 512), A("DW")), A("DA"))
         kept = A("SW", 512 * c, 512 * c + 256)
         fill(5)
         if t < R - 1:
-            cp(A("SU", SU + 256, SU + 512), kept)
+            if t == 1:
+                cp(A("SU", SU + 256, SU + 512), kept)
+            else:
+                gcp(A("SU", SU + 256, SU + 512), kept, K)
             send_names(t + 1)
-            if t + 2 < R:
-                iota(table(t + 2, W), [[0, W]], 256, 0)
-            iota(A("SW", 512 * t, 512 * t + 256), [[0, 256]], -1 if t == R - 2 else NEW, 0)
-            cp(B("S16"), kept)
+            gather("V" if t == 1 else "S", B("S16"), kept)
         else:
             dma("Y", "st", 64, T.yd[:], kept[0], [], [kept])
-        if t < R - 1:
-            pick_first()
         fill(6)
         if t > 1:
-            sums(0, K)
-            act(A("TT"), A("PS1", 0, K))
-        cp(IND(A("AW", w1, w1 + 512), A("DW")), A("AW", w0, w0 + 256))
-        if t == 1:
-            own_max(*PASSES[2])
-            sums(64, K)
-            act(A("TT", 64, K), A("PS1", 64, K))
-            cp(A("AT"), A("AW", w1, w1 + 256))
-            own_max(*PASSES[3])
-            sums(0, 64, "PS0")
-            ts(A("TR", 64, K), A("TT", 64, K), 16.0, OP.is_ge, -16.0, OP.mult)
-            ts(A("TR", 0, 64), A("PS0", 0, 64), 16.0, OP.is_ge, -16.0, OP.mult)
-            cp(A("TT", 0, 64), A("PS0", 0, 64))
-        else:
-            ts(A("TR"), A("TT"), 16.0, OP.is_ge, -16.0, OP.mult)
-            if t < R - 1:
-                cp(A("AT"), A("AW", w1, w1 + 256))
+            sums(*late, "PS0")
         if t < R - 1:
+            pick_first()
+        if t > 1:
+            o, i = IND(A("AW", w1, w1 + 512), A("DW")), A("AW", w0, w0 + 256)
+            run("S", [o], [i], lambda: g.scalar.activation(o[0], i[0], AF.Silu))
+        else:
+            cp(IND(A("AW", w1, w1 + 512), A("DW")), A("AW", w0, w0 + 256))
+            run("V", [A("PW", 65, 66)], [pdown], lambda: g.vector.reciprocal(T.PW[:, 65:66], pdown[0]))
+            ts(A("IB"), A("II"), 1024.0, OP.mult)
+            ts(A("BW"), A("BB", 0, 128), A("PW", 65, 66), OP.mult)
+            ms(A("ZC"), 0.0)
+            own_max(*PASSES[2])
+            ts(A("ZC", 15, 256, 16), A("BB", 15, 256, 16), 2048.0, OP.mult)
+            sums(*early)
+            act(A("TT", *early), A("PS1", *early))
+        if t < R - 1:
+            gcp(A("AT"), A("AW", w1, w1 + 256), K)
             spread_first()
-        tt(IND(A("X"), A("OFF", 16 * c, 16 * c + 16)), A("TT"), A("TR"), OP.add)
+        if t == 1:
+            own_max(*PASSES[3])
+            sums(*late, "PS0")
+        ts(A("TR", *early), A("TT", *early), 16.0, OP.is_ge, -16.0, OP.mult)
+        ts(A("TR", *late), A("PS0", *late), 16.0, OP.is_ge, -16.0, OP.mult)
+        cp(A("TT", *late), A("PS0", *late))
+        if t == 1:
+            iota(table(2, W), [[0, W]], 256, 0)
+        if t + 2 < R:
+            iota(table(t + 2, W), [[0, W]], 256, 0)
+        if t < R - 1:
+            iota(A("SW", 512 * t, 512 * t + 256), [[0, 256]], -1 if t == R - 2 else NEW, 0)
+        if t == R - 1:
+            act(A("DI"), A("AW", w1, w1 + 256), scale=4.0, bias=-0.25)
+        tt(IND(A("X", PAD, PAD + 2560), A("OFF", 16 * c, 16 * c + 16)), A("TT"), A("TR"), OP.add)
 
-    dma("Y", "st", 64, T.yx[0:64, :], T.X[0:64, 0:W], [], [A("X")])
-    dma("S", "st", 64, T.yx[64:128, :], T.X[64:128, 0:W], [], [A("X")])
-    w1 = 512 * ((R - 1) % 2)
-    cp(A("DN"), A("AW", w1, w1 + 256))
-    tt(A("T0"), A("AW", w1, w1 + 256), A("DN"), OP.subtract)
-    act(A("T1"), A("T0"), scale=2048.0)
+    ts(A("DJ"), A("DI"), 1, OP.bitwise_and)
+    dma("Y", "st", 64, T.yx[0:64, :], T.X[0:64, PAD:PAD + W], [], [A("X")])
+    dma("S", "st", 64, T.yx[64:128, :], T.X[64:128, PAD:PAD + W], [], [A("X")])
+    act(A("RM"), A("DJ"))
+    mm(A("PS1", 0, K), A("BW"), A("RM"), True, True)
+    act(A("T1"), A("PS1", 0, K))
     dma("Y", "st", 64, T.yq[:], T.T1[0:128:16, :], [], [A("T1")])
     for q in ("V", "S", "P", "G"):
         wait("G", "e" + q, cnt[q])

@@ -6,8 +6,9 @@ W, TX, K, R = 2048, 1024, 256, 7
 SR, SG = (1, 3), (0, 5)
 F32, BF, F16, I32, U16 = "float32", "bfloat16", "float16", "int32", "uint16"
 NEW = -40960
-PAD = 32
 FAR = float(2 ** 26)
+OLD = TX + K
+PAD = 32
 
 
 def _sb(n, d):
@@ -15,37 +16,32 @@ def _sb(n, d):
 
 
 PASSES = ((192, 256), (128, 192), (64, 128), (0, 64))
-NV = (32, 32, 28, 20)
 CMP = ("PS3", "PS5", "PS6", "PS7")
-START = "q6 v0 n0 v1 n1 t0 q7 a2 r0 b2 n2 u0 g0 t1 a3 r1"
-LATER = "v0 n0 v1 n1 t0 a2 d0 c0 b2 n2 t1 k0 d1 c1 s0 a3 l0 b3 n3 t2 w7 k1 d2 c2 w6 s1 t3 l1 d3 c3 z0 w5 k2 w4 s2 k3 l2 s3 w3 l3 w2 e0 e1 w1 e2 e3 w0"
-FIRST = "k1 s0 s1 l0 l1 w7 q2 w6 k2 w5 k3 s2 w4 s3 l2 l3 q4 w3 p0 w2 p1 w1 p2 w0"
-FILL = ("x2 m0-4 x3 x4 x5", "m4-5", "m5-6", "m6-9", "m9-10", "m10-16", "")
-FILL6 = FILL[:4] + (FILL[4] + " " + FILL[5], "", "")
-EARLY = 160
-LV1, LS, LV2 = (0, 84), ((84, 144), (144, 192)), (192, 256)
-OWN0, OWNM, OWN1 = ((0, 64), (64, 136)), (136, 160), ((160, 256),)
-FILL1 = ("p3 p4 p5 p6 p7 q5", "q3", "", "m12-14", "m14-16", "m8-12", "")
+PARTS = ((0, 80), (80, 192), (192, 256))
+LV1, LV2 = PARTS[0], PARTS[2]
+FIRST = "wz pb pq pc pa zq qf tz zz ig pf qm eo ha hh ia le pz nz dm nm xz wa qw nd wb at prb lf N224-256 hb bb wc du v192-224 N160-192 ww n0 v128-160 n1 v64-96 N96-128 t0 tri N24-64 r0 t1 zd u0 r1 pp v0-24 n2 p4-8 ii hc rr hd ni pra em q4-8 u1 pn n3 fi t2 Q4-8 pl pj t3 K4-8 r2 ez r3 ua Q0-4 fk fj bf k4-8 u2 p0-4 o1 fs o0 u3 s5 s6 s7 l0 fr g0 q0-4 s4 K0-4 k0-4 o2 w7 o3 ph nf aqb g1 l1 w6 s3 s2 w5 bq l2 w4 da s1 s0 om w3 nu l3 w2 A1 zy mo A0 w1 mz aqa G224-256 w0 G192-224 A2 sm iw fl L0-80 rf L192-256 cc S80-140 P80-140 H0-16 C0-80-1 B0-80 S140-192 add P140-192 C192-256-1 po G128-192 cur T80-192-1 cf G64-128 he in m14-16 B192-256 G16-64 B80-192 m12-14 R0 O nx I R1 m8-12 wi R2 R5 m4-8 R3 bw run R6 h64-256-1 J0 R7 R4 m0-4 V3 h0-64-0 J5 J7 ib i64-256-1 f64-256 f0-64-0 j0-64-0 J1 J6 J2 zc J9 J8 J4 X pu"
+LATER = "v192-224 k4-8 N224-256 v128-160 N160-192 n0 t0 o0 n1 v64-80 o1 d0 c0 N96-128 v80-96 t1 v12-24 d1 k0-4 s6 s7 N24-64 v0-12 n2 l0 t2 c1 s5 s4 w7 o2 d2 l1 w6 e2 n3 t3 w5 d3 c2 y0 s2 s3 w4 o3 l2 c3 e1 e0 w3 G0-48 s1 G48-96 A0 z0 s0 G96-128 w2 A1 l3 m2-3 w1 e3 m0-1 w0 x5 A2 x4 S80-140 P80-140 S140-192 L0-80 C0-80-1 L192-256 P140-192 C192-256-1 x2 m7-8 G128-160 m4-5 T80-192-1 m3-4 G160-208 m1-2 B0-80 m6-7 m9-10 B192-256 B80-192 m8-9 R0 O m5-6 R1 H240-256 m11-12 R2 R5 m10-11 R3 G208-240 m12-13 R6 J0 R4 J5 m14-15 h0-208-1 m13-14 m15-16 h208-256-0 i0-208-1 J1 V3 J7 J8 f0-208 J6 j208-256-0 f208-256-0 J2 J4 R7 J9 X"
+TAIL = "v192-224 k4-8 v128-160 v64-80 N224-256 n0 t0 k0-4 N160-192 o0 d0 n1 v80-96 o1 t1 v12-24 c0 d1 s6 s7 v0-12 N96-128 n2 l0 t2 c1 e2 o2 w7 d2 s4 s5 w6 N24-64 n3 c2 l1 t3 w5 o3 y0 s3 d3 s2 w4 l2 c3 w3 s1 s0 G0-48 z0 e0 G48-96 w2 A0 l3 m2-3 w1 A2 x2 e1 w0 A1 G96-128 S80-140 e3 P80-140 S140-192 m1-2 L0-80 C0-80-1 L192-256 G128-160 m7-8 m0-1 P140-192 C192-256-1 m4-5 T80-192-1 x5 m9-10 x4 B0-80 m6-7 B192-256 B80-192 m3-4 R0 O R1 H240-256 G208-240 R5 R6 R2 m13-14 R3 m14-15 m5-6 G160-208 m10-11 m8-9 m15-16 h208-256-0 J0 m12-13 m11-12 R4 h0-208-1 J5 J1 j208-256-0 J6 J7 i0-208-1 f208-256-0 J8 f0-208 X J9"
 
 SCRATCH = {
-    "X": _sb(PAD + 2560, BF), "IDX": _sb(TX, I32), "IDQ": _sb(2560, F32), "FR": _sb(260, F32), "FI": _sb(260, I32), "FJ": _sb(260, I32),
-    "PW": _sb(80, F32), "BW": _sb(128, BF), "L": _sb(2 * 2560, BF),
+    "X": _sb(PAD + 2560, BF), "IDX": _sb(TX, I32), "AQ": _sb(OLD, F32), "AW": _sb(2 * 512, F32), "L": _sb(2 * 2560, BF),
+    "FR": _sb(260, F32), "FI": _sb(260, I32), "FJ": _sb(260, I32), "PW": _sb(72, F32), "BW": _sb(128, BF),
     "G": _sb(4096, BF), "LG": _sb(4096, BF), "OG": _sb(4096, BF), "OS": _sb(4096, BF), "PR": _sb(4096, BF),
     "QI": _sb(260, I32), "QF": _sb(258, F16), "QW": _sb(16, U16),
-    "PI": _sb(260, F32), "PB": _sb(256, BF), "IA": _sb(256, F32), "IG": _sb(256, F32), "DI": _sb(256, I32), "DJ": _sb(256, I32),
+    "PB": _sb(256, BF), "IA": _sb(256, BF), "IG": _sb(128, BF), "DI": _sb(256, I32), "DJ": _sb(256, I32),
     "PC": _sb(4, I32), "PF": _sb(10, F32), "IW": _sb(16, F32),
     "ZQ": _sb(144, BF), "BQ": _sb(128, BF), "BB": _sb(256, BF), "B4": _sb(256, BF), "RR": _sb(256, BF), "R4": _sb(256, BF),
     "ZD": _sb(256, BF), "ZC": _sb(256, BF), "II": _sb(256, BF), "NI": _sb(128, BF), "NU": _sb(256, BF), "IB": _sb(256, BF), "IN": _sb(256, BF),
-    "DM": _sb(256, BF), "ML": _sb((6, 16), F32), "DU": _sb(2, F32), "T0": _sb(256, F32), "T1": _sb(256, F32),
-    "OM": _sb(1024, BF), "WW": _sb(2064, BF), "W16": _sb(64, BF), "H": _sb(8, F32),
-    "TRI": _sb((12, 16), BF), "EP": _sb(768, F16), "EM": _sb(192, F16), "EO": _sb(768, F16),
-    "SLI": _sb(24, I32), "SL": _sb(24, U16), "SRP": _sb(384, F32), "S0W": _sb(16, F32), "LO": _sb(16, U16),
-    "M": _sb(256, F32), "SM": _sb(256, BF), "MN": _sb(256, F16), "SC": _sb(256, F16), "LT": _sb(256, BF), "OFS": _sb(96, U16),
-    "AT": _sb(256, U16), "RM": _sb(256, BF), "NE": _sb((16, 16), BF), "DN": _sb(256, I32), "DA": _sb(256, I32),
-    "S16": _sb((16, 16), F16), "SU": _sb(6 * 256, U16),
-    "FL": _sb(32, BF), "CF": _sb(32, BF), "ZE": _sb(32, BF), "THK": _sb(16, F32), "C3": _sb(48, F16), "M3": _sb(48, F32),
-    "PP": _sb(48, F32), "DW": _sb(16, U16), "TL": _sb(16, U16), "NX": _sb(8, F32),
-    "SW": _sb(6 * 512, F32), "AW": _sb(2 * 512, F32), "TT": _sb(256, BF), "TR": _sb(256, BF),
+    "DM": _sb(32, BF), "DU": _sb(4, F32), "T1": _sb(256, F32), "YD": _sb(256, F32), "NG": _sb(256, BF), "ND": _sb((10, 16), BF), "N4": _sb(128, BF),
+    "OM": _sb(1024, BF), "WW": _sb(2064, BF), "W16": _sb(64, BF), "H": _sb(8, F32), "SP": _sb(16, F32), "OD": _sb(16, BF),
+    "TRI": _sb((6, 16), BF), "EQ": _sb(384, BF), "EM": _sb(80, F32), "PL": _sb(256, BF), "EO": _sb((8, 80), F32),
+    "S0X": _sb((8, 3), F16), "LO": _sb(16, U16),
+    "SM": _sb(256, BF), "SC": _sb(256, F32), "LT": _sb(256, BF), "OFS": _sb(96, U16),
+    "AT": _sb(256, U16), "RM": _sb(256, BF), "NE": _sb(256, BF), "DN": _sb(256, I32), "DA": _sb(K, I32),
+    "S16": _sb(256, F16), "SU": _sb(6 * 256, U16),
+    "FL": _sb(48, BF), "CF": _sb(32, BF), "PU": _sb(256, BF), "C3": _sb(48, F16), "M3": _sb(48, F32),
+    "PP": _sb(48, F32), "DW": _sb(16, U16), "TL": _sb(16, U16), "NX": _sb(16, F32),
+    "SW": _sb(6 * 512, F32), "TT": _sb(256, BF), "TR": _sb(256, BF),
     "NM": _sb(6 * 256, U16), "OFF": _sb(96, U16),
 }
 
@@ -60,7 +56,7 @@ for _b in range(8):
 for _t in range(1, R, 2):
     for _name, _a, _b in _names(_t):
         SCRATCH["D" + _name] = ("dram", [256, _b - _a], U16)
-SEMAPHORES = (["eV", "eS", "eP", "eG", "ldq", "ldi", "ldx", "ldc", "lda", "lde", "ldf", "ldg", "st", "ls"]
+SEMAPHORES = (["eV", "eS", "eP", "eG", "ldq", "ldi", "ldx", "ldc", "lda", "lde", "st", "ls"]
               + [m[0] for t in range(1, R) for m in _names(t)] + ["o%d" % t for t in range(1, R)])
 
 
@@ -131,8 +127,7 @@ def rank_program(g, core, T, topo):
         at = np.arange(int(np.prod(dims))).reshape(dims)[ix]
         return (T[name][(slice(None),) + ix], name, _bits(at.ravel().tolist()))
 
-    def P16(name, c0, c1):
-        return B(name, (c0 // 16, c1 // 16))
+    P16 = A
 
     def IND(w, o):
         return (w[0].indirect(o[0]), w[1], w[2], o)
@@ -224,6 +219,12 @@ def rank_program(g, core, T, topo):
     def gather(q, o, i):
         (cp if q == "V" else act)(o, i)
 
+    def copy(q, o, i):
+        if q == "G":
+            gcp(o, i, K)
+        else:
+            gather(q, o, i)
+
     rl = _relay(T, topo, rank)
     rrid, rpid = topo.addr(rl, core)
     reng = topo.engines(core, rl)
@@ -258,145 +259,170 @@ def rank_program(g, core, T, topo):
     def table(t, width):
         return A("L", 2560 * (t % 2), 2560 * (t % 2) + width)
 
+    def no_place(t):
+        iota(A("SW", 512 * (t - 1), 512 * (t - 1) + K), [[0, K]], -1 if t == R - 1 else NEW, 0)
+
     q8 = (0, 8)
     dma("Y", "ldq", 16, T.QI[0:8, 0:256], T.que[:], [A("QI", 0, 256)], [])
     dma("Y", "ldi", 16, T.IDX[:], T.idx[:], [A("IDX")], [])
     dma("Y", "ldx", 16, T.X[:, PAD:PAD + W], T.rec[:], [A("X", PAD, PAD + W)], [])
 
-    PI = A("PI", 0, K)
-    pa, pg, pz, pq, pp = [A("PF", j, j + 1) for j in range(5)]
-    iota(PI, [[1, 256]], 0, 0)
-    iota(pq, [[0, 1]], 15, 16)
-    iota(A("PC", 0, 1), [[0, 1]], 0, 1, False)
-    iota(A("DI"), [[1, 256]], 128, -1, False)
-    iota(A("IG"), [[0, 2], [1, 8], [0, 16]], 0, 0)
-    iota(A("PI", K, K + 4), [[K, 4]], 0, 0)
-    iota(A("IA"), [[0, 16], [1, 16]], 0, 0)
-    for j, b in enumerate((1, 1, 3, 3, 0, 2)):
-        iota(A("SLI", j, 24, 6), [[-4, 4]], 12 + b, 0, False)
-    iota(A("DU"), [[32, 2]], W, 2)
-    iota(pp, [[0, 1]], 0, 1)
+    PB, down, up = A("PB"), A("PW", 64, 65), A("PW", 65, 66)
+    pa, pg, pz, pq, pp, ph, pn = [A("PF", j, j + 1) for j in range(7)]
 
     def places(c0, c1):
         iota(A("PR", 16 * c0, 16 * c1), [[1, c1 - c0], [0, 16]], c0, 0)
 
-    iota(A("L", 2560 + TX, 2560 + W), [[0, TX]], 256, 0)
-    ms(A("WW"), 0.0)
-    ms(A("X", 0, PAD), 0.0)
-    for j in range(4):
-        act(A("L", 2560 + K * j, 2560 + K * j + K), PI, bias=256.0, scale=0.0, f=AF.Silu)
-    ts(A("ZQ", p=q8), A("PI", 0, 144, p=q8), A("PF", 3, 4, p=q8), OP.is_equal)
-    ts(A("PC", 1, 2), A("PC", 0, 1), 15, OP.bitwise_and)
-    ts(A("PC", 2, 3), A("PC", 0, 1), 4, OP.arith_shift_right)
-    cp(A("QF", 0, 256, p=q8), A("QI", 0, 256, p=q8))
-    for a in range(16):
-        mm(A("PS2", 0, 16), A("ZQ", 15 - a, 143 - a, p=q8), A("QF", a, 256, 16, p=q8), a == 0, a == 15)
-    cp(A("PF", 0, 2), A("PC", 1, 3))
-    ts(A("DJ"), A("DI"), 15, OP.bitwise_and)
-    ts(A("H", 0, 8), A("PI", 0, 8), pg, OP.is_equal)
-    ts(A("W16", 0, 16), A("DJ", 0, 16), 0.0, OP.is_equal, 256.0, OP.mult)
-    ts(A("W16", 16, 32), A("DJ", 0, 16), 15.0, OP.is_equal, 16.0, OP.mult)
-    ts(A("W16", 32, 48), A("DJ", 0, 16), 14.0, OP.is_equal)
-    ts(pz, pa, 0.0, OP.is_equal)
-    tt(A("W16", 48, 64), A("W16", 0, 16), A("W16", 16, 32), OP.add)
-    cp(A("QW"), A("PS2", 0, 16))
-    tt(A("W16", 0, 16), A("W16", 48, 64), A("W16", 32, 48), OP.add)
-    ts(A("BB"), A("IG"), pg, OP.is_equal)
-    ts(A("AT"), IND(A("IDX"), A("QW")), float(PAD), OP.add)
-    half, own1, pdown = A("PW", 0, 16), A("PW", 16, 32), A("PW", 64, 65)
-    ms(half, 0.5)
-    ts(own1, A("DJ", 0, 16), 0.0, OP.is_equal)
-    ms(A("PW", 32, 48), 0.0)
-    for j in range(8):
-        ts(A("WW", 16 * j, 16 * j + 129 * 15 + 1, 129), A("W16", 0, 16), A("H", j, j + 1), OP.mult)
-        if j == 1:
-            scan(A("PW", 48, 64), half, A("PW", 32, 48), 2.0, OP.mult, OP.add)
-        elif j == 4:
-            tt(A("PW", 32, 48), A("PW", 48, 64), own1, OP.mult)
-    run("V", [pdown], [A("PW", 32, 48)], lambda: g.vector.tensor_reduce(pdown[0], T.PW[:, 32:48], AX.X, OP.add))
-    act(A("RR"), A("BB"), scale=pz)
-    act(A("FI"), A("PI"), scale=pdown, bias=-0.4995)
-    own = ((1, 4, 2), (4, 6))
+    def halves(name, src, s1, op0, s2=None, op1=None):
+        for j in range(2):
+            ts(A(name, 128 * j, 128 * j + 128), src, s1, op0, s2, op1)
 
-    def vector_constants(part):
-        if part == 6:
-            ms(A("ZD"), 0.0)
-            ms(A("S0W"), 0.0)
-            cp(A("SL"), A("SLI"))
-            cp(A("ZD", 15, 256, 16), A("RR", 15, 256, 16))
-        elif part == 7:
-            ts(A("FJ"), A("FI"), 1, OP.bitwise_and)
-        elif part == 0:
-            ms(B("TRI"), 0.0)
-            for j in range(2):
-                ts(A("II", 128 * j, 128 * j + 128), A("DI", 128 * j, 128 * j + 128), 128.0 * j + 128, OP.is_equal)
-            for blocks in own:
-                ts(B("TRI", blocks), A("IA", 0, 32), pa, OP.is_ge, FAR, OP.mult)
-        elif part == 1:
-            ts(A("DM"), A("DJ"), 0.0, OP.is_equal)
-            ms(B("ML", (0, 3, 2)), 0.0)
-            ms(A("EM", 0, 192, 2), 1.0)
-            for blocks, j in zip(own, (1, 0)):
-                ts(B("ML", blocks), A("DM", 0, 32), A("DU", j, j + 1), OP.mult)
-            ms(A("EM", 0, 128, 64), 0.0)
-            ms(A("EM", 128, 192, 32), 0.0)
-            ts(A("EM", 1, 192, 2), B("ML"), 1.0, OP.max)
-        elif part == 2:
-            ts(A("LT"), A("IA"), pa, OP.is_le, -1.0, OP.mult)
-        elif part == 3:
-            ms(A("FL"), 0.0)
-            ms(A("ZE"), 0.0)
-        elif part == 4:
-            ts(A("B4"), A("BB"), 4096.0, OP.mult)
-        else:
-            ts(A("BQ", p=q8), A("IG", 0, 128, p=q8), A("PF", 4, 5, p=q8), OP.is_equal)
-            cp(A("QF", 256, 257, p=q8), A("QI", 256, 257, p=q8))
-            mm(A("PS2", 16, 17), A("BQ", p=q8), A("QF", 256, 257, p=q8), True, True)
+    def every(fn, items):
+        for x in items:
+            fn(x)
 
-    def product(j):
-        a = 64 * (j % 4)
-        o, x, y = ("NU", "LT", "BB") if j < 4 else ("M", "T1", "DM")
-        tt(A(o, a, a + 64), A(x, a, a + 64), A(y, a, a + 64), OP.mult)
+    const = {
+        "pb": lambda: iota(PB, [[1, K]], 0, 0),
+        "pq": lambda: iota(pq, [[0, 1]], 15, 16),
+        "pc": lambda: iota(A("PC", 0, 1), [[0, 1]], 0, 1, False),
+        "pp": lambda: iota(pp, [[0, 1]], 0, 1),
+        "ig": lambda: iota(A("IG"), [[1, 8], [0, 16]], 0, 0),
+        "ia": lambda: iota(A("IA"), [[0, 16], [1, 16]], 0, 0),
+        "du": lambda: iota(A("DU"), [[0, 2], [1, 2]], W, 2),
+        "pra": lambda: places(*LV1), "prb": lambda: places(*LV2),
+        "om": lambda: iota(A("OM"), [[0, 64], [16, 16]], -16, 0),
+        "da": lambda: gcp(A("DA"), A("S16"), K),
+        "wi": lambda: no_place(1),
+        "cur": lambda: dma("G", "ldc", 16, T.QI[0:8, 256:257], T.cur[:], [A("QI", 256, 257)], [], allow_slow_non_contiguous=True),
+        "add": lambda: every(lambda j: dma("G", "lda", 64, T.AQ[:, j:j + K], T.FR[:, 0:K], [A("AQ", j, j + K)], [A("FR", 0, K)], accum_op=OP.add), range(0, TX, K)),
+        "run": lambda: dma("Y", "lde", 16, T.AQ[:, TX:OLD], T.AQ[:, 0:K], [A("AQ", TX, OLD)], [A("AQ", 0, K)]),
+        "zq": lambda: ts(A("ZQ", p=q8), A("PB", 0, 144, p=q8), A("PF", 3, 4, p=q8), OP.is_equal),
+        "qf": lambda: cp(A("QF", 0, K, p=q8), A("QI", 0, K, p=q8)),
+        "qm": lambda: every(lambda a: mm(A("PS2", 0, 16), A("ZQ", 15 - a, 143 - a, p=q8), A("QF", a, K, 16, p=q8), a == 0, a == 15), range(16)),
+        "qw": lambda: cp(A("QW"), A("PS2", 0, 16)),
+        "at": lambda: ts(A("AT"), IND(A("IDX"), A("QW")), float(PAD), OP.add),
+        "bq": lambda: ts(A("BQ", p=q8), A("IG", p=q8), A("PF", 4, 5, p=q8), OP.is_equal),
+        "cf": lambda: (cp(A("QF", K, K + 1, p=q8), A("QI", K, K + 1, p=q8)), mm(A("PS4", 0, 1), A("BQ", p=q8), A("QF", K, K + 1, p=q8), True, True)),
+        "nx": lambda: cp(A("NX", 0, 1), A("PS4", 0, 1)),
+        "pj": lambda: iota(A("PW", 68, 72), [[K, 4]], 0, 0),
+        "ha": lambda: (ms(A("PW", 0, 16), 0.5), ms(A("PW", 16, 32), 0.0)),
+        "hb": lambda: scan(A("PW", 32, 48), A("PW", 0, 16), A("PW", 16, 32), 2.0, OP.mult, OP.add),
+        "hc": lambda: tt(A("PW", 48, 64), A("PW", 32, 48), A("DM", 0, 16), OP.mult),
+        "hd": lambda: run("V", [down], [A("PW", 48, 64)], lambda: g.vector.tensor_reduce(down[0], T.PW[:, 48:64], AX.X, OP.add)),
+        "he": lambda: run("V", [up], [down], lambda: g.vector.reciprocal(up[0], down[0])),
+        "bw": lambda: ts(A("BW"), A("BB", 0, 128), up, OP.mult),
+        "fi": lambda: act(A("FI", 0, K), PB, scale=down, bias=-0.4995),
+        "fk": lambda: act(A("FI", K, K + 4), A("PW", 68, 72), scale=down, bias=-0.4995),
+        "fj": lambda: ts(A("FJ"), A("FI"), 1, OP.bitwise_and),
+        "fr": lambda: act(A("FR", 0, K), A("FJ", 0, K), scale=0.25),
+        "fs": lambda: act(A("FR", K, K + 4), A("FJ", K, K + 4), scale=0.25, bias=PAD + 0.125),
+        "aqa": lambda: every(lambda j: act(A("AQ", K * j, K * j + K), A("IDX", K * j, K * j + K), bias=A("FR", K + j, K + j + 1)), (0, 1)),
+        "aqb": lambda: every(lambda j: act(A("AQ", K * j, K * j + K), A("IDX", K * j, K * j + K), bias=A("FR", K + j, K + j + 1)), (2, 3)),
+        "xz": lambda: ms(A("X", 0, PAD), 0.0),
+        "wz": lambda: ms(A("WW"), 0.0),
+        "pa": lambda: (ts(A("PC", 1, 2), A("PC", 0, 1), 15, OP.bitwise_and), ts(A("PC", 2, 3), A("PC", 0, 1), 4, OP.arith_shift_right)),
+        "pf": lambda: cp(A("PF", 0, 2), A("PC", 1, 3)),
+        "pz": lambda: ts(pz, pa, 0.0, OP.is_equal),
+        "ph": lambda: ts(ph, pa, 0.5, OP.mult),
+        "pn": lambda: ts(pn, pa, 0.5, OP.mult, pp, OP.subtract),
+        "hh": lambda: ts(A("H"), A("PB", 0, 8), pg, OP.is_equal),
+        "dm": lambda: ts(A("DM"), A("IA", 0, 32), pa, OP.is_equal),
+        "wa": lambda: (ts(A("W16", 0, 16), A("DM", 0, 16), 256.0, OP.mult), ts(A("W16", 16, 32), A("DM", 1, 17), 16.0, OP.mult)),
+        "wb": lambda: tt(A("W16", 32, 48), A("W16", 16, 32), A("DM", 2, 18), OP.add),
+        "wc": lambda: tt(A("W16", 48, 64), A("W16", 0, 16), A("W16", 32, 48), OP.add),
+        "ww": lambda: every(lambda j: ts(A("WW", 16 * j, 16 * j + 129 * 15 + 1, 129), A("W16", 48, 64), A("H", j, j + 1), OP.mult), range(8)),
+        "bb": lambda: halves("BB", A("IG"), pg, OP.is_equal),
+        "ii": lambda: halves("II", A("PB", 0, 128), pp, OP.is_equal),
+        "ua": lambda: act(A("LT", 0, 128), A("PB", 0, 128), bias=pn, f=AF.Abs),
+        "nu": lambda: halves("NU", A("LT", 0, 128), ph, OP.is_le, -1.0, OP.mult),
+        "rr": lambda: ts(A("RR"), A("BB"), pz, OP.mult),
+        "rf": lambda: ts(A("R4"), A("BB"), pz, OP.mult, 4096.0, OP.mult),
+        "bf": lambda: ts(A("B4"), A("BB"), 4096.0, OP.mult),
+        "ni": lambda: ts(A("NI"), A("II", 0, 128), -1.0, OP.mult),
+        "in": lambda: ts(A("IN"), A("II"), -1024.0, OP.mult),
+        "ib": lambda: ts(A("IB"), A("II"), 1024.0, OP.mult),
+        "zz": lambda: ms(A("ZD"), 0.0),
+        "zd": lambda: ts(A("ZD", 15, K, 16), A("BB", 15, K, 16), pz, OP.mult),
+        "zy": lambda: ms(A("ZC"), 0.0),
+        "zc": lambda: ts(A("ZC", 15, K, 16), A("BB", 15, K, 16), 2048.0, OP.mult),
+        "le": lambda: act(A("L", 2560, 2560 + K), PB, bias=256.0, scale=0.0, f=AF.Silu),
+        "lf": lambda: act(A("L", 2560 + K, 2560 + W), A("WW", K, W), bias=256.0),
+        "tz": lambda: ms(B("TRI"), 0.0),
+        "tri": lambda: every(lambda b: ts(B("TRI", b), A("IA", 0, 32), pa, OP.is_ge, FAR, OP.mult), ((0, 3, 2), (3, 6, 2))),
+        "nm": lambda: ts(A("NG"), A("IA"), pa, OP.not_equal, -FAR, OP.mult),
+        "nz": lambda: ms(B("ND"), 0.0),
+        "nd": lambda: every(lambda b: cp(B("ND", b), A("NG", 0, 32)), ((2, 5, 2), (7, 10, 2))),
+        "nf": lambda: ts(A("N4"), A("BB", 0, 128), -4096.0, OP.mult),
+        "eo": lambda: ms(A("EM"), 1.0),
+        "ez": lambda: ms(A("EM", 0, 80, 48), 0.0),
+        "em": lambda: ms(A("EM", 32, 80, 32), 8192.0),
+        "pl": lambda: iota(A("PL"), [[32, 8], [-16, 2], [1, 16]], 16, 0),
+        "po": lambda: ts(A("SP"), A("IW"), float(W), OP.add),
+        "sm": lambda: ts(A("SM"), A("IA"), 0.0, OP.not_equal),
+        "iw": lambda: ts(A("IW"), A("PB", 0, K, 16), pa, OP.add),
+        "pu": lambda: ts(A("PU"), A("NU"), -1.0, OP.mult),
+        "mo": lambda: (ms(A("M3"), 1.0), ms(A("C3"), 0.0)),
+        "mz": lambda: (ms(A("M3", 0, 48, 3), 0.0), ms(A("C3", 1, 48, 3), -1024.0)),
+        "cc": lambda: ts(A("C3", 2, 48, 3), A("IW"), 256.0, OP.add),
+        "fl": lambda: ms(A("FL", 16, 48), 0.0),
+    }
 
     def obank(c0, c1):
-        return A("PS7" if c0 >= LV2[0] else "PS6", c0, c1)
+        return A([b for b, (a, _) in zip(("PS3", "PS6", "PS7"), PARTS) if a <= c0][-1], c0, c1)
 
-    def pick_first(ps="PS4", b0=0, b1=16):
+    def pick16(o, weights, shift, rows, start=True, stop=True):
         for a in range(16):
-            mm(A(ps, b0, b1), A("ZD", 15 - a, 143 - a), B("S16", (b0, b1), a), a == 0, a == 15)
+            mm(o, A(weights, 15 - a + shift, 143 - a + shift), rows(a), start and a == 0, stop and a == 15)
 
-    def open_compare(t, passes=range(4)):
-        for p in passes:
-            mm(A(CMP[p], 0, 192), A("II", 0, 128), B("TRI"), True, False)
-            views(p, "RR", "S16", t == 1)
+    def pick_first(e0, e1):
+        pick16(A("PS2", 2 * e0, 2 * e1), "ZD", 0, lambda a: A("S16", 32 * e0 + a, 32 * e1, 16))
 
-    def views(p, weights, name, stop):
-        b = PASSES[p][0] // 16
-        for o in (0, 96):
-            mm(A(CMP[p], o, o + 64), A(weights, 0, 128), B(name, (b, b + 4)), False, False)
-            mm(A(CMP[p], o + 64, o + 96), A(weights, 0, 128), B(name, (b, b + 4, 2)), False, stop and o == 96)
+    def others(e0, e1):
+        for e in range(e0, e1):
+            if e % 2 == 0:
+                mm(A("PS4", 48 * e, 48 * e + 96), A("II", 0, 128), B("TRI"), e == e0, False)
+            mm(A("PS4", 48 * e, 48 * e + 16), A("RR", 0, 128), A("S16", 32 * e, 32 * e + 16), False, False)
+            mm(A("PS4", 48 * e + 16, 48 * e + 48), A("RR", 0, 128), A("S16", 32 * e, 32 * e + 32), False, False)
+
+    def own_first(e0, e1):
+        act(B("S0X", (e0, e1), (0, 2)), A("PS2", 2 * e0, 2 * e1))
+        act(B("S0X", (e0, e1), 2), A("PS2", 2 * e0 + 1, 2 * e1, 2))
+
+    def less_own(e0, e1):
+        for a in range(16):
+            mm(A("PS4", 48 * e0 + a, 48 * e1, 16), A("NI"), B("S0X", (e0, e1)), False, a == 15)
+
+    def matches(e0, e1):
+        ts(A("EQ", 48 * e0, 48 * e1), A("PS4", 48 * e0, 48 * e1), 0.0, OP.is_equal)
+
+    def run_terms(p, w1, x1, w2, x2, stop):
+        for b in range(*PASSES[p], 32):
+            o = (b - PASSES[p][0]) // 32 * 80
+            a, a2 = (b * 3 // 2, b * 3 // 2 + 16) if x1 == "EQ" else (b, b)
+            mm(A(CMP[p], o, o + 32), A(w1, 0, 128), A(x1, a2, a2 + 32), False, False)
+            mm(A(CMP[p], o + 48, o + 64), A(w1, 0, 128), A(x1, a, a + 16), False, False)
+            mm(A(CMP[p], o + 32, o + 48), A(w2, 0, 128), A(x2, b + 16, b + 32), False, False)
+            mm(A(CMP[p], o + 64, o + 80), A(w2, 0, 128), A(x2, b, b + 16), False, stop and b + 32 == PASSES[p][1])
+
+    def open_compare(t, p):
+        n32 = (PASSES[p][1] - PASSES[p][0]) // 32
+        mm(A(CMP[p], 0, 80 * n32), A("II", 0, 128), B("ND", (0, 5 * n32)), True, False)
+        run_terms(p, "II", "EQ", "RR", "S16", t == 1)
 
     def close_compare(p):
-        views(p, "B4", "NE", True)
+        run_terms(p, "N4", "NE", "B4", "NE", True)
 
-    def spread_first(ps="PS4", b0=0, b1=16, p0=0, p1=4):
-        act(A("S0W", b0, b1), A(ps, b0, b1))
-        act(A("SRP", 96 * p0, 96 * p1), IND(A("S0W", 0, b1), A("SL", 6 * p0, 6 * p1)))
-
-    def compare(p):
-        tt(A("EP", 192 * p + 1, 192 * p + 192, 2), A(CMP[p], 96, 192), B("ML"), OP.min)
-        tt(A("EP", 192 * p, 192 * p + 192, 2), A(CMP[p], 0, 96), A("SRP", 96 * p, 96 * p + 96), OP.is_equal)
-
-    def lock_scan(p):
-        scan(A("EO", 192 * p, 192 * p + 192), A("EM"), A("EP", 192 * p, 192 * p + 192), 0.0, OP.mult, OP.max)
+    def lock_scan(e):
+        p = [c0 <= 32 * e for c0, _ in PASSES].index(True)
+        o = (32 * e - PASSES[p][0]) // 32 * 80
+        scan(B("EO", e), A("EM"), A(CMP[p], o, o + 80), 0.0, OP.mult, OP.max)
 
     def lock_list(p):
-        b = PASSES[p][0] // 16
-        cp(A("LO", b + 1, b + 4, 2), A("EO", 192 * p + 63, 192 * p + 128, 64))
-        cp(A("LO", b, b + 4, 2), A("EO", 192 * p + 159, 192 * p + 192, 32))
+        e0, e1 = PASSES[p][0] // 32, PASSES[p][1] // 32
+        tt(A("LO", 2 * e0, 2 * e1), B("EO", (e0, e1), (47, 80, 32)), A("DU", 0, 2 * (e1 - e0)), OP.min)
 
     def lock_write(t, e):
-        cp(IND(table(t, 2560), A("LO", 2 * e, 2 * e + 2)), A("PB", 32 * e, 32 * e + 32))
+        cp(IND(table(t, 2560), A("LO", 2 * e, 2 * e + 2)), A("PL", 32 * e, 32 * e + 32))
 
     def own_gather(q, t, c0, c1):
         gather(q, A("OG", 16 * c0, 16 * c1), IND(A("X", PAD, PAD + W), A("NM", 256 * (t - 1) + c0, 256 * (t - 1) + c1)))
@@ -410,25 +436,19 @@ def rank_program(g, core, T, topo):
         mm(A(ps, c0, c1), A("II", 0, 128), A("OG", 16 * c0, 16 * c1, 16), True, False)
         mm(A(ps, c0, c1), A("II", 0, 128), A("OS", 16 * c0 + 15, 16 * c1, 16), False, True)
 
-    def clamp(c0, c1):
-        tt(A("MN", c0, c1), obank(c0, c1), A("M", c0, c1), OP.min)
-
     def offsets(c0, c1):
-        scan(A("SC", c0, c1), A("SM", c0, c1), A("MN", c0, c1), 0.0, OP.mult, OP.add)
+        scan(A("SC", c0, c1), A("SM", c0, c1), obank(c0, c1), 0.0, OP.mult, OP.max)
 
     for t in range(1, R):
         c, u = t - 1, SG[t % 2]
         SU = 256 * c
         rot, back = 16 * ((8 - u) % 8), 16 * u
+        last = t == R - 1
+
         def nbank(p):
             return A(("PS0", "PS1", "PS6", "PS7")[p if t == 1 else p % 2], *PASSES[p])
 
-        def digits(q, p, half=None):
-            c0, c1 = PASSES[p]
-            v = c0 + (32 if t == 1 else NV[p])
-            a, b = (c0, v) if q == "V" else (v, c1)
-            if half is not None:
-                a, b = (a, (a + b) // 4 * 2) if half == 0 else ((a + b) // 4 * 2, b)
+        def digits(q, a, b):
             gather(q, A("G", 16 * a, 16 * b), IND(A("X", 0, PAD + W), A("AT", a, b)))
 
         def weigh(p):
@@ -447,88 +467,39 @@ def rank_program(g, core, T, topo):
         def restore(p):
             tt(A("DN", *PASSES[p]), nbank(p), P16("S16", *PASSES[p]), OP.add)
 
-        def count_changed(_):
-            for a in range(16):
-                mm(A("PS2", 0, 16), A("ZC", 15 - a + rot, 143 - a + rot), B("NE", None, a), False, a == 15)
-
         def small(j):
             if j == 2:
                 ts(A("FL", 16, 32), A("PS2", 0, 16), 2048.0, OP.is_ge)
-            elif j == 3:
-                ts(A("THK"), A("FL", 16, 32), 8192.0, OP.mult, W - 0.5, OP.add)
             else:
                 a = 128 * (j - 4)
                 ts(A("DA", a, a + 128), A("DN", a, a + 128), W - 1, OP.bitwise_and)
 
-        step = {"v": lambda p: digits("V", p), "a": lambda p: digits("V", p, 0), "b": lambda p: digits("V", p, 1), "n": weigh, "t": top, "d": differ, "e": restore,
-                "c": close_compare, "k": compare, "s": lock_scan, "l": lock_list, "w": lambda e: lock_write(t, e), "z": count_changed,
-                "x": small, "m": lambda a, b: own_max(16 * a, 16 * b)}
+        step = {"v": lambda a, b: digits("V", a, b), "n": weigh, "t": top, "d": differ,
+                "e": restore, "o": lambda p: open_compare(t, p), "c": close_compare, "s": lock_scan, "l": lock_list,
+                "N": lambda a, b: digits("S", a, b), "G": lambda a, b: own_gather("S", t, a, b), "H": lambda a, b: own_gather("V", t, a, b),
+                "k": matches, "p": pick_first, "q": own_first, "Q": others, "K": less_own,
+                "w": lambda e: lock_write(t, e), "x": small, "m": lambda a, b: own_max(16 * a, 16 * b),
+                "y": lambda _: mm(A("PS2", 0, 16), A("II", rot, rot + 128), B("S0X", None, (0, 2)), True, False),
+                "z": lambda _: pick16(A("PS2", 0, 16), "ZC", rot, lambda a: A("NE", a, K, 16), start=False)}
 
         def steps(text):
             for s in text.split():
-                step[s[0]](*[int(j) for j in s[1:].split("-")])
+                if s in const:
+                    const[s]()
+                else:
+                    step[s[0]](*[int(j) for j in s[1:].split("-") if j])
 
-        def fill(j):
-            steps((FILL1 if t == 1 else FILL if t < R - 1 else FILL6)[j])
-
-        if t > 1:
-            for a in range(16):
-                mm(A("PS2", 0, 16), A("ZD", 15 - a + rot, 143 - a + rot), B("S16", None, a), a == 0, False)
-            open_compare(t)
-            for p in range(4):
-                digits("S", p)
-            for c0, c1 in OWN0:
-                own_gather("S", t, c0, c1)
-            steps(LATER)
-        else:
+        if t == 1:
             step["r"] = lambda p: tt(P16("S16", *PASSES[p]), nbank(p), A("RM", *PASSES[p]), OP.subtract)
             step["u"] = lambda p: cp(A("SU", *PASSES[p]), P16("S16", *PASSES[p]))
             step["g"] = lambda j: send_names(1, j)
-            step["q"] = vector_constants
-            step["p"] = product
-            for p in range(4):
-                digits("S", p)
-            steps(START)
-            dma("G", "ldc", 16, T.QI[0:8, 256:257], T.cur[:], [A("QI", 256, 257)], [], allow_slow_non_contiguous=True)
-            places(*LV1)
-            act(A("PB"), PI)
-            act(A("FR", 0, K), A("FJ", 0, K), scale=0.25)
-            act(A("FR", K, K + 4), A("FJ", K, K + 4), scale=0.25, bias=PAD + 0.125)
-            pick_first("PS4", 8, 16)
-            spread_first("PS4", 8, 16, 0, 2)
-            for j in range(4):
-                act(A("IDQ", K * j, K * j + K), A("IDX", K * j, K * j + K), bias=A("FR", K + j, K + j + 1))
-            steps("b3 n3 t2 q0 r2 u1")
-            open_compare(t, (0, 1))
-            steps("q1 t3 u2 r3")
-            pick_first("PS2", 0, 8)
-            open_compare(t, (2, 3))
-            spread_first("PS2", 0, 8, 2, 4)
-            steps("k0 u3 g1")
-            for j in range(4):
-                dma("G", "lda", 64, T.IDQ[:, K * j:K * j + K], T.FR[:, 0:K], [A("IDQ", K * j, K * j + K)], [A("FR", 0, K)], accum_op=OP.add)
-            act(A("T1"), PI, bias=2048.0, scale=2.0)
-            for sem, a, b in (("lde", TX, TX + K), ("ldf", TX + K, 2 * TX), ("ldg", 2 * TX, 2560)):
-                dma("Y", sem, 16, T.IDQ[:, a:b], T.IDQ[:, a % TX:a % TX + b - a], [A("IDQ", a, b)], [A("IDQ", a % TX, a % TX + b - a)])
-            places(*LV2)
-            act(A("R4"), A("RR"), scale=4096.0)
-            act(A("NI"), A("II", 0, 128), scale=-1.0)
-            act(A("IW"), A("PI", 0, 256, 16), bias=pa)
-            act(A("SM"), A("IA"), f=AF.Sign)
-            act(A("IN"), A("II"), scale=-1024.0)
-            for o, v in ((A("THK"), W - 0.5), (A("M3", 0, 48, 3), 0.0), (A("M3", 1, 48, 3), 1.0), (A("M3", 2, 48, 3), 1.0),
-                         (A("C3", 0, 48, 3), 0.0), (A("C3", 1, 48, 3), -1024.0)):
-                act(o, A("IW"), bias=v, scale=0.0)
-            act(A("C3", 2, 48, 3), A("IW"), bias=256.0)
-            gcp(A("DA"), B("S16"), K)
-            iota(A("SW", 0, 256), [[0, 256]], NEW, 0)
-            iota(A("OM"), [[0, 64], [16, 16]], -16, 0)
-            steps(FIRST)
-        for c0, c1 in ((0, LV2[0]), LV2):
+
+        def open_offsets(j):
+            c0, c1 = PARTS[j]
             mm(obank(c0, c1), A("RR", rot, rot + 128), P16("S16", c0, c1), True, False)
+            mm(obank(c0, c1), A("II", 0, 128), A("NG", c0, c1), False, False)
             if t > 1:
                 mm(obank(c0, c1), A("B4", rot, rot + 128), P16("NE", c0, c1), False, False)
-        s0, s1 = LS[0][0], LS[-1][1]
 
         def waits(c0, c1):
             tt(A("LG", 16 * c0, 16 * c1), IND(table(t, W), A("SU", SU + c0, SU + c1)), A("PR", 16 * c0, 16 * c1), OP.is_lt)
@@ -542,127 +513,122 @@ def rank_program(g, core, T, topo):
             for k in range(16):
                 mm(A("PS4", c0, c1), A("ZD", 15 - k, 143 - k), A("LG", 16 * c0 + k, 16 * c1, 16), False, k == 15)
 
-        waits(*LV1)
-        for c0, c1 in LS:
+        def locks(c0, c1):
             act(A("LG", 16 * c0, 16 * c1), IND(table(t, W), A("SU", SU + c0, SU + c1)))
-        waits(*LV2)
-        pick(*LS[0])
-        count(*LV1, False)
-        pick(*LS[1])
-        if t > 1:
-            own_gather("S", t, *OWNM)
-        else:
-            act(A("AW", 0, 256), IND(A("IDQ", 0, TX), A("QW")))
-        act(A("LT", s0, s1), A("PS4", s0, s1), scale=-1.0, f=AF.Relu)
-        count(*LV2, True)
-        mm(obank(s0, s1), A("B4", rot, rot + 128), A("LT", s0, s1), False, True)
-        if t > 1:
-            for c0, c1 in OWN1:
-                own_gather("S", t, c0, c1)
-        else:
-            for c0, c1 in PASSES[:2]:
-                own_gather("S", t, c0, c1)
-        fill(0)
-        clamp(*LV2)
-        clamp(0, LV2[0])
-        offsets(*LV2)
-        offsets(0, LV2[0])
-        fill(1)
-        cp(A("OFS", 16 * c, 16 * c + 16), A("SC", 15, 256, 16))
-        send_offsets(t)
+
+        def lower(c0, c1, stop):
+            act(A("LT", c0, c1), A("PS4", c0, c1), scale=-1.0, f=AF.Relu)
+            mm(obank(c0, c1), A("B4", rot, rot + 128), A("LT", c0, c1), False, bool(stop))
+
+        def send():
+            tt(A("OFS", 16 * c, 16 * c + 16), A("SC", 15, 256, 16), A("SP"), OP.min)
+            send_offsets(t)
+
         def cand(j):
             return A("PS0", j, 48, 3)
 
         def un(name):
             return A(name, back, back + 128)
 
-        keep, redo = A("FL", 0, 16), A("FL", 16, 32)
-        tt(keep, A("SC", 15, 256, 16), A("THK"), OP.is_gt)
-        mm(A("PS0", 0, 48), A("II", 0, 128), A("C3"), True, False)
-        if t > 1:
-            mm(cand(1), un("NU"), redo, False, False)
-            mm(cand(1), un("IB"), redo, False, False)
-            mm(cand(2), un("IN"), redo, False, False)
-        else:
-            cp(A("NX", 0, 1), A("PS2", 16, 17))
-        fill(2)
-        scan(A("CF"), A("ZE"), A("FL"), 0.0, OP.add, OP.add)
-        mm(cand(0), un("NU"), keep, False, False)
-        mm(cand(2), un("IN"), keep, False, False)
-        mm(cand(0), un("BB"), A("CF", 0, 16), False, False)
-        mm(cand(1), un("BB"), A("CF", 16, 32), False, True, False)
-        mm(A("PS0", 64, 65), un("BB"), A("CF", 31, 32), True, True)
-        fill(3)
-        scan(A("PP"), A("M3"), A("PS0", 0, 48), 0.0, OP.mult, OP.max)
-        ts(A("TL"), A("IW"), A("NX", c, t), OP.add, A("PS0", 64, 65), OP.subtract)
-        ts(A("NX", t, t + 1), A("NX", c, t), A("PS0", 64, 65), OP.subtract, 256.0, OP.add)
-        cp(A("DW"), A("PP", 2, 48, 3))
-        w0, w1 = 512 * (c % 2), 512 * (t % 2)
-        act(A("AW", w1, w1 + 256), IND(A("IDQ", 0, TX + K * t), A("TL")))
-        if t == 1:
-            for c0, c1 in PASSES[2:]:
-                own_gather("S", t, c0, c1)
-        fill(4)
-        early, late = ((64, K), (0, 64)) if t == 1 else ((0, EARLY), (EARLY, K))
-        if t > 1:
-            sums(*early)
-            act(A("TT", *early), A("PS1", *early))
-        cp(IND(A("SW", 512 * c, 512 * c + 512), A("DW")), A("DA"))
-        kept = A("SW", 512 * c, 512 * c + 256)
-        fill(5)
-        if t < R - 1:
-            if t == 1:
-                cp(A("SU", SU + 256, SU + 512), kept)
-            else:
-                gcp(A("SU", SU + 256, SU + 512), kept, K)
-            send_names(t + 1)
-            gather("V" if t == 1 else "S", B("S16"), kept)
-        else:
-            dma("Y", "st", 64, T.yd[:], kept[0], [], [kept])
-        fill(6)
-        if t > 1:
-            sums(*late, "PS0")
-        if t < R - 1:
-            pick_first()
-        if t > 1:
-            o, i = IND(A("AW", w1, w1 + 512), A("DW")), A("AW", w0, w0 + 256)
-            run("S", [o], [i], lambda: g.scalar.activation(o[0], i[0], AF.Silu))
-        else:
-            cp(IND(A("AW", w1, w1 + 512), A("DW")), A("AW", w0, w0 + 256))
-            run("V", [A("PW", 65, 66)], [pdown], lambda: g.vector.reciprocal(T.PW[:, 65:66], pdown[0]))
-            ts(A("IB"), A("II"), 1024.0, OP.mult)
-            ts(A("BW"), A("BB", 0, 128), A("PW", 65, 66), OP.mult)
-            ms(A("ZC"), 0.0)
-            own_max(*PASSES[2])
-            ts(A("ZC", 15, 256, 16), A("BB", 15, 256, 16), 2048.0, OP.mult)
-            sums(*early)
-            act(A("TT", *early), A("PS1", *early))
-        if t < R - 1:
-            gcp(A("AT"), A("AW", w1, w1 + 256), K)
-            spread_first()
-        if t == 1:
-            own_max(*PASSES[3])
-            sums(*late, "PS0")
-        ts(A("TR", *early), A("TT", *early), 16.0, OP.is_ge, -16.0, OP.mult)
-        ts(A("TR", *late), A("PS0", *late), 16.0, OP.is_ge, -16.0, OP.mult)
-        cp(A("TT", *late), A("PS0", *late))
-        if t == 1:
-            iota(table(2, W), [[0, W]], 256, 0)
-        if t + 2 < R:
-            iota(table(t + 2, W), [[0, W]], 256, 0)
-        if t < R - 1:
-            iota(A("SW", 512 * t, 512 * t + 256), [[0, 256]], -1 if t == R - 2 else NEW, 0)
-        if t == R - 1:
-            act(A("DI"), A("AW", w1, w1 + 256), scale=4.0, bias=-0.25)
-        tt(IND(A("X", PAD, PAD + 2560), A("OFF", 16 * c, 16 * c + 16)), A("TT"), A("TR"), OP.add)
+        keep, redo, stay, z = A("FL", 0, 16), A("FL", 16, 32), A("PS0", 64, 65), A("NX", t, t + 1)
 
-    ts(A("DJ"), A("DI"), 1, OP.bitwise_and)
-    dma("Y", "st", 64, T.yx[0:64, :], T.X[0:64, PAD:PAD + W], [], [A("X")])
-    dma("S", "st", 64, T.yx[64:128, :], T.X[64:128, PAD:PAD + W], [], [A("X")])
-    act(A("RM"), A("DJ"))
-    mm(A("PS1", 0, K), A("BW"), A("RM"), True, True)
-    act(A("T1"), A("PS1", 0, K))
-    dma("Y", "st", 64, T.yq[:], T.T1[0:128:16, :], [], [A("T1")])
+        def renumber(j):
+            if j == 0:
+                ts(keep, A("SC", 15, 256, 16), float(W), OP.is_ge)
+                mm(A("PS0", 0, 48), A("II", 0, 128), A("C3"), True, False)
+                if t > 1:
+                    mm(cand(1), un("NU"), redo, False, False)
+                    mm(cand(1), un("IB"), redo, False, False)
+                    mm(cand(0), un("PU"), redo, False, False)
+            elif j == 1:
+                scan(A("CF"), A("FL", 0, 32), A("FL", 16, 48), 0.0, OP.add, OP.subtract)
+                mm(cand(0), un("NU"), keep, False, False)
+                mm(cand(2), un("IN"), keep, False, False)
+                mm(cand(0), un("BB"), A("CF", 0, 16), False, False)
+                mm(cand(1), un("BB"), A("CF", 16, 32), False, True, False)
+                mm(stay, un("BB"), A("CF", 31, 32), True, True)
+            elif j == 2:
+                scan(A("PP"), A("M3"), A("PS0", 0, 48), 0.0, OP.mult, OP.max)
+            elif j == 3:
+                cp(A("DW"), A("PP", 2, 48, 3))
+            elif j == 4:
+                cp(IND(A("SW", 512 * c, 512 * c + 512), A("DW")), A("DA"))
+            elif j == 5:
+                if t == 1:
+                    ts(z, A("NX", c, t), stay, OP.subtract)
+                else:
+                    ts(z, A("NX", c, t), A("NX", 8 + c, 8 + t), OP.add, stay, OP.subtract)
+            elif j == 6:
+                ts(A("TL"), A("IW"), z, OP.add, float(K * c), OP.add)
+            elif not last:
+                ts(A("NX", 8 + t, 9 + t), z, float(TX - K * t), OP.is_ge, -float(TX), OP.mult)
+
+        w0, w1, kept = 512 * (c % 2), 512 * (t % 2), A("SW", 512 * c, 512 * c + K)
+
+        def reorder(j, q="G"):
+            if j == 0:
+                act(A("AW", w1, w1 + K), IND(A("AQ"), A("TL")))
+            elif j == 1:
+                o, i = IND(A("AW", w1, w1 + 512), A("DW")), A("AW", w0, w0 + K)
+                if q == "V":
+                    cp(o, i)
+                else:
+                    run("S", [o], [i], lambda: g.scalar.activation(o[0], i[0], AF.Silu))
+            elif last:
+                if j == 5:
+                    dma("Y", "st", 64, T.yd[:], kept[0], [], [kept])
+                elif j == 6:
+                    act(A("DI"), A("AW", w1, w1 + K), scale=4.0, bias=-0.25)
+                elif j == 7:
+                    ts(A("DJ"), A("DI"), 1, OP.bitwise_and)
+                elif j == 8:
+                    act(A("RM"), A("DJ"))
+                    mm(A("PS1", 0, K), A("BW"), A("RM"), True, True)
+                elif j == 9:
+                    act(A("T1"), A("PS1", 0, K))
+                    dma("Y", "st", 64, T.yq[:], T.T1[0:128:16, :], [], [A("T1")])
+            elif j == 2:
+                others(0, 8)
+            elif j == 4:
+                less_own(0, 8)
+            elif j == 3:
+                copy(q, A("S16"), kept)
+            elif j == 5:
+                copy(q, A("SU", SU + 256, SU + 512), kept)
+                send_names(t + 1)
+            elif j == 6:
+                copy(q, A("AT"), A("AW", w1, w1 + K))
+            elif j == 7:
+                pick_first(0, 8)
+            elif j == 8:
+                own_first(0, 8)
+            else:
+                if t == 1:
+                    iota(table(2, W), [[0, W]], 256, 0)
+                no_place(t + 1)
+                if t + 2 < R:
+                    iota(table(t + 2, W), [[0, W]], 256, 0)
+
+        def digit(c0, c1, j):
+            return A("PS%d" % j, c0, c1)
+
+        step.update({"L": waits, "S": locks, "P": pick, "C": lambda a, b, s: count(a, b, bool(s)), "T": lower, "A": open_offsets, "B": offsets, "O": send,
+                     "U": lambda j: reorder(j, "S"), "V": lambda j: reorder(j, "V"),
+                     "R": renumber, "J": reorder,
+                     "h": lambda a, b, j: sums(a, b, "PS%d" % j), "i": lambda a, b, j: act(A("TT", a, b), digit(a, b, j)),
+                     "j": lambda a, b, j: cp(A("TT", a, b), digit(a, b, j)),
+                     "f": lambda a, b, j=None: ts(A("TR", a, b), A("TT", a, b) if j is None else digit(a, b, j), 16.0, OP.is_ge, -16.0, OP.mult),
+                     "I": lambda: act(A("AW", 0, K), IND(A("AQ", 0, TX), A("QW")))})
+
+        def write():
+            tt(IND(A("X", PAD, PAD + 2560), A("OFF", 16 * c, 16 * c + 16)), A("TT"), A("TR"), OP.add)
+            if last:
+                dma("Y", "st", 64, T.yx[0:64, :], T.X[0:64, PAD:PAD + W], [], [A("X")])
+                dma("S", "st", 64, T.yx[64:128, :], T.X[64:128, PAD:PAD + W], [], [A("X")])
+
+        step["X"] = write
+        steps(FIRST if t == 1 else TAIL if last else LATER)
+
     for q in ("V", "S", "P", "G"):
         wait("G", "e" + q, cnt[q])
     wait("G", "ls", sends)

import numpy as np
from concourse.bass import DstId, RemoteDMATransfer
from concourse.mybir import AluOpType as OP, ActivationFunctionType as AF, AxisListType as AX

W, TX, K, R = 2048, 1024, 256, 7
SR, SG = (1, 3), (0, 5)
F32, BF, F16, I32, U16 = "float32", "bfloat16", "float16", "int32", "uint16"
NEW = -40960
FAR = float(2 ** 26)
OLD = TX + K
PAD = 32


def _sb(n, d):
    return ("sbuf", [128] + (list(n) if isinstance(n, tuple) else [n]), d)


PASSES = ((192, 256), (128, 192), (64, 128), (0, 64))
CMP = ("PS3", "PS5", "PS6", "PS7")
PARTS = ((0, 80), (80, 192), (192, 256))
LV1, LV2 = PARTS[0], PARTS[2]
FIRST = "wz pb pq pc pa zq qf tz zz ig pf qm eo ha hh ia le pz nz dm nm xz wa qw nd wb at prb lf N224-256 hb bb wc du v192-224 N160-192 ww n0 v128-160 n1 v64-96 N96-128 t0 tri N24-64 r0 t1 zd u0 r1 pp v0-24 n2 p4-8 ii hc rr hd ni pra em q4-8 u1 pn n3 fi t2 Q4-8 pl pj t3 K4-8 r2 ez r3 ua Q0-4 fk fj bf k4-8 u2 p0-4 o1 fs o0 u3 s5 s6 s7 l0 fr g0 q0-4 s4 K0-4 k0-4 o2 w7 o3 ph nf aqb g1 l1 w6 s3 s2 w5 bq l2 w4 da s1 s0 om w3 nu l3 w2 A1 zy mo A0 w1 mz aqa G224-256 w0 G192-224 A2 sm iw fl L0-80 rf L192-256 cc S80-140 P80-140 H0-16 C0-80-1 B0-80 S140-192 add P140-192 C192-256-1 po G128-192 cur T80-192-1 cf G64-128 he in m14-16 B192-256 G16-64 B80-192 m12-14 R0 O nx I R1 m8-12 wi R2 R5 m4-8 R3 bw run R6 h64-256-1 J0 R7 R4 m0-4 V3 h0-64-0 J5 J7 ib i64-256-1 f64-256 f0-64-0 j0-64-0 J1 J6 J2 zc J9 J8 J4 X pu"
LATER = "v192-224 k4-8 N224-256 v128-160 N160-192 n0 t0 o0 n1 v64-80 o1 d0 c0 N96-128 v80-96 t1 v12-24 d1 k0-4 s6 s7 N24-64 v0-12 n2 l0 t2 c1 s5 s4 w7 o2 d2 l1 w6 e2 n3 t3 w5 d3 c2 y0 s2 s3 w4 o3 l2 c3 e1 e0 w3 G0-48 s1 G48-96 A0 z0 s0 G96-128 w2 A1 l3 m2-3 w1 e3 m0-1 w0 x5 A2 x4 S80-140 P80-140 S140-192 L0-80 C0-80-1 L192-256 P140-192 C192-256-1 x2 m7-8 G128-160 m4-5 T80-192-1 m3-4 G160-208 m1-2 B0-80 m6-7 m9-10 B192-256 B80-192 m8-9 R0 O m5-6 R1 H240-256 m11-12 R2 R5 m10-11 R3 G208-240 m12-13 R6 J0 R4 J5 m14-15 h0-208-1 m13-14 m15-16 h208-256-0 i0-208-1 J1 V3 J7 J8 f0-208 J6 j208-256-0 f208-256-0 J2 J4 R7 J9 X"
TAIL = "v192-224 k4-8 v128-160 v64-80 N224-256 n0 t0 k0-4 N160-192 o0 d0 n1 v80-96 o1 t1 v12-24 c0 d1 s6 s7 v0-12 N96-128 n2 l0 t2 c1 e2 o2 w7 d2 s4 s5 w6 N24-64 n3 c2 l1 t3 w5 o3 y0 s3 d3 s2 w4 l2 c3 w3 s1 s0 G0-48 z0 e0 G48-96 w2 A0 l3 m2-3 w1 A2 x2 e1 w0 A1 G96-128 S80-140 e3 P80-140 S140-192 m1-2 L0-80 C0-80-1 L192-256 G128-160 m7-8 m0-1 P140-192 C192-256-1 m4-5 T80-192-1 x5 m9-10 x4 B0-80 m6-7 B192-256 B80-192 m3-4 R0 O R1 H240-256 G208-240 R5 R6 R2 m13-14 R3 m14-15 m5-6 G160-208 m10-11 m8-9 m15-16 h208-256-0 J0 m12-13 m11-12 R4 h0-208-1 J5 J1 j208-256-0 J6 J7 i0-208-1 f208-256-0 J8 f0-208 X J9"

SCRATCH = {
    "X": _sb(PAD + 2560, BF), "IDX": _sb(TX, I32), "AQ": _sb(OLD, F32), "AW": _sb(2 * 512, F32), "L": _sb(2 * 2560, BF),
    "FR": _sb(260, F32), "FI": _sb(260, I32), "FJ": _sb(260, I32), "PW": _sb(72, F32), "BW": _sb(128, BF),
    "G": _sb(4096, BF), "LG": _sb(4096, BF), "OG": _sb(4096, BF), "OS": _sb(4096, BF), "PR": _sb(4096, BF),
    "QI": _sb(260, I32), "QF": _sb(258, F16), "QW": _sb(16, U16),
    "PB": _sb(256, BF), "IA": _sb(256, BF), "IG": _sb(128, BF), "DI": _sb(256, I32), "DJ": _sb(256, I32),
    "PC": _sb(4, I32), "PF": _sb(10, F32), "IW": _sb(16, F32),
    "ZQ": _sb(144, BF), "BQ": _sb(128, BF), "BB": _sb(256, BF), "B4": _sb(256, BF), "RR": _sb(256, BF), "R4": _sb(256, BF),
    "ZD": _sb(256, BF), "ZC": _sb(256, BF), "II": _sb(256, BF), "NI": _sb(128, BF), "NU": _sb(256, BF), "IB": _sb(256, BF), "IN": _sb(256, BF),
    "DM": _sb(32, BF), "DU": _sb(4, F32), "T1": _sb(256, F32), "YD": _sb(256, F32), "NG": _sb(256, BF), "ND": _sb((10, 16), BF), "N4": _sb(128, BF),
    "OM": _sb(1024, BF), "WW": _sb(2064, BF), "W16": _sb(64, BF), "H": _sb(8, F32), "SP": _sb(16, F32), "OD": _sb(16, BF),
    "TRI": _sb((6, 16), BF), "EQ": _sb(384, BF), "EM": _sb(80, F32), "PL": _sb(256, BF), "EO": _sb((8, 80), F32),
    "S0X": _sb((8, 3), F16), "LO": _sb(16, U16),
    "SM": _sb(256, BF), "SC": _sb(256, F32), "LT": _sb(256, BF), "OFS": _sb(96, U16),
    "AT": _sb(256, U16), "RM": _sb(256, BF), "NE": _sb(256, BF), "DN": _sb(256, I32), "DA": _sb(K, I32),
    "S16": _sb(256, F16), "SU": _sb(6 * 256, U16),
    "FL": _sb(48, BF), "CF": _sb(32, BF), "PU": _sb(256, BF), "C3": _sb(48, F16), "M3": _sb(48, F32),
    "PP": _sb(48, F32), "DW": _sb(16, U16), "TL": _sb(16, U16), "NX": _sb(16, F32),
    "SW": _sb(6 * 512, F32), "TT": _sb(256, BF), "TR": _sb(256, BF),
    "NM": _sb(6 * 256, U16), "OFF": _sb(96, U16),
}


def _names(t):
    c = 256 * (t - 1)
    return (("n1", *PASSES[0]), ("m1", 0, PASSES[0][0])) if t == 1 else (("n%d" % t, c, c + 256),)


for _b in range(8):
    SCRATCH["PS%d" % _b] = ("psum", [128, 512], F32)
for _t in range(1, R, 2):
    for _name, _a, _b in _names(_t):
        SCRATCH["D" + _name] = ("dram", [256, _b - _a], U16)
SEMAPHORES = (["eV", "eS", "eP", "eG", "ldq", "ldi", "ldx", "ldc", "lda", "lde", "st", "ls"]
              + [m[0] for t in range(1, R) for m in _names(t)] + ["o%d" % t for t in range(1, R)])


def _bits(es):
    return sum(1 << e for e in es)


def _owner(T, r, t):
    return T.cores[(r + SR[t % 2]) % len(T.cores)]


def _relay(T, topo, r):
    c = T.cores[r]
    ok = [x for x in topo.cores_of(c) if T.rank_of(x) is None and all(topo.may_write(x, _owner(T, r, t)) for t in range(1, R))]
    ok.sort(key=lambda x: topo.die(x) != topo.die(c))
    return ok[0]


def _rot(t):
    return (128 - 16 * SG[t % 2]) % 128


def _relay_program(g, core, T, topo, r):
    src = T.cores[r]
    nin = len(topo.engines(src, core))
    total = 0
    for t in range(1, R):
        d = _owner(T, r, t)
        rid, pid = topo.addr(d, core)
        m = topo.mask(core, d)
        c = t - 1
        for name, a, b in _names(t):
            g.wait_ge(T.sem[name], nin)
            here = T["D" + name][_rot(t):_rot(t) + 128, :] if _rot(t) else T.NM[:, a:b]
            g.remote_dma(T.NM[:, a:b], here, T.sem[name], T.sem.ls, pid, rid, m)
        g.wait_ge(T.sem["o%d" % t], nin)
        g.remote_dma(T.OFF[:, 16 * c:16 * c + 16], T.OFF[:, 16 * c:16 * c + 16], T.sem["o%d" % t], T.sem.ls, pid, rid, m)
        total += (len(_names(t)) + 1) * len(topo.engines(core, d))
    g.wait_ge(T.sem.ls, total)


def rank_program(g, core, T, topo):
    rank = T.rank_of(core)
    if rank is None:
        for r in range(len(T.cores)):
            if _relay(T, topo, r) == core:
                _relay_program(g, core, T, topo, r)
        return
    n = len(T.cores)
    Q = {"V": g.vector, "S": g.scalar, "P": g.tensor, "G": g, "Y": g.sync}
    cnt = {"V": 0, "S": 0, "P": 0, "G": 0}
    known = {q: {} for q in Q}
    snap = {}
    log = {}

    def A(name, a=None, b=None, s=None, p=None):
        t = T[name]
        if a is None:
            a, b = 0, SCRATCH[name][1][1]
        rows = slice(None) if p is None else slice(p[0], p[1])
        ap = t[rows, a:b] if s is None else t[rows, a:b:s]
        return (ap, name, (1 << b) - (1 << a) if s is None else _bits(range(a, b, s)))

    def B(name, *ix):
        dims = SCRATCH[name][1][1:]
        ix = tuple(slice(None) if i is None else slice(*i) if isinstance(i, tuple) else i for i in ix)
        ix += (slice(None),) * (len(dims) - len(ix))
        at = np.arange(int(np.prod(dims))).reshape(dims)[ix]
        return (T[name][(slice(None),) + ix], name, _bits(at.ravel().tolist()))

    P16 = A

    def IND(w, o):
        return (w[0].indirect(o[0]), w[1], w[2], o)

    def wait(q, sem, val):
        if known[q].get(sem, 0) >= val:
            return
        Q[q].wait_ge(T.sem[sem], val)
        known[q][sem] = val
        for k2, v2 in snap.get((sem, val), {}).items():
            if known[q].get(k2, 0) < v2:
                known[q][k2] = v2

    def order(q, outs, ins, ev):
        acc = [(o, True) for o in outs] + [(i, False) for i in ins]
        acc += [(x[3], False) for x in outs + ins if len(x) > 3]
        need = {}
        for x, wr in acc:
            ps = x[1].startswith("PS")
            for cols, w2, q2, e2 in log.get(x[1], []):
                if q == "P" and q2 == "P":
                    continue
                hit = (ps and q2 != q) or ((wr or w2) and cols & x[2])
                if hit and need.get(e2[0], 0) < e2[1]:
                    need[e2[0]] = e2[1]
        for sem in sorted(need, key=lambda s: s == "e" + q):
            wait(q, sem, need[sem])
        for x, wr in acc:
            log.setdefault(x[1], []).append((x[2], wr, q, ev))
        old = snap.setdefault(ev, {})
        for k2, v2 in known[q].items():
            old[k2] = max(old.get(k2, 0), v2)

    def run(q, outs, ins, fn, inc=True):
        order(q, outs, ins, ("e" + q, cnt[q] + 1))
        ins_ = fn()
        if inc:
            ins_.then_inc(T.sem["e" + q], 1)
            cnt[q] += 1

    def landed(x, sem, val):
        log.setdefault(x[1], []).append((x[2], True, "remote", (sem, val)))

    def aps(*xs):
        return [x for x in xs if isinstance(x, tuple)]

    def val(x):
        return x[0] if isinstance(x, tuple) else x

    def cp(o, i):
        run("V", [o], [i], lambda: g.vector.tensor_copy(o[0], i[0]))

    def tt(o, a, b, op):
        run("V", [o], [a, b], lambda: g.vector.tensor_tensor(o[0], a[0], b[0], op))

    def ts(o, a, s1, op0, s2=None, op1=None):
        if s2 is None:
            run("V", [o], aps(a, s1), lambda: g.vector.tensor_scalar(o[0], a[0], val(s1), None, op0))
        else:
            run("V", [o], aps(a, s1, s2), lambda: g.vector.tensor_scalar(o[0], a[0], val(s1), val(s2), op0, op1))

    def scan(o, d0, d1, init, op0, op1):
        run("V", [o], [d0, d1], lambda: g.vector.tensor_tensor_scan(o[0], d0[0], d1[0], init, op0, op1))

    def ms(o, c):
        run("V", [o], [], lambda: g.vector.memset(o[0], c))

    def act(o, i, bias=0.0, scale=1.0, f=None):
        if f is None:
            f = AF.Copy if (not isinstance(bias, tuple) and bias == 0.0) else AF.Identity
        run("S", [o], aps(i, bias, scale), lambda: g.scalar.activation(o[0], i[0], f, bias=val(bias), scale=val(scale)))

    def mm(o, l, r, start, stop, inc=None):
        run("P", [o], [l, r], lambda: g.tensor.matmul(o[0], l[0], r[0], start, stop), stop if inc is None else inc)

    def iota(o, pat, base, cm, fl=True):
        if fl:
            run("G", [o], [], lambda: g.iota(o[0], pat, base, cm, allow_small_or_imprecise_dtypes=True))
        else:
            run("G", [o], [], lambda: g.iota(o[0], pat, base, cm))

    def dma(q, sem, total, o, i, outs, ins, **kw):
        order(q, outs, ins, (sem, total))
        Q[q].dma_start(o, i, **kw).then_inc(T.sem[sem], 16)

    def gcp(o, i, width):
        run("G", [o], [i], lambda: g.affine_select(o[0], i[0], [[0, width]], OP.is_ge, 0.0, 0, 0))

    def gather(q, o, i):
        (cp if q == "V" else act)(o, i)

    def copy(q, o, i):
        if q == "G":
            gcp(o, i, K)
        else:
            gather(q, o, i)

    rl = _relay(T, topo, rank)
    rrid, rpid = topo.addr(rl, core)
    reng = topo.engines(core, rl)
    sends = sum(len(_names(t)) + 1 for t in range(1, R)) * len(reng)

    def send_names(t, j=0):
        name, a, b = _names(t)[j]
        src = A("SU", a, b)
        order("G", [], [src], ("ls", sends))
        sem = T.sem[name]
        if _rot(t):
            h = len(reng) // 2
            g.remote_dma_fused([RemoteDMATransfer(dst_ids=[DstId(rid=rrid, pnc=rpid)], dma_engine_mask=_bits(reng[h * i:h * i + h]), remote_sem=sem,
                                                  src=src[0], dst=T["D" + name][128 * i:128 * i + 128, :]) for i in range(2)],
                               local_sem=T.sem.ls)
        else:
            g.remote_dma(T.NM[:, a:b], src[0], sem, T.sem.ls, rpid, rrid, _bits(reng))

    def send_offsets(t):
        c = t - 1
        src = A("OFS", 16 * c, 16 * c + 16)
        order("G", [], [src], ("ls", sends))
        g.remote_dma(T.OFF[:, 16 * c:16 * c + 16], src[0], T.sem["o%d" % t], T.sem.ls, rpid, rrid, _bits(reng))

    for t in range(1, R):
        back = (rank - SR[t % 2]) % n
        e = len(topo.engines(_relay(T, topo, back), core))
        for name, a, b in _names(t):
            landed(A("NM", a, b), name, e)
        landed(A("OFF", 16 * (t - 1), 16 * t), "o%d" % t, e)

    def table(t, width):
        return A("L", 2560 * (t % 2), 2560 * (t % 2) + width)

    def no_place(t):
        iota(A("SW", 512 * (t - 1), 512 * (t - 1) + K), [[0, K]], -1 if t == R - 1 else NEW, 0)

    q8 = (0, 8)
    dma("Y", "ldq", 16, T.QI[0:8, 0:256], T.que[:], [A("QI", 0, 256)], [])
    dma("Y", "ldi", 16, T.IDX[:], T.idx[:], [A("IDX")], [])
    dma("Y", "ldx", 16, T.X[:, PAD:PAD + W], T.rec[:], [A("X", PAD, PAD + W)], [])

    PB, down, up = A("PB"), A("PW", 64, 65), A("PW", 65, 66)
    pa, pg, pz, pq, pp, ph, pn = [A("PF", j, j + 1) for j in range(7)]

    def places(c0, c1):
        iota(A("PR", 16 * c0, 16 * c1), [[1, c1 - c0], [0, 16]], c0, 0)

    def halves(name, src, s1, op0, s2=None, op1=None):
        for j in range(2):
            ts(A(name, 128 * j, 128 * j + 128), src, s1, op0, s2, op1)

    def every(fn, items):
        for x in items:
            fn(x)

    const = {
        "pb": lambda: iota(PB, [[1, K]], 0, 0),
        "pq": lambda: iota(pq, [[0, 1]], 15, 16),
        "pc": lambda: iota(A("PC", 0, 1), [[0, 1]], 0, 1, False),
        "pp": lambda: iota(pp, [[0, 1]], 0, 1),
        "ig": lambda: iota(A("IG"), [[1, 8], [0, 16]], 0, 0),
        "ia": lambda: iota(A("IA"), [[0, 16], [1, 16]], 0, 0),
        "du": lambda: iota(A("DU"), [[0, 2], [1, 2]], W, 2),
        "pra": lambda: places(*LV1), "prb": lambda: places(*LV2),
        "om": lambda: iota(A("OM"), [[0, 64], [16, 16]], -16, 0),
        "da": lambda: gcp(A("DA"), A("S16"), K),
        "wi": lambda: no_place(1),
        "cur": lambda: dma("G", "ldc", 16, T.QI[0:8, 256:257], T.cur[:], [A("QI", 256, 257)], [], allow_slow_non_contiguous=True),
        "add": lambda: every(lambda j: dma("G", "lda", 64, T.AQ[:, j:j + K], T.FR[:, 0:K], [A("AQ", j, j + K)], [A("FR", 0, K)], accum_op=OP.add), range(0, TX, K)),
        "run": lambda: dma("Y", "lde", 16, T.AQ[:, TX:OLD], T.AQ[:, 0:K], [A("AQ", TX, OLD)], [A("AQ", 0, K)]),
        "zq": lambda: ts(A("ZQ", p=q8), A("PB", 0, 144, p=q8), A("PF", 3, 4, p=q8), OP.is_equal),
        "qf": lambda: cp(A("QF", 0, K, p=q8), A("QI", 0, K, p=q8)),
        "qm": lambda: every(lambda a: mm(A("PS2", 0, 16), A("ZQ", 15 - a, 143 - a, p=q8), A("QF", a, K, 16, p=q8), a == 0, a == 15), range(16)),
        "qw": lambda: cp(A("QW"), A("PS2", 0, 16)),
        "at": lambda: ts(A("AT"), IND(A("IDX"), A("QW")), float(PAD), OP.add),
        "bq": lambda: ts(A("BQ", p=q8), A("IG", p=q8), A("PF", 4, 5, p=q8), OP.is_equal),
        "cf": lambda: (cp(A("QF", K, K + 1, p=q8), A("QI", K, K + 1, p=q8)), mm(A("PS4", 0, 1), A("BQ", p=q8), A("QF", K, K + 1, p=q8), True, True)),
        "nx": lambda: cp(A("NX", 0, 1), A("PS4", 0, 1)),
        "pj": lambda: iota(A("PW", 68, 72), [[K, 4]], 0, 0),
        "ha": lambda: (ms(A("PW", 0, 16), 0.5), ms(A("PW", 16, 32), 0.0)),
        "hb": lambda: scan(A("PW", 32, 48), A("PW", 0, 16), A("PW", 16, 32), 2.0, OP.mult, OP.add),
        "hc": lambda: tt(A("PW", 48, 64), A("PW", 32, 48), A("DM", 0, 16), OP.mult),
        "hd": lambda: run("V", [down], [A("PW", 48, 64)], lambda: g.vector.tensor_reduce(down[0], T.PW[:, 48:64], AX.X, OP.add)),
        "he": lambda: run("V", [up], [down], lambda: g.vector.reciprocal(up[0], down[0])),
        "bw": lambda: ts(A("BW"), A("BB", 0, 128), up, OP.mult),
        "fi": lambda: act(A("FI", 0, K), PB, scale=down, bias=-0.4995),
        "fk": lambda: act(A("FI", K, K + 4), A("PW", 68, 72), scale=down, bias=-0.4995),
        "fj": lambda: ts(A("FJ"), A("FI"), 1, OP.bitwise_and),
        "fr": lambda: act(A("FR", 0, K), A("FJ", 0, K), scale=0.25),
        "fs": lambda: act(A("FR", K, K + 4), A("FJ", K, K + 4), scale=0.25, bias=PAD + 0.125),
        "aqa": lambda: every(lambda j: act(A("AQ", K * j, K * j + K), A("IDX", K * j, K * j + K), bias=A("FR", K + j, K + j + 1)), (0, 1)),
        "aqb": lambda: every(lambda j: act(A("AQ", K * j, K * j + K), A("IDX", K * j, K * j + K), bias=A("FR", K + j, K + j + 1)), (2, 3)),
        "xz": lambda: ms(A("X", 0, PAD), 0.0),
        "wz": lambda: ms(A("WW"), 0.0),
        "pa": lambda: (ts(A("PC", 1, 2), A("PC", 0, 1), 15, OP.bitwise_and), ts(A("PC", 2, 3), A("PC", 0, 1), 4, OP.arith_shift_right)),
        "pf": lambda: cp(A("PF", 0, 2), A("PC", 1, 3)),
        "pz": lambda: ts(pz, pa, 0.0, OP.is_equal),
        "ph": lambda: ts(ph, pa, 0.5, OP.mult),
        "pn": lambda: ts(pn, pa, 0.5, OP.mult, pp, OP.subtract),
        "hh": lambda: ts(A("H"), A("PB", 0, 8), pg, OP.is_equal),
        "dm": lambda: ts(A("DM"), A("IA", 0, 32), pa, OP.is_equal),
        "wa": lambda: (ts(A("W16", 0, 16), A("DM", 0, 16), 256.0, OP.mult), ts(A("W16", 16, 32), A("DM", 1, 17), 16.0, OP.mult)),
        "wb": lambda: tt(A("W16", 32, 48), A("W16", 16, 32), A("DM", 2, 18), OP.add),
        "wc": lambda: tt(A("W16", 48, 64), A("W16", 0, 16), A("W16", 32, 48), OP.add),
        "ww": lambda: every(lambda j: ts(A("WW", 16 * j, 16 * j + 129 * 15 + 1, 129), A("W16", 48, 64), A("H", j, j + 1), OP.mult), range(8)),
        "bb": lambda: halves("BB", A("IG"), pg, OP.is_equal),
        "ii": lambda: halves("II", A("PB", 0, 128), pp, OP.is_equal),
        "ua": lambda: act(A("LT", 0, 128), A("PB", 0, 128), bias=pn, f=AF.Abs),
        "nu": lambda: halves("NU", A("LT", 0, 128), ph, OP.is_le, -1.0, OP.mult),
        "rr": lambda: ts(A("RR"), A("BB"), pz, OP.mult),
        "rf": lambda: ts(A("R4"), A("BB"), pz, OP.mult, 4096.0, OP.mult),
        "bf": lambda: ts(A("B4"), A("BB"), 4096.0, OP.mult),
        "ni": lambda: ts(A("NI"), A("II", 0, 128), -1.0, OP.mult),
        "in": lambda: ts(A("IN"), A("II"), -1024.0, OP.mult),
        "ib": lambda: ts(A("IB"), A("II"), 1024.0, OP.mult),
        "zz": lambda: ms(A("ZD"), 0.0),
        "zd": lambda: ts(A("ZD", 15, K, 16), A("BB", 15, K, 16), pz, OP.mult),
        "zy": lambda: ms(A("ZC"), 0.0),
        "zc": lambda: ts(A("ZC", 15, K, 16), A("BB", 15, K, 16), 2048.0, OP.mult),
        "le": lambda: act(A("L", 2560, 2560 + K), PB, bias=256.0, scale=0.0, f=AF.Silu),
        "lf": lambda: act(A("L", 2560 + K, 2560 + W), A("WW", K, W), bias=256.0),
        "tz": lambda: ms(B("TRI"), 0.0),
        "tri": lambda: every(lambda b: ts(B("TRI", b), A("IA", 0, 32), pa, OP.is_ge, FAR, OP.mult), ((0, 3, 2), (3, 6, 2))),
        "nm": lambda: ts(A("NG"), A("IA"), pa, OP.not_equal, -FAR, OP.mult),
        "nz": lambda: ms(B("ND"), 0.0),
        "nd": lambda: every(lambda b: cp(B("ND", b), A("NG", 0, 32)), ((2, 5, 2), (7, 10, 2))),
        "nf": lambda: ts(A("N4"), A("BB", 0, 128), -4096.0, OP.mult),
        "eo": lambda: ms(A("EM"), 1.0),
        "ez": lambda: ms(A("EM", 0, 80, 48), 0.0),
        "em": lambda: ms(A("EM", 32, 80, 32), 8192.0),
        "pl": lambda: iota(A("PL"), [[32, 8], [-16, 2], [1, 16]], 16, 0),
        "po": lambda: ts(A("SP"), A("IW"), float(W), OP.add),
        "sm": lambda: ts(A("SM"), A("IA"), 0.0, OP.not_equal),
        "iw": lambda: ts(A("IW"), A("PB", 0, K, 16), pa, OP.add),
        "pu": lambda: ts(A("PU"), A("NU"), -1.0, OP.mult),
        "mo": lambda: (ms(A("M3"), 1.0), ms(A("C3"), 0.0)),
        "mz": lambda: (ms(A("M3", 0, 48, 3), 0.0), ms(A("C3", 1, 48, 3), -1024.0)),
        "cc": lambda: ts(A("C3", 2, 48, 3), A("IW"), 256.0, OP.add),
        "fl": lambda: ms(A("FL", 16, 48), 0.0),
    }

    def obank(c0, c1):
        return A([b for b, (a, _) in zip(("PS3", "PS6", "PS7"), PARTS) if a <= c0][-1], c0, c1)

    def pick16(o, weights, shift, rows, start=True, stop=True):
        for a in range(16):
            mm(o, A(weights, 15 - a + shift, 143 - a + shift), rows(a), start and a == 0, stop and a == 15)

    def pick_first(e0, e1):
        pick16(A("PS2", 2 * e0, 2 * e1), "ZD", 0, lambda a: A("S16", 32 * e0 + a, 32 * e1, 16))

    def others(e0, e1):
        for e in range(e0, e1):
            if e % 2 == 0:
                mm(A("PS4", 48 * e, 48 * e + 96), A("II", 0, 128), B("TRI"), e == e0, False)
            mm(A("PS4", 48 * e, 48 * e + 16), A("RR", 0, 128), A("S16", 32 * e, 32 * e + 16), False, False)
            mm(A("PS4", 48 * e + 16, 48 * e + 48), A("RR", 0, 128), A("S16", 32 * e, 32 * e + 32), False, False)

    def own_first(e0, e1):
        act(B("S0X", (e0, e1), (0, 2)), A("PS2", 2 * e0, 2 * e1))
        act(B("S0X", (e0, e1), 2), A("PS2", 2 * e0 + 1, 2 * e1, 2))

    def less_own(e0, e1):
        for a in range(16):
            mm(A("PS4", 48 * e0 + a, 48 * e1, 16), A("NI"), B("S0X", (e0, e1)), False, a == 15)

    def matches(e0, e1):
        ts(A("EQ", 48 * e0, 48 * e1), A("PS4", 48 * e0, 48 * e1), 0.0, OP.is_equal)

    def run_terms(p, w1, x1, w2, x2, stop):
        for b in range(*PASSES[p], 32):
            o = (b - PASSES[p][0]) // 32 * 80
            a, a2 = (b * 3 // 2, b * 3 // 2 + 16) if x1 == "EQ" else (b, b)
            mm(A(CMP[p], o, o + 32), A(w1, 0, 128), A(x1, a2, a2 + 32), False, False)
            mm(A(CMP[p], o + 48, o + 64), A(w1, 0, 128), A(x1, a, a + 16), False, False)
            mm(A(CMP[p], o + 32, o + 48), A(w2, 0, 128), A(x2, b + 16, b + 32), False, False)
            mm(A(CMP[p], o + 64, o + 80), A(w2, 0, 128), A(x2, b, b + 16), False, stop and b + 32 == PASSES[p][1])

    def open_compare(t, p):
        n32 = (PASSES[p][1] - PASSES[p][0]) // 32
        mm(A(CMP[p], 0, 80 * n32), A("II", 0, 128), B("ND", (0, 5 * n32)), True, False)
        run_terms(p, "II", "EQ", "RR", "S16", t == 1)

    def close_compare(p):
        run_terms(p, "N4", "NE", "B4", "NE", True)

    def lock_scan(e):
        p = [c0 <= 32 * e for c0, _ in PASSES].index(True)
        o = (32 * e - PASSES[p][0]) // 32 * 80
        scan(B("EO", e), A("EM"), A(CMP[p], o, o + 80), 0.0, OP.mult, OP.max)

    def lock_list(p):
        e0, e1 = PASSES[p][0] // 32, PASSES[p][1] // 32
        tt(A("LO", 2 * e0, 2 * e1), B("EO", (e0, e1), (47, 80, 32)), A("DU", 0, 2 * (e1 - e0)), OP.min)

    def lock_write(t, e):
        cp(IND(table(t, 2560), A("LO", 2 * e, 2 * e + 2)), A("PL", 32 * e, 32 * e + 32))

    def own_gather(q, t, c0, c1):
        gather(q, A("OG", 16 * c0, 16 * c1), IND(A("X", PAD, PAD + W), A("NM", 256 * (t - 1) + c0, 256 * (t - 1) + c1)))

    def own_max(c0, c1):
        for a in range(c0, c1, 64):
            b = min(a + 64, c1)
            scan(A("OS", 16 * a, 16 * b), A("OM", 0, 16 * (b - a)), A("OG", 16 * a, 16 * b), 0.0, OP.min, OP.max)

    def sums(c0, c1, ps="PS1"):
        mm(A(ps, c0, c1), A("II", 0, 128), A("OG", 16 * c0, 16 * c1, 16), True, False)
        mm(A(ps, c0, c1), A("II", 0, 128), A("OS", 16 * c0 + 15, 16 * c1, 16), False, True)

    def offsets(c0, c1):
        scan(A("SC", c0, c1), A("SM", c0, c1), obank(c0, c1), 0.0, OP.mult, OP.max)

    for t in range(1, R):
        c, u = t - 1, SG[t % 2]
        SU = 256 * c
        rot, back = 16 * ((8 - u) % 8), 16 * u
        last = t == R - 1

        def nbank(p):
            return A(("PS0", "PS1", "PS6", "PS7")[p if t == 1 else p % 2], *PASSES[p])

        def digits(q, a, b):
            gather(q, A("G", 16 * a, 16 * b), IND(A("X", 0, PAD + W), A("AT", a, b)))

        def weigh(p):
            c0, c1 = PASSES[p]
            if t > 1:
                mm(nbank(p), A("NI"), P16("S16", c0, c1), True, False)
            for k in range(16):
                mm(nbank(p), A("WW", 128 * k, 128 * k + 128), A("G", 16 * c0 + k, 16 * c1, 16), t == 1 and k == 0, k == 15)

        def top(p):
            ts(A("RM", *PASSES[p]), nbank(p), 2048.0 if t == 1 else 1024.0, OP.is_ge, 2048.0, OP.mult)

        def differ(p):
            tt(P16("NE", *PASSES[p]), nbank(p), A("RM", *PASSES[p]), OP.not_equal)

        def restore(p):
            tt(A("DN", *PASSES[p]), nbank(p), P16("S16", *PASSES[p]), OP.add)

        def small(j):
            if j == 2:
                ts(A("FL", 16, 32), A("PS2", 0, 16), 2048.0, OP.is_ge)
            else:
                a = 128 * (j - 4)
                ts(A("DA", a, a + 128), A("DN", a, a + 128), W - 1, OP.bitwise_and)

        step = {"v": lambda a, b: digits("V", a, b), "n": weigh, "t": top, "d": differ,
                "e": restore, "o": lambda p: open_compare(t, p), "c": close_compare, "s": lock_scan, "l": lock_list,
                "N": lambda a, b: digits("S", a, b), "G": lambda a, b: own_gather("S", t, a, b), "H": lambda a, b: own_gather("V", t, a, b),
                "k": matches, "p": pick_first, "q": own_first, "Q": others, "K": less_own,
                "w": lambda e: lock_write(t, e), "x": small, "m": lambda a, b: own_max(16 * a, 16 * b),
                "y": lambda _: mm(A("PS2", 0, 16), A("II", rot, rot + 128), B("S0X", None, (0, 2)), True, False),
                "z": lambda _: pick16(A("PS2", 0, 16), "ZC", rot, lambda a: A("NE", a, K, 16), start=False)}

        def steps(text):
            for s in text.split():
                if s in const:
                    const[s]()
                else:
                    step[s[0]](*[int(j) for j in s[1:].split("-") if j])

        if t == 1:
            step["r"] = lambda p: tt(P16("S16", *PASSES[p]), nbank(p), A("RM", *PASSES[p]), OP.subtract)
            step["u"] = lambda p: cp(A("SU", *PASSES[p]), P16("S16", *PASSES[p]))
            step["g"] = lambda j: send_names(1, j)

        def open_offsets(j):
            c0, c1 = PARTS[j]
            mm(obank(c0, c1), A("RR", rot, rot + 128), P16("S16", c0, c1), True, False)
            mm(obank(c0, c1), A("II", 0, 128), A("NG", c0, c1), False, False)
            if t > 1:
                mm(obank(c0, c1), A("B4", rot, rot + 128), P16("NE", c0, c1), False, False)

        def waits(c0, c1):
            tt(A("LG", 16 * c0, 16 * c1), IND(table(t, W), A("SU", SU + c0, SU + c1)), A("PR", 16 * c0, 16 * c1), OP.is_lt)

        def count(c0, c1, stop):
            for k in range(16):
                mm(obank(c0, c1), A("R4", rot, rot + 128), A("LG", 16 * c0 + k, 16 * c1, 16), False, stop and k == 15)

        def pick(c0, c1):
            mm(A("PS4", c0, c1), A("NI"), A("PB", c0, c1), True, False)
            for k in range(16):
                mm(A("PS4", c0, c1), A("ZD", 15 - k, 143 - k), A("LG", 16 * c0 + k, 16 * c1, 16), False, k == 15)

        def locks(c0, c1):
            act(A("LG", 16 * c0, 16 * c1), IND(table(t, W), A("SU", SU + c0, SU + c1)))

        def lower(c0, c1, stop):
            act(A("LT", c0, c1), A("PS4", c0, c1), scale=-1.0, f=AF.Relu)
            mm(obank(c0, c1), A("B4", rot, rot + 128), A("LT", c0, c1), False, bool(stop))

        def send():
            tt(A("OFS", 16 * c, 16 * c + 16), A("SC", 15, 256, 16), A("SP"), OP.min)
            send_offsets(t)

        def cand(j):
            return A("PS0", j, 48, 3)

        def un(name):
            return A(name, back, back + 128)

        keep, redo, stay, z = A("FL", 0, 16), A("FL", 16, 32), A("PS0", 64, 65), A("NX", t, t + 1)

        def renumber(j):
            if j == 0:
                ts(keep, A("SC", 15, 256, 16), float(W), OP.is_ge)
                mm(A("PS0", 0, 48), A("II", 0, 128), A("C3"), True, False)
                if t > 1:
                    mm(cand(1), un("NU"), redo, False, False)
                    mm(cand(1), un("IB"), redo, False, False)
                    mm(cand(0), un("PU"), redo, False, False)
            elif j == 1:
                scan(A("CF"), A("FL", 0, 32), A("FL", 16, 48), 0.0, OP.add, OP.subtract)
                mm(cand(0), un("NU"), keep, False, False)
                mm(cand(2), un("IN"), keep, False, False)
                mm(cand(0), un("BB"), A("CF", 0, 16), False, False)
                mm(cand(1), un("BB"), A("CF", 16, 32), False, True, False)
                mm(stay, un("BB"), A("CF", 31, 32), True, True)
            elif j == 2:
                scan(A("PP"), A("M3"), A("PS0", 0, 48), 0.0, OP.mult, OP.max)
            elif j == 3:
                cp(A("DW"), A("PP", 2, 48, 3))
            elif j == 4:
                cp(IND(A("SW", 512 * c, 512 * c + 512), A("DW")), A("DA"))
            elif j == 5:
                if t == 1:
                    ts(z, A("NX", c, t), stay, OP.subtract)
                else:
                    ts(z, A("NX", c, t), A("NX", 8 + c, 8 + t), OP.add, stay, OP.subtract)
            elif j == 6:
                ts(A("TL"), A("IW"), z, OP.add, float(K * c), OP.add)
            elif not last:
                ts(A("NX", 8 + t, 9 + t), z, float(TX - K * t), OP.is_ge, -float(TX), OP.mult)

        w0, w1, kept = 512 * (c % 2), 512 * (t % 2), A("SW", 512 * c, 512 * c + K)

        def reorder(j, q="G"):
            if j == 0:
                act(A("AW", w1, w1 + K), IND(A("AQ"), A("TL")))
            elif j == 1:
                o, i = IND(A("AW", w1, w1 + 512), A("DW")), A("AW", w0, w0 + K)
                if q == "V":
                    cp(o, i)
                else:
                    run("S", [o], [i], lambda: g.scalar.activation(o[0], i[0], AF.Silu))
            elif last:
                if j == 5:
                    dma("Y", "st", 64, T.yd[:], kept[0], [], [kept])
                elif j == 6:
                    act(A("DI"), A("AW", w1, w1 + K), scale=4.0, bias=-0.25)
                elif j == 7:
                    ts(A("DJ"), A("DI"), 1, OP.bitwise_and)
                elif j == 8:
                    act(A("RM"), A("DJ"))
                    mm(A("PS1", 0, K), A("BW"), A("RM"), True, True)
                elif j == 9:
                    act(A("T1"), A("PS1", 0, K))
                    dma("Y", "st", 64, T.yq[:], T.T1[0:128:16, :], [], [A("T1")])
            elif j == 2:
                others(0, 8)
            elif j == 4:
                less_own(0, 8)
            elif j == 3:
                copy(q, A("S16"), kept)
            elif j == 5:
                copy(q, A("SU", SU + 256, SU + 512), kept)
                send_names(t + 1)
            elif j == 6:
                copy(q, A("AT"), A("AW", w1, w1 + K))
            elif j == 7:
                pick_first(0, 8)
            elif j == 8:
                own_first(0, 8)
            else:
                if t == 1:
                    iota(table(2, W), [[0, W]], 256, 0)
                no_place(t + 1)
                if t + 2 < R:
                    iota(table(t + 2, W), [[0, W]], 256, 0)

        def digit(c0, c1, j):
            return A("PS%d" % j, c0, c1)

        step.update({"L": waits, "S": locks, "P": pick, "C": lambda a, b, s: count(a, b, bool(s)), "T": lower, "A": open_offsets, "B": offsets, "O": send,
                     "U": lambda j: reorder(j, "S"), "V": lambda j: reorder(j, "V"),
                     "R": renumber, "J": reorder,
                     "h": lambda a, b, j: sums(a, b, "PS%d" % j), "i": lambda a, b, j: act(A("TT", a, b), digit(a, b, j)),
                     "j": lambda a, b, j: cp(A("TT", a, b), digit(a, b, j)),
                     "f": lambda a, b, j=None: ts(A("TR", a, b), A("TT", a, b) if j is None else digit(a, b, j), 16.0, OP.is_ge, -16.0, OP.mult),
                     "I": lambda: act(A("AW", 0, K), IND(A("AQ", 0, TX), A("QW")))})

        def write():
            tt(IND(A("X", PAD, PAD + 2560), A("OFF", 16 * c, 16 * c + 16)), A("TT"), A("TR"), OP.add)
            if last:
                dma("Y", "st", 64, T.yx[0:64, :], T.X[0:64, PAD:PAD + W], [], [A("X")])
                dma("S", "st", 64, T.yx[64:128, :], T.X[64:128, PAD:PAD + W], [], [A("X")])

        step["X"] = write
        steps(FIRST if t == 1 else TAIL if last else LATER)

    for q in ("V", "S", "P", "G"):
        wait("G", "e" + q, cnt[q])
    wait("G", "ls", sends)
    wait("G", "st", 64)
